import numpy as np, ml_dtypes
CORES = [10,34,74,98]
N = 4
BF = ml_dtypes.bfloat16
W, L, B, CAP, C, S, RO = 4096, 256, 16, 64, 8, 64, 8
def work(rng, *shape):
    return B * rng.integers(0, L, shape) + rng.integers(0, RO, shape)
def land(rng, *shape):
    return S * rng.integers(0, CAP, shape) + RO + rng.integers(0, RO, shape)
def parts(rng):
    X = rng.integers(0, 256, (N, 8, 16, W)); R = rng.integers(0, W, (N, 8, 16, W)); R = np.where(rng.random(R.shape) < 0.5, R[:, :, :1], R)
    z = rng.random((N, 8, W)); A = np.where(z < 0.3, work(rng, N, 8, W), np.where(z < 0.5, land(rng, N, 8, W), rng.integers(0, W, (N, 8, W))))
    return X, R, A, rng.integers(0, 256, (N, 8, 16)), rng.integers(1000, 1250, (N, 8, 1)) + rng.integers(0, 200, (N, 8, 16))
def pack(X, R, A, w, th):
    return {"xc": np.ascontiguousarray(X.reshape(N, 128, W)).astype(np.float32).astype(BF), "rf": np.ascontiguousarray(R.reshape(N, 128, W)).astype(np.int32),
            "an": np.ascontiguousarray(A).astype(np.int32), "w": w.reshape(N, 128, 1).astype(np.int32), "th": th.reshape(N, 128, 1).astype(np.int32)}
def setup_inputs(rng):
    return pack(*parts(rng))
def setup_inputs_copies(rng):
    X, R, A, w, th = parts(rng); x = np.arange(W)
    R[:, 1::4] = np.repeat(R[:, 1::4, :1], 16, axis=2)
    R[:, 2::4, 1:] = (R[:, 2::4, :1] + rng.integers(1, W, (N, 2, 15, W))) & (W - 1)
    A[:, ::2] = (x - B) & (W - 1)
    A[:, 1::2] = np.where(rng.random((N, 4, W)) < 0.5, land(rng, N, 4, W), work(rng, N, 4, W))
    th = rng.choice(np.array([1100, 1300, 1500]), (N, 8, 1)) + rng.integers(0, 200, (N, 8, 16))
    return pack(X, R, A, w, th)
def setup_inputs_corners(rng):
    X, R, A, w, th = parts(rng); kk = np.arange(16).reshape(1, 1, 16, 1); x = np.arange(W); heads = B * np.arange(L); off = x & (B - 1)
    X = rng.integers(0, 4, (N, 8, 16, W)); R = rng.integers(0, W, (N, 8, 16, W))
    first = R[:, :, :1]; first = np.where((first & (B - 1)) == 0, first ^ 1, first)
    R = np.where((rng.random(R.shape) < 0.5) | (kk == 0), first, R)
    R = np.where(((R + 613 * kk) & (B - 1)) == 0, R ^ 1, R)
    th = rng.integers(49, 101, (N, 8, 16)); slow = []
    for q in range(N):
        for g in range(8):
            k = int(rng.choice(np.array([0, 1, CAP - 1, CAP, CAP + 1, L])))
            if q == 0: k = (CAP, CAP + 1, L, CAP - 1, 1, 0, CAP, CAP + 1)[g]
            if q == 1: k = (CAP, CAP - 1, 1, 0, 0, 0, 0, 256 - 2 * CAP)[g]
            if q == 2: k = 31 + int(g < 7)
            if q == N - 1 and g == 7: k = CAP
            o = rng.permutation(L)
            if g == 7 and k > 0:
                i = int(np.flatnonzero(o < k)[-1]); o[[i, L - 1]] = o[[L - 1, i]]
            go = o < k; h = np.where(go, 0, rng.integers(100, 256, (16, L))); near = rng.integers(10, 13, (16, L))
            if q == 1: h = np.where(~go & (rng.random(L) < 0.5), near, h)
            if q == 2:
                h = np.where(o < 56, 0, np.where(o < 186, near, h)); slow.append(heads[(o >= k) & (o < 186)])
            X[q, g][:, heads] = h
    w[:, 0::4] = 255; w[:, 1::4] = 0; w[1:3] = 0
    A[:, 0] = x; A[:, 1] = (W - 1) * rng.integers(0, 2, (N, W)); A[:, 2] = (x + 1) & (W - 1); A[:, 3] = (x - B) & (W - 1); A[:, 5] = (x - 1) & (W - 1)
    A[:, 6] = np.where(rng.random((N, W)) < 0.5, x, W - 1 - x)
    X[2][:, :, off == 1] = rng.integers(100, 256, (8, 16, L))
    to = B * rng.integers(0, L, (8, 16, W)) + np.where(off == 2, 1, rng.integers(2, B, (8, 16, W)))
    R[2] = (to - 613 * kk[0]) & (W - 1)
    A[2] = B * rng.integers(0, L, (8, W)) + 3
    A[2][:, 2 * B * np.arange(L // 2) + 2] = 2 * B * rng.integers(0, L // 2, (8, L // 2)) + B + 2
    for g in range(8): A[2, g, slow[g]] = 2 * B * rng.integers(0, L // 2, len(slow[g])) + 2
    return pack(X, R, A, w, th)
def setup_inputs_ends(rng):
    kind = rng.integers(0, 3, (N, 8, 1, W)); X = 255 * np.where(kind == 2, rng.integers(0, 2, (N, 8, 16, W)), kind)
    R = (W - 1) * rng.integers(0, 2, (N, 8, 16, W)); A = (W - 1) * rng.integers(0, 2, (N, 8, W))
    z = rng.random((N, 8, W)); A = np.where(z < 0.12, work(rng, N, 8, W), np.where(z < 0.25, land(rng, N, 8, W), A))
    w = 255 * rng.integers(0, 2, (N, 8, 16)); th = np.zeros((N, 8, 16), np.int64)
    for q in range(N):
        many = np.append(rng.permutation(np.array([C, C - 1, C - 2, C + 1, C - 1, C, C - 1])), C)
        i = int(np.flatnonzero(many == C)[0]); many[[i, 6]] = many[[6, i]]
        for g in range(8): th[q, g, rng.permutation(16)[:many[g]]] = 4080
    w[:, 7] = 255; w[:, 6] = 0; w[:, 6, 0] = 255; w[:, 6, 1] = 1
    for x in (0, W - B):
        X[:, 7, :, x] = 255; A[:, 7, x] = 0
    X[:, 6, 0, W - B] = 16; X[:, 6, 1, W - B] = 15; A[:, 6, W - B] = W - 1; R[:, 6, 0, W - B] = 0
    X[:, 6, 0, 0] = 15; X[:, 6, 1, 0] = 250; A[:, 6, 0] = W - 2; R[:, 6, 0, 0] = 0
    R[:, 6, :, W - 1] = W - 1
    R[:, 6, :, W - 2] = W - 3
    R[:, 7, 0, 0] = W - 1; R[:, 7, 14:, 0] = 0
    X[:, 7, :, (613 * 15) & (W - 1)] = 0; X[:, 7, :, (613 * 14) & (W - 1)] = 255
    return pack(X, R, A, w, th)
def setup_inputs_spread(rng):
    X = (rng.random((N, 8, 16, W)) * np.exp2(rng.integers(0, 9, (N, 8, 1, W)))).astype(np.int64)
    p = rng.choice(np.array([1, 2, 4]), (N, 8, 16, 1)); R = np.minimum((W * rng.random((N, 8, 16, W)) ** p).astype(np.int64), W - 1)
    R = np.where(rng.random(R.shape) < rng.random((N, 8, 1, W)), R[:, :, :1], R)
    p = rng.choice(np.array([1, 2, 4]), (N, 8, 1)); A = np.minimum((W * rng.random((N, 8, W)) ** p).astype(np.int64), W - 1)
    w = np.minimum(np.exp2(8 * rng.random((N, 8, 16))).astype(np.int64), 255) * (rng.random((N, 8, 16)) > 0.1)
    p = rng.choice(np.array([1, 2, 4, 8]), (N, 8, 1)); th = np.minimum((4081 * rng.random((N, 8, 16)) ** p).astype(np.int64), 4080)
    return pack(X, R, A, w, th)
def setup_inputs_ties(rng):
    X, R, A, w, th = parts(rng)
    pool = rng.integers(0, 256, (N, 8, 16, 6)); X = np.take_along_axis(pool, rng.integers(0, 6, (N, 8, 1, W)), 3)
    i = rng.integers(0, 6, (N, 8, 1, 16)); j = rng.integers(0, 6, (N, 8, 1, 16))
    d = np.add.reduce(np.abs(np.take_along_axis(pool, i, 3) - np.take_along_axis(pool, j, 3)), axis=2)
    return pack(X, R, A, w, np.minimum(d + rng.integers(0, 2, d.shape), 4080))
def check_inputs(d):
    bad = []
    for k, lo, hi in (("xc", 0, 255), ("rf", 0, W - 1), ("an", 0, W - 1), ("w", 0, 255), ("th", 0, 4080)):
        a = np.asarray(d[k]).astype(np.float64)
        if not (np.min(a) >= lo and np.max(a) <= hi): bad.append("range of " + k)
        elif np.any(a != np.floor(a)): bad.append("whole numbers in " + k)
    return bad
def cols(T, ix):
    return np.take_along_axis(T, ix[:, :, None, :], 3)
def dist(X, q, u, m):
    kk = np.arange(16).reshape(1, 1, 16, 1); s = ((m * u >> 5) + m + 613 * kk) & (W - 1)
    x = cols(X, s.reshape(N, 8, 16 * L)).reshape(N, 8, 16, 16, L)
    return np.add.reduce(np.abs(x - q[:, :, :, None, :]), axis=2).astype(np.int64)
def reference(xc, rf, an, w, th):
    X = xc.astype(np.float32).astype(np.int32).reshape(N, 8, 16, W); R = rf.astype(np.int64).reshape(N, 8, 16, W); A = an.astype(np.int64)
    ww = w.astype(np.int64).reshape(N, 8, 16, 1); tt = th.astype(np.int64).reshape(N, 8, 16, 1)
    v = np.zeros((N, 8, 1), np.int64) + B * np.arange(L); a = np.take_along_axis(A, v, 2); b = np.zeros((N, 1, 1, 1), np.int64)
    for t in range(RO):
        q = cols(X, v); u = np.add.reduce(ww * q, axis=2, keepdims=True) & 4095
        e = cols(R, a); own = np.take_along_axis(R[:, :, 0], v, 2)[:, :, None, :]
        n = np.where(e == e[:, :, :1], own, e)
        d, d2 = dist(X, q, u, e), dist(X, q, u, n)
        f = np.where(d2 < d, n, e); f[:, :, 0] = own[:, :, 0]
        fit = (np.add.reduce((np.minimum(d, d2) < tt + b).astype(np.int64), axis=2) >= C).astype(np.int64)
        b = (np.add.reduce(fit, axis=(1, 2)) & 255).reshape(N, 1, 1, 1)
        after = np.where(fit == 1, np.take_along_axis(A, v + 1, 2), np.take_along_axis(A, a, 2))
        r, g, i = np.nonzero(fit)
        R[r, g, :, v[r, g, i]] = f[r, g, :, i]; A[r, g, v[r, g, i]] = a[r, g, i]
        before = np.add.accumulate(fit, axis=2) - fit
        r, g, i = np.nonzero((fit == 1) & (before < CAP))
        R[(r + 1 + t % (N - 1)) % N, g, :, S * before[r, g, i] + RO + t] = f[r, g, :, i]
        v = v + fit; a = after
    o = R.reshape(N, 8, 16, L, B); o = o[..., :RO // 2] + 4096 * o[..., RO // 2:RO]
    h = R.reshape(N, 8, 16, CAP, S)[..., RO:2 * RO]
    return {"yr": o.reshape(N, 128, L * (RO // 2)).astype(np.float32), "yh": h.reshape(N, 128, CAP * RO).astype(np.float32),
            "yan": A.reshape(N, 8, L, B)[..., :RO].reshape(N, 8, L * RO).astype(np.float32), "yv": v.astype(np.float32), "ya": a.astype(np.float32)}

@@ -1,0 +1,438 @@
+from concourse.bass import DstId, RemoteDMATransfer
+from concourse.mybir import AluOpType as A, AxisListType, ActivationFunctionType as F
+
+NST, CH = 8, 4
+HOOK, WHOOK, EHOOK, EQ_AFTER = 3, 4, 4, 2
+NEG = -255.0 * 65536.0
+CBW = 768
+E_ON_S = ()
+O_ON_V = ()
+
+SCRATCH = {}
+for _n, _s, _d in (
+        ("XW", 12288, "bfloat16"), ("RI", 4096, "int32"), ("RW", 8192, "float32"), ("AW", 8192, "bfloat16"),
+        ("IOT", 4096, "bfloat16"), ("LOW", 4096, "bfloat16"), ("SV", 4096, "bfloat16"), ("UT", 4096, "int32"),
+        ("KOT", 4096, "float32"), ("CB", NST * CBW, "float32"), ("LAND", NST * 64, "float32"), ("PRES", NST * 64, "float32"),
+        ("GE", 4096, "bfloat16"), ("GO", 4096, "bfloat16"),
+        ("AB0", 1024, "bfloat16"), ("AB1", 1024, "bfloat16"),
+        ("AR", 512, "int32"), ("ARS", 1024, "int32"), ("ARB", 1040, "bfloat16"),
+        ("WI", 1, "int32"), ("TI", 1, "int32"), ("PI", 1, "int32"), ("PGI", 1, "int32"), ("PKI", 1, "int32"), ("KCI", 1, "int32"),
+        ("BI", 1, "int32"), ("BI2", 1, "int32"), ("COL", 32, "float32"),
+        ("CI", 144, "int32"), ("MG", 128, "int32"), ("T0", 128, "float32"), ("T1", 128, "float32"),
+        ("IDM", 128, "bfloat16"), ("NID", 128, "bfloat16"), ("Z8", 144, "bfloat16"), ("Z1", 144, "bfloat16"),
+        ("ZA", 144, "bfloat16"), ("ZB", 144, "bfloat16"), ("EQM", 128, "float32"), ("DNM", 128, "float32"),
+        ("SVE", 128, "bfloat16"), ("SVR", 128, "bfloat16"), ("SVK", 128, "bfloat16"), ("TRI", 128, "bfloat16"),
+        ("BLK", 128, "bfloat16"), ("ALL1", 128, "bfloat16"), ("WM", 128, "bfloat16"),
+        ("VI", 16, "int32"), ("KI", 16, "int32"), ("KD", 16, "float32"), ("ZERO", 16, "float32"), ("SC", 32, "float32"),
+        ("VF0", 16, "float32"), ("VF1", 16, "float32"), ("AAS", 16, "float32"), ("DA", 16, "float32"), ("MA", 16, "float32"),
+        ("AN", 16, "float32"), ("FW", 16, "bfloat16"), ("NF", 16, "float32"), ("GD", 16, "float32"), ("P1", 16, "float32"),
+        ("P2", 16, "float32"), ("DD", 16, "float32"), ("JK", 16, "float32"),
+        ("A16", 16, "uint16"), ("V16", 16, "uint16"), ("D16", 16, "uint16"), ("C16", 16, "uint16"),
+        ("QG", 256, "bfloat16"), ("SVG", 256, "bfloat16"), ("AWG", 256, "bfloat16"), ("IOG", 256, "bfloat16"),
+        ("EG", 256, "float32"), ("UG", 256, "float32"), ("TA", 256, "int32"), ("TB", 256, "int32"), ("TC", 256, "int32"),
+        ("PLE", 256, "uint16"), ("PLO0", 256, "uint16"), ("PLO1", 256, "uint16"), ("UC", 256, "int32"),
+        ("OA", 256, "int32"), ("OB", 256, "int32"), ("OC", 256, "int32"),
+        ("NEQ", 256, "float32"), ("DM", 256, "float32"), ("MN", 256, "int32"), ("IND", 256, "bfloat16"), ("FV", 256, "int32"),
+        ("YH", 512, "float32"), ("YVA", 512, "float32")):
+    SCRATCH[_n] = ("sbuf", [128, _s], _d)
+for _n, _s in (("W0", 1024), ("W1", 1024), ("KE", 512), ("KO", 512), ("M1", 512), ("M2", 512)):
+    SCRATCH[_n] = ("psum", [128, _s], "float32")
+SEMAPHORES = ["qv", "qs", "qp", "qg", "pre", "sent"] + ["arr%d" % t for t in range(NST)] + ["d%d" % i for i in range(28)]
+
+
+def rank_program(g, core, T, topo):
+    rank = T.rank_of(core)
+    if rank is None:
+        return
+    n_ranks = len(T.cores)
+    queue = {"v": g.vector, "s": g.scalar, "p": g.tensor, "g": g, "y": g.sync}
+    seen = {q: {} for q in queue}
+    count = {}
+    last, readers = {}, {}
+
+    def need(q, tok):
+        s, n, clock = tok
+        if seen[q].get(s, 0) < n:
+            queue[q].wait_ge(T.sem[s], n)
+            for k, x in clock.items():
+                seen[q][k] = max(seen[q].get(k, 0), x)
+            seen[q][s] = n
+
+    def before(q, own, rd, wr):
+        for k in rd:
+            if k in last:
+                need(q, last[k])
+            if k[0] == "#":
+                for s, tok in readers.get(k, {}).items():
+                    if s != own:
+                        need(q, tok)
+        for k in wr:
+            if k in last and (q != "p" or last[k][0] != own):
+                need(q, last[k])
+            for s, tok in readers.get(k, {}).items():
+                need(q, tok)
+
+    def after(tok, rd, wr):
+        for k in wr:
+            last[k] = tok
+            readers[k] = {}
+        for k in rd:
+            readers.setdefault(k, {})[tok[0]] = tok
+
+    def split(keys):
+        return keys.split() if keys else []
+
+    def op(q, name, args, rd="", wr="", **kw):
+        rd, wr, own = split(rd), split(wr), "q" + q
+        before(q, own, rd, wr)
+        eng = queue[q]
+        fns = {"copy": ("v", lambda: eng.tensor_copy(*args)), "tt": ("v", lambda: eng.tensor_tensor(*args)),
+               "ts": ("v", lambda: eng.tensor_scalar(*args)), "act": ("s", lambda: eng.activation(*args, **kw)),
+               "mm": ("p", lambda: eng.matmul(*args)), "scan": ("v", lambda: eng.tensor_tensor_scan(*args)),
+               "red": ("v", lambda: eng.tensor_reduce(*args)), "set": ("v", lambda: eng.memset(*args)),
+               "iota": ("g", lambda: eng.iota(*args, **kw))}
+        fns[name][1]().then_inc(T.sem[own], 1)
+        count[own] = count.get(own, 0) + 1
+        after((own, count[own], dict(seen[q])), rd, wr)
+
+    dmas = [0]
+
+    def dma(q, out, in_, rd="", wr=""):
+        rd, wr = split(rd), split(wr)
+        s = "d%d" % dmas[0]
+        dmas[0] += 1
+        before(q, s, rd, wr)
+        queue[q].dma_start(out, in_).then_inc(T.sem[s], 16)
+        count[s] = 16
+        after((s, 16, dict(seen[q])), rd, wr)
+
+    def mm(out, lhs, rhs, start, stop, rd, wr):
+        op("p", "mm", (out, lhs, rhs, start, stop), rd, wr)
+
+    dma("y", T.AR[:, 0:256], T.rf[0::16, :], wr="AR0")
+    dma("y", T.AR[:, 256:512], T.an[:, :], wr="AR1")
+    dma("y", T.WI[:], T.w[:], wr="WI")
+    dma("y", T.TI[:], T.th[:], wr="TI")
+    dma("y", T.XW[:, 0:4096], T.xc[:], wr="X1")
+    dma("y", T.XW[:, 8192:12288], T.xc[:], wr="X3")
+    for h in range(2):
+        dma("y", T.RI[:, 2048 * h:2048 * h + 2048], T.rf[:, 2048 * h:2048 * h + 2048], wr="RI%d" % h)
+
+    op("g", "iota", (T.PI[:], [[0, 1]], 0, 1), wr="PI")
+    op("g", "iota", (T.CI[:], [[1, 144]], 0, 0), wr="CI")
+    op("g", "iota", (T.VI[:], [[256, 16]], 0, 16), wr="VI")
+    op("g", "iota", (T.KI[:], [[16, 16]], 256, 1), wr="KI")
+    op("g", "iota", (T.LOW[:], [[0, 64], [1, 64]], 0, 0), wr="LOW", allow_small_or_imprecise_dtypes=True)
+    op("g", "iota", (T.IOT[:], [[1, 64], [0, 64]], 0, 0), wr="IOT", allow_small_or_imprecise_dtypes=True)
+
+    ncol = {}
+
+    def col(name):
+        if name not in ncol:
+            ncol[name] = len(ncol)
+        return T.COL[:, ncol[name]:ncol[name] + 1]
+
+    def ts(out, in0, s1, s2, o0, o1, rd, wr):
+        op("v", "ts", (out, in0, s1, s2, o0) if o1 is None else (out, in0, s1, s2, o0, o1), rd, wr)
+
+    def tt(out, a, b, o, rd, wr):
+        op("v", "tt", (out, a, b, o), rd, wr)
+
+    def cp(out, in_, rd, wr):
+        op("v", "copy", (out, in_), rd, wr)
+
+    SVall = "SV0 SV1 SV2 SV3 SVx"
+    Xall = "X1 X2 X3"
+    op("v", "set", (T.SV[:], 1.0), wr=SVall)
+    op("s", "act", (T.AW[:, 0:4096], T.SV[:], F.Copy), SVall, "AW AWr")
+    op("v", "set", (T.ARB[:, 1024:1040], 0.0), wr="pad")
+    ts(T.ARS[:, 0:512], T.AR[:], 6, None, A.arith_shift_right, None, "AR0 AR1", "ARS0")
+    ts(T.ARS[:, 512:1024], T.AR[:], 63, None, A.bitwise_and, None, "AR0 AR1", "ARS1")
+    cp(T.ARB[:, 0:1024], T.ARS[:], "ARS0 ARS1", "ARB")
+    dma("y", T.SV[0::16, :], T.ARB[:, 0:256], rd="ARB", wr="SV0")
+    dma("y", T.SV[1::16, :], T.ARB[:, 512:768], rd="ARB", wr="SV1")
+    dma("y", T.SV[2::16, :], T.ARB[:, 257:513], rd="ARB", wr="SV2")
+    dma("y", T.SV[3::16, :], T.ARB[:, 769:1025], rd="ARB pad", wr="SV3")
+    dma("y", T.AW[0::16, 0:4096], T.ARB[:, 256:512], rd="ARB", wr="AW")
+    dma("y", T.AW[1::16, 0:4096], T.ARB[:, 768:1024], rd="ARB", wr="AWr")
+    dma("y", T.IOT[1::16, :], T.LOW[0:8, :], rd="LOW", wr="IOT")
+    op("v", "copy", (col("p"), T.PI[:]), "PI", "c_p")
+    ts(T.PGI[:], T.PI[:], 112, None, A.bitwise_and, None, "PI", "PGI")
+    ts(T.PKI[:], T.PI[:], 15, None, A.bitwise_and, None, "PI", "PKI")
+    ts(T.MG[:], T.CI[:, 0:128], 112, None, A.bitwise_and, None, "CI", "MG")
+    cp(col("pg"), T.PGI[:], "PGI", "c_pg")
+    ts(col("pg16"), T.PGI[:], 16.0, None, A.add, None, "PGI", "c_pg16")
+    ts(col("pgx"), T.PGI[:], 16.0, None, A.mult, None, "PGI", "c_pgx")
+    ts(col("k0"), T.PKI[:], 0.0, 64.0, A.is_equal, A.mult, "PKI", "c_k0")
+    ts(col("k1"), T.PKI[:], 1.0, None, A.is_equal, None, "PKI", "c_k1")
+    ts(col("k2"), T.PKI[:], 2.0, 64.0, A.is_equal, A.mult, "PKI", "c_k2")
+    ts(col("k3"), T.PKI[:], 3.0, None, A.is_equal, None, "PKI", "c_k3")
+    ts(col("k4"), T.PKI[:], 4.0, NEG, A.is_equal, A.mult, "PKI", "c_k4")
+    ts(col("k5"), T.PKI[:], 5.0, 4096.0, A.is_equal, A.mult, "PKI", "c_k5")
+    ts(col("nk"), T.PKI[:], 0.0, None, A.is_gt, None, "PKI", "c_nk")
+    ts(T.KCI[:], T.PKI[:], 613.0, None, A.mult, None, "PKI", "KCI")
+    tt(col("kr"), col("k0"), col("k1"), A.add, "c_k0 c_k1", "c_kr")
+    tt(col("kb"), col("k2"), col("k3"), A.add, "c_k2 c_k3", "c_kb")
+    ts(T.BI[:], T.KCI[:], 4095, None, A.bitwise_and, None, "KCI", "BI")
+    tt(col("k45"), col("k4"), col("k5"), A.add, "c_k4 c_k5", "c_k45")
+    cp(col("kc"), T.BI[:], "BI", "c_kc")
+    tt(col("kk"), col("kr"), col("k45"), A.add, "c_kr c_k45", "c_kk")
+    ts(T.IDM[:], T.CI[:, 0:128], col("p"), None, A.is_equal, None, "CI c_p", "IDM")
+    ts(T.NID[:], T.CI[:, 0:128], col("p"), -1.0, A.is_equal, A.mult, "CI c_p", "NID")
+    ts(T.BLK[:], T.MG[:], col("pg"), None, A.is_equal, None, "MG c_pg", "BLK")
+    ts(T.SVR[:], T.MG[:], col("pg"), col("kr"), A.is_equal, A.mult, "MG c_pg c_kr", "SVR")
+    cp(col("w"), T.WI[:], "WI", "c_w")
+    ts(col("th"), T.TI[:], 8192.0, NEG, A.mult, A.add, "TI", "c_th")
+    ts(T.WM[:], T.MG[:], col("pg"), col("w"), A.is_equal, A.mult, "MG c_pg c_w", "WM")
+    ts(T.SVK[:], T.MG[:], col("pg"), col("kk"), A.is_equal, A.mult, "MG c_pg c_kk", "SVK")
+    ts(T.Z8[:], T.CI[:], col("pg16"), 8192.0, A.is_equal, A.mult, "CI c_pg16", "Z8")
+
+    def prep_u(c):
+        mm(T.M1[:, 0:256], T.WM[:], T.XW[:, c:4096:16], True, True, "WM X1", "#M1")
+        mm(T.M1[:, 256:512], T.SVR[:], T.SV[:, c::16], True, True, "SVR " + SVall, "#M1")
+
+    def prep_v(c):
+        cp(T.UC[:], T.M1[:, 0:256], "#M1", "UC")
+        ts(T.UT[:, c::16], T.UC[:], 4095, None, A.bitwise_and, None, "UC", "UT")
+        tt(T.OA[:], T.M1[:, 256:512], T.UT[:, c::16], A.mult, "#M1 UT", "OA")
+        ts(T.OB[:], T.OA[:], 5, 4095, A.arith_shift_right, A.bitwise_and, "OA", "OB")
+        tt(T.OC[:], T.M1[:, 256:512], T.OB[:], A.add, "#M1 OB", "OC")
+        ts(T["PLO%d" % (c % 2)][:], T.OC[:], col("kc"), None, A.add, None, "OC c_kc", "PLO%d" % (c % 2))
+
+    turn = [0]
+
+    def gather(e, c, q, b=0):
+        G, pl = (T.GE, "PLE") if e else (T.GO, "PLO%d" % (b % 2))
+        src = T.XW[:].indirect(T[pl][:, 64 * c:64 * c + 64])
+        out = G[:, 1024 * c:1024 * c + 1024]
+        key = ("GE%d" if e else "GO%d") % c
+        if q == "v":
+            cp(out, src, Xall + " " + pl, key)
+        else:
+            op("s", "act", (out, src, F.Copy), Xall + " " + pl, key)
+
+    pending = []
+
+    def sums(item):
+        e, c, w, b = item
+        K, key = (T.KE, "#KE") if e else (T.KO, "#KO")
+        o = K[:, 64 * c:64 * c + 64]
+        for h in range(2):
+            if h == 0 and e:
+                mm(o, T.SVE[:], T.SVG[:, 64 * c:64 * c + 64], True, False, "SVE SVG", key)
+                mm(o, T.DNM[:], T.EG[:, 64 * c:64 * c + 64], False, False, "DNM EG", key)
+            elif h == 0:
+                mm(o, T.SVK[:], T.SV[:, 1024 * c + b:1024 * c + 1024:16], True, False, "SVK " + SVall, key)
+            for k in range(8 * h, 8 * h + 8):
+                mm(o, T.Z8[:, 16 - k:144 - k], T["AB%d" % w][:, 64 * k:64 * k + 64], False, k == 15, "Z8 AB%d_%d" % (w, h), key)
+
+    def diff(e, c, b=0, halves=False):
+        w = turn[0] % 2
+        turn[0] += 1
+        G, key = (T.GE, "GE%d" % c) if e else (T.GO, "GO%d" % c)
+        q, qk = (T.QG[:, 64 * c:64 * c + 64], "QG") if e else (T.XW[:, 1024 * c + b:1024 * c + 1024:16], "X1")
+        W, AB = T["W%d" % w], T["AB%d" % w]
+        for k in range(16):
+            o, wk = W[:, 64 * k:64 * k + 64], "#W%d_%d" % (w, k // 8)
+            mm(o, T.IDM[:], G[:, 1024 * c + k:1024 * c + 1024:16], True, False, "IDM " + key, wk)
+            mm(o, T.NID[:], q, False, True, "NID " + qk, wk)
+            if halves and k % 8 == 7:
+                h = k // 8
+                op("s", "act", (AB[:, 512 * h:512 * h + 512], W[:, 512 * h:512 * h + 512], F.Abs), wk, "AB%d_%d" % (w, h))
+        if not halves:
+            op("s", "act", (AB[:], W[:], F.Abs), "#W%d_0 #W%d_1" % (w, w), "AB%d_0 AB%d_1" % (w, w))
+        pending.append((e, c, w, b))
+        while len(pending) > 1:
+            sums(pending.pop(0))
+
+    def flush():
+        while pending:
+            sums(pending.pop(0))
+
+    def own_unit(b, hooks):
+        for c in range(CH + 1):
+            for at, f in hooks:
+                if at == c:
+                    f()
+            if c < CH:
+                gather(False, c, "v" if c in O_ON_V else "s", b)
+            if c:
+                diff(False, c - 1, b)
+
+    def own_table(b):
+        op("s", "act", (T.KOT[:, b::16], T.KO[:, 0:256], F.Copy), "#KO", "KOT")
+
+    def wrap(o, Z, src, zk, sk):
+        for il in range(16):
+            mm(o, Z[:, 16 - il:144 - il], src(il), il == 0, il == 15, zk + " " + sk, "#M2")
+
+    CNT, AAW, AVW, TRI_, TOT, FITS = (T.M2[:, 256 + 16 * j:272 + 16 * j] for j in range(6))
+
+    def smalls():
+        op("s", "act", (T.QG[:], T.XW[:, 0:4096].indirect(T.V16[:]), F.Copy), "X1 V16", "QG")
+        op("s", "act", (T.AWG[:], T.AW[:, 0:4096].indirect(T.A16[:]), F.Copy), "AW AWr A16", "AWG")
+        op("s", "act", (T.SVG[:], T.SV[:].indirect(T.V16[:]), F.Copy), SVall + " V16", "SVG")
+
+    def wraps():
+        wrap(AVW, T.ZB, lambda il: T.SVG[:, il::16], "ZB", "SVG")
+        wrap(AAW, T.ZA, lambda il: T.AWG[:, il::16], "ZA", "AWG")
+        op("s", "act", (T.AAS[:], AAW, F.Copy), "#M2", "AAS")
+
+    def fits():
+        op("s", "act", (T.JK[:], FITS, F.Copy), "#M2", "JK c_bs", accum_out=col("bs"))
+
+    def place_e():
+        tt(T.TA[:], T.RW[:, 0:4096].indirect(T.A16[:]), T.UG[:], A.mult, "RW A16 UG", "TA")
+        op("s", "act", (T.EG[:], T.RW[:, 0:4096].indirect(T.A16[:]), F.Copy), "RW A16", "EG")
+        ts(T.TB[:], T.TA[:], 5, 4095, A.arith_shift_right, A.bitwise_and, "TA", "TB")
+        tt(T.TC[:], T.RW[:, 0:4096].indirect(T.A16[:]), T.TB[:], A.add, "RW A16 TB", "TC")
+        ts(T.PLE[:], T.TC[:], col("kc"), None, A.add, None, "TC c_kc", "PLE")
+
+    def merge(t):
+        cp(T.RW[:, 8 + t:4096:64], T.LAND[:, 64 * t:64 * t + 64], "LAND%d" % t, "RW")
+
+    def keep_yh(t):
+        op("s", "act", (T.YH[:, t::8], T.LAND[:, 64 * t:64 * t + 64], F.Copy), "LAND%d" % t, "YH")
+
+    def gathers_e():
+        for c in E_ON_S:
+            gather(True, c, "s")
+        for c in range(CH):
+            if c not in E_ON_S:
+                gather(True, c, "v")
+
+    prep_u(0)
+    prep_v(0)
+    ts(T.ZA[:], T.CI[:], col("pg16"), col("kr"), A.is_equal, A.mult, "CI c_pg16 c_kr", "ZA")
+    ts(T.VF0[:], T.VI[:], col("pgx"), None, A.subtract, None, "VI c_pgx", "VF0")
+    wrap(AAW, T.ZA, lambda il: T.AW[:, 16 * il:4096:256], "ZA", "AW AWr")
+    op("s", "act", (T.XW[:, 4096:8192], T.XW[:, 0:4096], F.Copy), "X1", "X2")
+    cp(T.V16[:], T.VF0[:], "VF0", "V16")
+    cp(T.UG[:], T.UT[:, 0:4096].indirect(T.V16[:]), "UT V16", "UG")
+    cp(T.A16[:], AAW, "#M2", "A16")
+    for h in range(2):
+        cp(T.RW[:, 2048 * h:2048 * h + 2048], T.RI[:, 2048 * h:2048 * h + 2048], "RI%d" % h, "RW")
+    own_unit(0, [(3, smalls), (4, place_e), (4, gathers_e)])
+    ts(T.T0[:], T.MG[:], col("pg"), col("k4"), A.is_equal, A.mult, "MG c_pg c_k4", "T0")
+    ts(T.T1[:], T.CI[:, 0:128], col("pg"), col("kr"), A.is_equal, A.mult, "CI c_pg c_kr", "T1")
+    tt(T.SVE[:], T.T0[:], T.T1[:], A.add, "T0 T1", "SVE")
+    ts(T.DNM[:], T.CI[:, 0:128], col("p"), col("nk"), A.is_equal, A.mult, "CI c_p c_nk", "DNM")
+    ts(T.T0[:], T.MG[:], col("p"), None, A.is_equal, None, "MG c_p", "T0")
+    tt(T.EQM[:], T.IDM[:], T.T0[:], A.subtract, "IDM T0", "EQM")
+    ts(T.ZB[:], T.CI[:], col("pg16"), col("kb"), A.is_equal, A.mult, "CI c_pg16 c_kb", "ZB")
+    prep_u(1)
+    prep_v(1)
+    op("v", "set", (T.ALL1[:], 1.0), wr="ALL1")
+    op("v", "set", (T.ZERO[:], 0.0), wr="ZERO")
+    op("v", "set", (T.SC[:], 0.0), wr="SC")
+    ts(T.Z1[:], T.CI[:], col("pg16"), None, A.is_equal, None, "CI c_pg16", "Z1")
+    ts(T.T1[:], T.CI[:, 0:128], col("p"), None, A.is_gt, None, "CI c_p", "T1")
+    tt(T.TRI[:], T.T1[:], T.BLK[:], A.mult, "T1 BLK", "TRI")
+    ts(T.KD[:], T.KI[:], col("pg"), 1.0 / 4096, A.subtract, A.mult, "KI c_pg", "KD")
+    for t in range(NST):
+        op("s", "act", (T.PRES[:, 64 * t:64 * t + 64], T.RW[:, 8 + t:4096:64], F.Copy), "RW", "PRES%d" % t)
+    before("g", "pre", ["PRES%d" % t for t in range(NST)], [])
+    trs = []
+    for t in range(NST):
+        src = T.cores[(rank - 1 - t % (n_ranks - 1)) % n_ranks]
+        rid, pid = topo.addr(src)[:2]
+        e = topo.engines(core, src)
+        trs.append(RemoteDMATransfer(dst_ids=[DstId(rid=rid, pnc=pid)], dma_engine_mask=1 << e[t % len(e)], remote_sem=T.sem.pre,
+                                     src=T.PRES[:, 64 * t:64 * t + 64], dst=T.CB[:, CBW * t:CBW * t + 64]))
+    g.remote_dma_fused(trs, local_sem=T.sem.sent)
+    sent = NST
+    after(("pre", NST, {}), [], ["CB%d" % t for t in range(NST)])
+    count["pre"] = NST
+
+    for t in range(NST):
+        lastep = t == NST - 1
+        vf, vn = T["VF%d" % (t % 2)], T["VF%d" % ((t + 1) % 2)]
+        vfk, vnk = "VF%d" % (t % 2), "VF%d" % ((t + 1) % 2)
+        if t > 0 and t + 1 < NST:
+            prep_u(t + 1)
+            prep_v(t + 1)
+        if t > 0:
+            cp(T.BI[:], col("bs"), "c_bs", "BI")
+            ts(T.BI2[:], T.BI[:], 255, None, A.bitwise_and, None, "BI", "BI2")
+            ts(col("thb"), T.BI2[:], 8192.0, col("th"), A.mult, A.add, "BI2 c_th", "c_thb")
+        order = [c for c in E_ON_S] + [c for c in range(CH) if c not in E_ON_S]
+        for c in order:
+            diff(True, c, 0, c == order[-1])
+            if c == order[0]:
+                own_table(t)
+                op("s", "act", (T.IOG[:], T.IOT[:].indirect(T.A16[:]), F.Copy), "IOT A16", "IOG")
+            if c == order[EQ_AFTER]:
+                if t == 0:
+                    wraps()
+                mm(T.M2[:, 0:256], T.EQM[:], T.EG[:], True, True, "EQM EG", "#M2")
+                op("s", "act", (T.NEQ[:], T.M2[:, 0:256], F.Abs), "#M2", "NEQ", scale=33554432.0)
+        flush()
+        tt(T.DM[:], T.KOT[:].indirect(T.V16[:]), T.NEQ[:], A.add, "KOT V16 NEQ", "DM")
+        tt(T.DA[:], AVW, T.AAS[:], A.subtract, "#M2 AAS", "DA")
+        tt(T.MN[:], T.KE[:, 0:256], T.DM[:], A.min, "#KE DM", "MN")
+        ts(T.IND[:], T.MN[:], col("th" if t == 0 else "thb"), None, A.is_lt, None, "MN " + ("c_th" if t == 0 else "c_thb"), "IND")
+        ts(T.FV[:], T.MN[:], 4095, None, A.bitwise_and, None, "MN", "FV")
+        wrap(CNT, T.Z1, lambda il: T.IND[:, il::16], "Z1", "IND")
+        ts(T.FW[:], CNT, 7.5, None, A.is_gt, None, "#M2", "FW")
+        ts(T.NF[:], CNT, 7.5, 4096.0, A.is_lt, A.mult, "#M2", "NF")
+        mm(TOT, T.BLK[:], T.FW[:], True, True, "BLK FW", "#M2")
+        mm(TRI_, T.TRI[:], T.FW[:], True, True, "TRI FW", "#M2")
+        if not lastep:
+            mm(FITS, T.ALL1[:], T.FW[:], True, True, "ALL1 FW", "#M2")
+        tt(T.GD[:], T.NF[:], T.KD[:], A.mult, "NF KD", "GD")
+        op("v", "scan", (T.SC[:, 1:17], TOT, T.ZERO[:], 0.0, A.add, A.add), "#M2 ZERO SC", "SC")
+        tt(T.P1[:], TRI_, T.GD[:], A.add, "#M2 GD", "P1")
+        tt(T.DD[:], vf[:], T.NF[:], A.add, vfk + " NF", "DD")
+        tt(T.P2[:], T.P1[:], T.SC[:, 0:16], A.add, "P1 SC", "P2")
+        tt(T.MA[:], T.FW[:], T.DA[:], A.mult, "FW DA", "MA")
+        cp(T.C16[:], T.P2[:], "P2", "C16")
+        cp(T.D16[:], T.DD[:], "DD", "D16")
+        cp(T.CB[:, CBW * t:CBW * t + CBW].indirect(T.C16[:]), T.FV[:], "C16 FV CB%d" % t, "CB%d" % t)
+        dst = T.cores[(rank + 1 + t % (n_ranks - 1)) % n_ranks]
+        rid, pid = topo.addr(dst)[:2]
+        ne = len(topo.engines(core, dst))
+        before("g", "x", ["CB%d" % t], [])
+        g.remote_dma(T.LAND[:, 64 * t:64 * t + 64], T.CB[:, CBW * t:CBW * t + 64], T.sem["arr%d" % t], T.sem.sent, pid, rid, topo.mask(core, dst))
+        sent += ne
+        after(("arr%d" % t, ne, {}), [], ["LAND%d" % t])
+        count["arr%d" % t] = ne
+        if lastep:
+            cp(T.RW[:].indirect(T.D16[:]), T.FV[:], "D16 FV", "RW")
+        tt(T.AN[:], T.MA[:], T.AAS[:], A.add, "MA AAS", "AN")
+        tt(vn[:], vf[:], T.FW[:], A.add, vfk + " FW", vnk)
+        cp(T.AW[:].indirect(T.D16[:]), T.IOG[:], "D16 IOG", "AW AWr")
+        cp(T.A16[:], T.AN[:], "AN", "A16")
+        cp(T.V16[:], vn[:], vnk, "V16")
+        if not lastep:
+            cp(T.RW[:].indirect(T.D16[:]), T.FV[:], "D16 FV", "RW")
+            cp(T.UG[:], T.UT[:, 0:4096].indirect(T.V16[:]), "UT V16", "UG")
+            own_unit(t + 1, [(2, fits), (HOOK, smalls), (WHOOK, wraps), (EHOOK, lambda: merge(t)), (EHOOK, place_e), (EHOOK, gathers_e), (4, lambda: keep_yh(t))])
+
+    for s in range(4):
+        w, h = s // 2, s % 2
+        o, wk = T["W%d" % w][:, 512 * h:512 * h + 256], "#W%d_%d" % (w, h)
+        op("s", "act", (o, T.RW[:, 4 + s:4096:16], F.Copy), "RW", wk, scale=4096.0)
+        tt(T.KOT[:, s:1024:4], o, T.RW[:, s:4096:16], A.add, "RW " + wk, "YR%d" % s)
+    dma("y", T.yr[:], T.KOT[:, 0:1024], rd="YR0 YR1 YR2 YR3")
+    op("s", "act", (T.IOG[:], T.IOT[:].indirect(T.A16[:]), F.Copy), "IOT A16", "IOG")
+    cp(T.SVG[:], T.IOT[:].indirect(T.V16[:]), "IOT V16", "SVG")
+    keep_yh(NST - 1)
+    dma("y", T.yh[:], T.YH[:], rd="YH")
+    for s in range(8):
+        w, h = s // 2 % 2, s % 2
+        o, wk = T["W%d" % w][:, 512 * h:512 * h + 256], "#W%d_%d" % (w, h)
+        mm(o, T.SVR[:], T.AW[:, s:4096:16], True, True, "SVR AW AWr", wk)
+        if h:
+            op("s", "act", (T.KOT[:, 2048 + s::8], o, F.Copy), wk, "YAN%d" % s)
+        else:
+            cp(T.KOT[:, 2048 + s::8], o, wk, "YAN%d" % s)
+    mm(T.KO[:, 0:256], T.SVR[:], T.SVG[:], True, True, "SVR SVG", "#KO")
+    mm(T.KO[:, 256:512], T.SVR[:], T.IOG[:], True, True, "SVR IOG", "#KO")
+    op("s", "act", (T.YVA[:], T.KO[:], F.Copy), "#KO", "YVA")
+    dma("y", T.yan[:], T.KOT[0::16, 2048:4096], rd=" ".join("YAN%d" % s for s in range(8)))
+    dma("y", T.yv[:], T.YVA[0::16, 0:256], rd="YVA")
+    dma("y", T.ya[:], T.YVA[0::16, 256:512], rd="YVA")
+    count["sent"] = sent
+    for s in count:
+        if seen["g"].get(s, 0) < count[s]:
+            g.wait_ge(T.sem[s], count[s])

@@ -1,51 +1,132 @@
 from concourse.bass import DstId, RemoteDMATransfer
 from concourse.mybir import AluOpType as A, AxisListType, ActivationFunctionType as F
 
-NST, CH = 8, 4
-HOOK, WHOOK, EHOOK, EQ_AFTER = 3, 4, 4, 2
+NST = 8
 NEG = -255.0 * 65536.0
-CBW = 768
-E_ON_S = ()
-O_ON_V = ()
+CBW = 320
+XA = 9216
+GATH = ((0, 2, "s"), (2, 2, "v"), (4, 2, "v"), (6, 1, "v"), (7, 1, "v"))
+SIZES = ((0, 2, "s"), (2, 2, "s"), (4, 2, "s"), (6, 2, "v"))
+BANK = (0, 1, 2, 3, 0, 1, 2, 3)
+SUMS = ((0, 2), (2, 2), (4, 2), (6, 2))
+CUT, NEQ_ON, ROUNDS, X2_BY = 128, "s", 3, "y"
+PLACES = (0, 128, 256)
+OWN = ((2, "s"),) * 8
+OWN0 = ((4, "s"), (4, "v"), (4, "s"), (4, "s"))
+NB = 3
+DIRECT, FOLDS, FLAT = 1, 2, 21.0
+PARK = (("XW", 0), ("XW", 4096), ("XW", 8192), ("AW", 0), ("AW", 4096), ("SV", 0), ("GE", 0), ("GO0", 0))
+CYC, FIX, PCY, HOP, GA, SC_, DFIX, DBW, RLAT = 0.83e-3, 0.065, 0.417e-3, 0.06, 1.56, 3.8, 1.8, 500e3, 3.6
 
 SCRATCH = {}
 for _n, _s, _d in (
         ("XW", 12288, "bfloat16"), ("RI", 4096, "int32"), ("RW", 8192, "float32"), ("AW", 8192, "bfloat16"),
-        ("IOT", 4096, "bfloat16"), ("LOW", 4096, "bfloat16"), ("SV", 4096, "bfloat16"), ("UT", 4096, "int32"),
+        ("SV", 4096, "bfloat16"), ("SEL", 2048, "bfloat16"),
         ("KOT", 4096, "float32"), ("CB", NST * CBW, "float32"), ("LAND", NST * 64, "float32"), ("PRES", NST * 64, "float32"),
-        ("GE", 4096, "bfloat16"), ("GO", 4096, "bfloat16"),
-        ("AB0", 1024, "bfloat16"), ("AB1", 1024, "bfloat16"),
-        ("AR", 512, "int32"), ("ARS", 1024, "int32"), ("ARB", 1040, "bfloat16"),
-        ("WI", 1, "int32"), ("TI", 1, "int32"), ("PI", 1, "int32"), ("PGI", 1, "int32"), ("PKI", 1, "int32"), ("KCI", 1, "int32"),
-        ("BI", 1, "int32"), ("BI2", 1, "int32"), ("COL", 32, "float32"),
-        ("CI", 144, "int32"), ("MG", 128, "int32"), ("T0", 128, "float32"), ("T1", 128, "float32"),
-        ("IDM", 128, "bfloat16"), ("NID", 128, "bfloat16"), ("Z8", 144, "bfloat16"), ("Z1", 144, "bfloat16"),
-        ("ZA", 144, "bfloat16"), ("ZB", 144, "bfloat16"), ("EQM", 128, "float32"), ("DNM", 128, "float32"),
-        ("SVE", 128, "bfloat16"), ("SVR", 128, "bfloat16"), ("SVK", 128, "bfloat16"), ("TRI", 128, "bfloat16"),
-        ("BLK", 128, "bfloat16"), ("ALL1", 128, "bfloat16"), ("WM", 128, "bfloat16"),
+        ("GE", 4096, "bfloat16"), ("GO0", 4096, "bfloat16"), ("GO1", 4096, "bfloat16"),
+        ("GO2", 4096, "bfloat16"), ("GO3", 4096, "bfloat16"), ("Q40", 1024, "bfloat16"), ("Q41", 1024, "bfloat16"), ("BM", 128, "bfloat16"),
+        ("AB", 4096, "bfloat16"), ("ZB", 16, "bfloat16"), ("AR", 768, "int32"), ("ARB", 1536, "bfloat16"),
+        ("WI", 1, "int32"), ("TI", 1, "int32"), ("PI", 1, "int32"), ("PGI", 1, "int32"), ("PKI", 1, "int32"), ("PK2", 1, "int32"),
+        ("KCI", 1, "int32"), ("KCM", 1, "int32"), ("KCH", 1, "bfloat16"), ("BI", 1, "int32"), ("BI2", 1, "int32"), ("COL", 32, "float32"),
+        ("CI", 144, "int32"), ("MG", 128, "int32"), ("DNG", 128, "bfloat16"), ("T2", 128, "float32"), ("T3", 128, "float32"),
+        ("IDM", 128, "bfloat16"), ("NID", 128, "bfloat16"), ("Z8", 144, "bfloat16"), ("Z16", 144, "bfloat16"), ("ZM", 144, "bfloat16"),
+        ("Z1", 144, "bfloat16"), ("ZA", 144, "bfloat16"), ("ZR", 144, "bfloat16"),
+        ("ZW", 144, "bfloat16"), ("EQM", 128, "float32"), ("DNM", 128, "float32"), ("DKH", 128, "bfloat16"), ("DKL", 128, "bfloat16"),
+        ("SVE", 128, "bfloat16"), ("SVA", 128, "bfloat16"), ("SVK", 128, "bfloat16"), ("TRI", 128, "bfloat16"),
+        ("BLK", 128, "bfloat16"), ("ALL1", 256, "bfloat16"), ("WM", 128, "bfloat16"),
         ("VI", 16, "int32"), ("KI", 16, "int32"), ("KD", 16, "float32"), ("ZERO", 16, "float32"), ("SC", 32, "float32"),
-        ("VF0", 16, "float32"), ("VF1", 16, "float32"), ("AAS", 16, "float32"), ("DA", 16, "float32"), ("MA", 16, "float32"),
-        ("AN", 16, "float32"), ("FW", 16, "bfloat16"), ("NF", 16, "float32"), ("GD", 16, "float32"), ("P1", 16, "float32"),
-        ("P2", 16, "float32"), ("DD", 16, "float32"), ("JK", 16, "float32"),
-        ("A16", 16, "uint16"), ("V16", 16, "uint16"), ("D16", 16, "uint16"), ("C16", 16, "uint16"),
-        ("QG", 256, "bfloat16"), ("SVG", 256, "bfloat16"), ("AWG", 256, "bfloat16"), ("IOG", 256, "bfloat16"),
-        ("EG", 256, "float32"), ("UG", 256, "float32"), ("TA", 256, "int32"), ("TB", 256, "int32"), ("TC", 256, "int32"),
-        ("PLE", 256, "uint16"), ("PLO0", 256, "uint16"), ("PLO1", 256, "uint16"), ("UC", 256, "int32"),
-        ("OA", 256, "int32"), ("OB", 256, "int32"), ("OC", 256, "int32"),
+        ("AAS", 32, "float32"), ("DA", 16, "float32"), ("MA", 16, "float32"),
+        ("FW", 16, "bfloat16"), ("NF", 16, "float32"), ("GD", 16, "float32"), ("P1", 16, "float32"), ("JK", 16, "float32"),
+        ("AV", 32, "uint16"), ("V16", 16, "uint16"), ("D16", 16, "uint16"), ("C16", 16, "uint16"),
+        ("QG", 256, "bfloat16"), ("QT", 256, "bfloat16"), ("AG", 512, "bfloat16"), ("IOG", 256, "bfloat16"),
+        ("EK", 256, "float32"), ("UG", 256, "int32"), ("TA", 256, "int32"), ("TB", 256, "int32"), ("UC", 256, "int32"),
+        ("PLE", 256, "uint16"), ("OU", 128, "int32"), ("OA", 128, "int32"), ("OB", 128, "int32"),
         ("NEQ", 256, "float32"), ("DM", 256, "float32"), ("MN", 256, "int32"), ("IND", 256, "bfloat16"), ("FV", 256, "int32"),
         ("YH", 512, "float32"), ("YVA", 512, "float32")):
     SCRATCH[_n] = ("sbuf", [128, _s], _d)
-for _n, _s in (("W0", 1024), ("W1", 1024), ("KE", 512), ("KO", 512), ("M1", 512), ("M2", 512)):
+SCRATCH["PLO"] = ("sbuf", [128, NST, 256], "uint16")
+for _n, _s in (("W0", 1024), ("W1", 1024), ("W2", 512), ("KE", 512), ("KO", 512), ("M2", 512)):
     SCRATCH[_n] = ("psum", [128, _s], "float32")
-SEMAPHORES = ["qv", "qs", "qp", "qg", "pre", "sent"] + ["arr%d" % t for t in range(NST)] + ["d%d" % i for i in range(28)]
+SEMAPHORES = ["qv", "qs", "qp", "qg", "pre", "sent"] + ["arr%d" % t for t in range(NST)] + ["d%d" % i for i in range(32)]
+SEMAPHORES += ["%s%d_%d" % (n, c, f) for n in ("hf", "mx") for c in range(NST) for f in range(2)]
+
+
+def issue_order(tasks):
+    last, readers, preds = {}, {}, []
+    for j, (q, rd, wr, cost, lat, emit) in enumerate(tasks):
+        p = [last[k] for k in rd + wr if k in last] + [i for k in wr for i in readers.get(k, ())]
+        p += [i for k in rd if k[0] == "#" for i in readers.get(k, ()) if tasks[i][0] != q]
+        p = {i: -tasks[i][4] if q == "p" == tasks[i][0] else HOP for i in p if i != j}
+        preds.append(p)
+        for k in wr:
+            last[k], readers[k] = j, []
+        for k in rd:
+            readers.setdefault(k, []).append(j)
+    every = range(len(tasks))
+    back = [{} for j in every]
+    way = [0.0] * len(tasks)
+    for j in reversed(every):
+        way[j] += tasks[j][3] + tasks[j][4]
+        for i, h in preds[j].items():
+            preds[j][i] = back[i][j] = h + tasks[i][4]
+            way[i] = max(way[i], way[j] + h)
+
+    def lay(order, edges, tail):
+        end, taken = {}, {}
+        for j in order:
+            q, cost = tasks[j][0], tasks[j][3]
+            t = max([end[i] + h for i, h in edges[j].items()] + [tasks[j][4] if tail else 0.0])
+            slots = taken.setdefault(q, [])
+            n = len(slots)
+            while n and slots[n - 1][1] > t:
+                n -= 1
+            while n < len(slots) and slots[n][0] < t + cost - 1e-9:
+                t = max(t, slots[n][1])
+                n += 1
+            slots.insert(n, (t, t + cost))
+            end[j] = t + cost
+        return end, max(end[j] + (0.0 if tail else tasks[j][4]) for j in every)
+
+    end, span = lay(sorted(every, key=lambda j: (-way[j], j)), preds, False)
+    best = (span, end)
+    for _ in range(ROUNDS):
+        late = lay(sorted(every, key=lambda j: (-end[j], -j)), back, True)[0]
+        end, span = lay(sorted(every, key=lambda j: (-late[j], j)), preds, False)
+        if span < best[0]:
+            best = (span, end)
+    end = best[1]
+    return sorted(every, key=lambda j: (end[j] - tasks[j][3], j))
+
+
+def helper(core, T, topo):
+    return [c for c in topo.cores_of(core) if c not in T.cores and topo.die(c) == topo.die(core)][0]
+
+
+def hand_back(g, core, owner, T, topo):
+    rid, pid = topo.addr(owner)[:2]
+    off_chip = set(e for other in T.cores if other != owner for e in topo.engines(owner, other))
+    n_in = len([e for e in topo.engines(owner, core) if e not in off_chip])
+    w, n = 4096 // FOLDS, 0
+    for c in range(DIRECT, NST):
+        name, c0 = PARK[c]
+        for f in range(FOLDS):
+            g.wait_ge(T.sem["hf%d_%d" % (c, f)], n_in)
+            g.remote_dma(T["GO%d" % (c % NB)][:, w * f:w * f + w], T[name][:, c0 + w * f:c0 + w * f + w], T.sem["mx%d_%d" % (c, f)],
+                         T.sem.sent, pid, rid, topo.mask(core, owner))
+            n += len(topo.engines(core, owner))
+    g.wait_ge(T.sem.sent, n)
 
 
 def rank_program(g, core, T, topo):
     rank = T.rank_of(core)
     if rank is None:
+        for other in T.cores:
+            if helper(other, T, topo) == core:
+                hand_back(g, core, other, T, topo)
         return
     n_ranks = len(T.cores)
     queue = {"v": g.vector, "s": g.scalar, "p": g.tensor, "g": g, "y": g.sync}
+    tasks = []
     seen = {q: {} for q in queue}
     count = {}
     last, readers = {}, {}
@@ -60,7 +141,7 @@ def rank_program(g, core, T, topo):
 
     def before(q, own, rd, wr):
         for k in rd:
-            if k in last:
+            if k in last and (q != "p" or last[k][0] != own):
                 need(q, last[k])
             if k[0] == "#":
                 for s, tok in readers.get(k, {}).items():
@@ -70,7 +151,8 @@ def rank_program(g, core, T, topo):
             if k in last and (q != "p" or last[k][0] != own):
                 need(q, last[k])
             for s, tok in readers.get(k, {}).items():
-                need(q, tok)
+                if q != "p" or s != own:
+                    need(q, tok)
 
     def after(tok, rd, wr):
         for k in wr:
@@ -79,51 +161,43 @@ def rank_program(g, core, T, topo):
         for k in rd:
             readers.setdefault(k, {})[tok[0]] = tok
 
-    def split(keys):
-        return keys.split() if keys else []
+    def op(q, call, rd, wr, cost):
+        rd, wr, own = rd.split(), wr.split(), "q" + q
 
-    def op(q, name, args, rd="", wr="", **kw):
-        rd, wr, own = split(rd), split(wr), "q" + q
-        before(q, own, rd, wr)
-        eng = queue[q]
-        fns = {"copy": ("v", lambda: eng.tensor_copy(*args)), "tt": ("v", lambda: eng.tensor_tensor(*args)),
-               "ts": ("v", lambda: eng.tensor_scalar(*args)), "act": ("s", lambda: eng.activation(*args, **kw)),
-               "mm": ("p", lambda: eng.matmul(*args)), "scan": ("v", lambda: eng.tensor_tensor_scan(*args)),
-               "red": ("v", lambda: eng.tensor_reduce(*args)), "set": ("v", lambda: eng.memset(*args)),
-               "iota": ("g", lambda: eng.iota(*args, **kw))}
-        fns[name][1]().then_inc(T.sem[own], 1)
-        count[own] = count.get(own, 0) + 1
-        after((own, count[own], dict(seen[q])), rd, wr)
+        def emit():
+            before(q, own, rd, wr)
+            call().then_inc(T.sem[own], 1)
+            count[own] = count.get(own, 0) + 1
+            after((own, count[own], dict(seen[q])), rd, wr)
+        tasks.append((q, rd, wr, cost, 0.1 if q == "p" else 0.0, emit))
 
     dmas = [0]
 
-    def dma(q, out, in_, rd="", wr=""):
-        rd, wr = split(rd), split(wr)
+    def dma(out, in_, nbytes, rd="", wr=""):
+        rd, wr = rd.split(), wr.split()
         s = "d%d" % dmas[0]
         dmas[0] += 1
-        before(q, s, rd, wr)
-        queue[q].dma_start(out, in_).then_inc(T.sem[s], 16)
-        count[s] = 16
-        after((s, 16, dict(seen[q])), rd, wr)
 
-    def mm(out, lhs, rhs, start, stop, rd, wr):
-        op("p", "mm", (out, lhs, rhs, start, stop), rd, wr)
+        def emit():
+            before("y", s, rd, wr)
+            g.sync.dma_start(out, in_).then_inc(T.sem[s], 16)
+            count[s] = 16
+            after((s, 16, dict(seen["y"])), rd, wr)
+        tasks.append(("y", rd, wr, 0.05 + nbytes / DBW, DFIX, emit))
 
-    dma("y", T.AR[:, 0:256], T.rf[0::16, :], wr="AR0")
-    dma("y", T.AR[:, 256:512], T.an[:, :], wr="AR1")
-    dma("y", T.WI[:], T.w[:], wr="WI")
-    dma("y", T.TI[:], T.th[:], wr="TI")
-    dma("y", T.XW[:, 0:4096], T.xc[:], wr="X1")
-    dma("y", T.XW[:, 8192:12288], T.xc[:], wr="X3")
-    for h in range(2):
-        dma("y", T.RI[:, 2048 * h:2048 * h + 2048], T.rf[:, 2048 * h:2048 * h + 2048], wr="RI%d" % h)
+    sent = [0]
 
-    op("g", "iota", (T.PI[:], [[0, 1]], 0, 1), wr="PI")
-    op("g", "iota", (T.CI[:], [[1, 144]], 0, 0), wr="CI")
-    op("g", "iota", (T.VI[:], [[256, 16]], 0, 16), wr="VI")
-    op("g", "iota", (T.KI[:], [[16, 16]], 256, 1), wr="KI")
-    op("g", "iota", (T.LOW[:], [[0, 64], [1, 64]], 0, 0), wr="LOW", allow_small_or_imprecise_dtypes=True)
-    op("g", "iota", (T.IOT[:], [[1, 64], [0, 64]], 0, 0), wr="IOT", allow_small_or_imprecise_dtypes=True)
+    def remote(call, rd, wr, sem, n, lat, n_sent, back=True):
+        def emit():
+            before("g", "x", rd, wr if back else [])
+            call()
+            sent[0] += n_sent
+            after((sem, n, dict(seen["g"]) if back else {}), rd if back else [], wr)
+            count[sem] = n
+        tasks.append(("g", rd, wr, 0.6, lat, emit))
+
+    def mm(out, lhs, rhs, start, stop, rd, wr, cy=64):
+        op("p", lambda: g.tensor.matmul(out, lhs, rhs, start, stop), rd, wr, cy * PCY)
 
     ncol = {}
 
@@ -132,307 +206,413 @@ def rank_program(g, core, T, topo):
             ncol[name] = len(ncol)
         return T.COL[:, ncol[name]:ncol[name] + 1]
 
-    def ts(out, in0, s1, s2, o0, o1, rd, wr):
-        op("v", "ts", (out, in0, s1, s2, o0) if o1 is None else (out, in0, s1, s2, o0, o1), rd, wr)
+    def ts(out, in0, s1, s2, o0, o1, rd, wr, cy=16):
+        args = (out, in0, s1, s2, o0) if o1 is None else (out, in0, s1, s2, o0, o1)
+        op("v", lambda: g.vector.tensor_scalar(*args), rd, wr, FIX + cy * CYC)
 
-    def tt(out, a, b, o, rd, wr):
-        op("v", "tt", (out, a, b, o), rd, wr)
+    def tt(out, a, b, o, rd, wr, cy=16):
+        op("v", lambda: g.vector.tensor_tensor(out, a, b, o), rd, wr, FIX + cy * CYC)
 
-    def cp(out, in_, rd, wr):
-        op("v", "copy", (out, in_), rd, wr)
+    def cp(out, in_, rd, wr, cy=16):
+        op("v", lambda: g.vector.tensor_copy(out, in_), rd, wr, FIX + cy * CYC)
 
-    SVall = "SV0 SV1 SV2 SV3 SVx"
-    Xall = "X1 X2 X3"
-    op("v", "set", (T.SV[:], 1.0), wr=SVall)
-    op("s", "act", (T.AW[:, 0:4096], T.SV[:], F.Copy), SVall, "AW AWr")
-    op("v", "set", (T.ARB[:, 1024:1040], 0.0), wr="pad")
-    ts(T.ARS[:, 0:512], T.AR[:], 6, None, A.arith_shift_right, None, "AR0 AR1", "ARS0")
-    ts(T.ARS[:, 512:1024], T.AR[:], 63, None, A.bitwise_and, None, "AR0 AR1", "ARS1")
-    cp(T.ARB[:, 0:1024], T.ARS[:], "ARS0 ARS1", "ARB")
-    dma("y", T.SV[0::16, :], T.ARB[:, 0:256], rd="ARB", wr="SV0")
-    dma("y", T.SV[1::16, :], T.ARB[:, 512:768], rd="ARB", wr="SV1")
-    dma("y", T.SV[2::16, :], T.ARB[:, 257:513], rd="ARB", wr="SV2")
-    dma("y", T.SV[3::16, :], T.ARB[:, 769:1025], rd="ARB pad", wr="SV3")
-    dma("y", T.AW[0::16, 0:4096], T.ARB[:, 256:512], rd="ARB", wr="AW")
-    dma("y", T.AW[1::16, 0:4096], T.ARB[:, 768:1024], rd="ARB", wr="AWr")
-    dma("y", T.IOT[1::16, :], T.LOW[0:8, :], rd="LOW", wr="IOT")
-    op("v", "copy", (col("p"), T.PI[:]), "PI", "c_p")
+    def fill(out, x, wr, cy=16):
+        op("v", lambda: g.vector.memset(out, x), "", wr, FIX + cy * CYC)
+
+    def act(out, in_, f, rd, wr, cy=16, **kw):
+        op("s", lambda: g.scalar.activation(out, in_, f, **kw), rd, wr, FIX + cy * CYC)
+
+    def iota(out, pattern, base, mult, wr, n):
+        op("g", lambda: g.iota(out, pattern, base, mult), "", wr, 0.13 + 2 * n * CYC)
+
+    def select(out, in_, pattern, mult, rd, wr, n):
+        op("g", lambda: g.affine_select(out, in_, pattern, A.is_equal, 0.0, 0, mult), rd, wr, 0.17 + 2 * n * CYC)
+
+    dma(T.AR[:, 0:256], T.rf[0::16, :], 1 << 17, wr="AR0")
+    dma(T.AR[:, 256:512], T.an[:, :], 1 << 17, wr="AR1")
+    dma(T.WI[:], T.w[:], 512, wr="WI")
+    dma(T.TI[:], T.th[:], 512, wr="TI")
+    dma(T.XW[:, 0:4096], T.xc[:], 1 << 20, wr="X1")
+    for h in range(4):
+        dma(T.RI[:, 1024 * h:1024 * h + 1024], T.rf[:, 1024 * h:1024 * h + 1024], 1 << 19, wr="RI%d" % h)
+    iota(T.PI[:], [[0, 1]], 0, 1, "PI", 1)
+    iota(T.CI[:], [[1, 144]], 0, 0, "CI", 144)
+    iota(T.AR[:, 512:768], [[1, 256]], 0, 256, "AR2", 256)
+    iota(T.VI[:], [[256, 16]], 0, 16, "VI", 16)
+    iota(T.KI[:], [[-16, 16]], 319, -1, "KI", 16)
+
+    SVall, AWall = "SV0 SV1 SV8 SV9", "AW0 AW1 AW8 AW9"
+    Xown, Xall = "X1 X2 X3a", "X1 X2 X3a X3b"
+    A16, V1 = T.AV[:, 0:16], T.AV[:, 16:32]
+    fill(T.SEL[:], 1.0, "SEL", 1024)
+    dma(T.AW[:, 0:4096], T.xc[:], 1 << 20, wr=AWall)
+    select(T.SEL[:], T.SEL[:], [[-1, 128], [0, 16]], 1, "SEL", "SEL", 2048)
+    fill(T.SV[:], 1.0, SVall, 2048)
+    ts(T.AR[:, 512:768], T.AR[:, 512:768], 4095, None, A.bitwise_and, None, "AR2", "AR2", 256)
+    for j in range(3):
+        a, b = 256 * j, 256 * j + 256
+        cp(T.ARB[:, a:b], T.AR[:, a:b], "AR%d" % j, "H%d" % j, 256)
+        tt(T.ARB[:, 768 + a:768 + b], T.AR[:, a:b], T.ARB[:, a:b], A.subtract, "AR%d H%d" % (j, j), "L%d" % j, 512)
+
+    def rows(name, row, j, shift=0):
+        for h in range(2):
+            dma(T[name][row + h::16, shift:4096 + shift], T.ARB[:, 768 * h + 256 * j:768 * h + 256 * j + 256], 1 << 16,
+                rd="HL"[h] + str(j), wr=name + str(row + h))
+
+    rows("SV", 0, 0)
+    rows("AW", 8, 1)
+    rows("SV", 8, 2)
+    rows("AW", 0, 0, 1)
+
+    cp(col("p"), T.PI[:], "PI", "c_p")
     ts(T.PGI[:], T.PI[:], 112, None, A.bitwise_and, None, "PI", "PGI")
     ts(T.PKI[:], T.PI[:], 15, None, A.bitwise_and, None, "PI", "PKI")
-    ts(T.MG[:], T.CI[:, 0:128], 112, None, A.bitwise_and, None, "CI", "MG")
+    ts(T.PK2[:], T.PI[:], 1, 7, A.arith_shift_right, A.bitwise_and, "PI", "PK2")
+    ts(T.MG[:], T.CI[:, 0:128], 112, None, A.bitwise_and, None, "CI", "MG", 128)
     cp(col("pg"), T.PGI[:], "PGI", "c_pg")
     ts(col("pg16"), T.PGI[:], 16.0, None, A.add, None, "PGI", "c_pg16")
     ts(col("pgx"), T.PGI[:], 16.0, None, A.mult, None, "PGI", "c_pgx")
-    ts(col("k0"), T.PKI[:], 0.0, 64.0, A.is_equal, A.mult, "PKI", "c_k0")
-    ts(col("k1"), T.PKI[:], 1.0, None, A.is_equal, None, "PKI", "c_k1")
-    ts(col("k2"), T.PKI[:], 2.0, 64.0, A.is_equal, A.mult, "PKI", "c_k2")
-    ts(col("k3"), T.PKI[:], 3.0, None, A.is_equal, None, "PKI", "c_k3")
+    for name, pair in (("kr", 0), ("ka", 4)):
+        ts(col(name), T.PK2[:], float(pair), None, A.is_equal, None, "PK2", "c_" + name)
     ts(col("k4"), T.PKI[:], 4.0, NEG, A.is_equal, A.mult, "PKI", "c_k4")
     ts(col("k5"), T.PKI[:], 5.0, 4096.0, A.is_equal, A.mult, "PKI", "c_k5")
     ts(col("nk"), T.PKI[:], 0.0, None, A.is_gt, None, "PKI", "c_nk")
-    ts(T.KCI[:], T.PKI[:], 613.0, None, A.mult, None, "PKI", "KCI")
-    tt(col("kr"), col("k0"), col("k1"), A.add, "c_k0 c_k1", "c_kr")
-    tt(col("kb"), col("k2"), col("k3"), A.add, "c_k2 c_k3", "c_kb")
-    ts(T.BI[:], T.KCI[:], 4095, None, A.bitwise_and, None, "KCI", "BI")
     tt(col("k45"), col("k4"), col("k5"), A.add, "c_k4 c_k5", "c_k45")
-    cp(col("kc"), T.BI[:], "BI", "c_kc")
     tt(col("kk"), col("kr"), col("k45"), A.add, "c_kr c_k45", "c_kk")
-    ts(T.IDM[:], T.CI[:, 0:128], col("p"), None, A.is_equal, None, "CI c_p", "IDM")
-    ts(T.NID[:], T.CI[:, 0:128], col("p"), -1.0, A.is_equal, A.mult, "CI c_p", "NID")
-    ts(T.BLK[:], T.MG[:], col("pg"), None, A.is_equal, None, "MG c_pg", "BLK")
-    ts(T.SVR[:], T.MG[:], col("pg"), col("kr"), A.is_equal, A.mult, "MG c_pg c_kr", "SVR")
     cp(col("w"), T.WI[:], "WI", "c_w")
     ts(col("th"), T.TI[:], 8192.0, NEG, A.mult, A.add, "TI", "c_th")
-    ts(T.WM[:], T.MG[:], col("pg"), col("w"), A.is_equal, A.mult, "MG c_pg c_w", "WM")
-    ts(T.SVK[:], T.MG[:], col("pg"), col("kk"), A.is_equal, A.mult, "MG c_pg c_kk", "SVK")
-    ts(T.Z8[:], T.CI[:], col("pg16"), 8192.0, A.is_equal, A.mult, "CI c_pg16", "Z8")
+    ts(T.KCI[:], T.PKI[:], 613.0, None, A.mult, None, "PKI", "KCI")
+    ts(T.KCM[:], T.KCI[:], 4095, None, A.bitwise_and, None, "KCI", "KCM")
+    cp(col("kc"), T.KCM[:], "KCM", "c_kc")
+    cp(T.KCH[:], T.KCM[:], "KCM", "KCH")
+    ts(col("kq"), T.KCM[:], -33554432.0, None, A.mult, None, "KCM", "c_kq")
+    tt(col("kl"), T.KCH[:], T.KCM[:], A.subtract, "KCH KCM", "c_kl")
+    ts(col("kh"), T.KCH[:], -1.0, None, A.mult, None, "KCH", "c_kh")
 
-    def prep_u(c):
-        mm(T.M1[:, 0:256], T.WM[:], T.XW[:, c:4096:16], True, True, "WM X1", "#M1")
-        mm(T.M1[:, 256:512], T.SVR[:], T.SV[:, c::16], True, True, "SVR " + SVall, "#M1")
+    ts(T.Z1[:], T.CI[:], col("pg16"), None, A.is_equal, None, "CI c_pg16", "Z1", 144)
+    ts(T.BLK[:], T.MG[:], col("pg"), None, A.is_equal, None, "MG c_pg", "BLK", 128)
+    ts(T.IDM[:], T.CI[:, 0:128], col("p"), None, A.is_equal, None, "CI c_p", "IDM", 128)
+    for base, names in (("Z1", (("ZW", "w"), ("ZR", "kr"), ("ZA", "ka"), ("Z8", 8192.0), ("Z16", 16384.0), ("ZM", -8192.0))),
+                        ("BLK", (("WM", "w"), ("SVK", "kk"), ("SVA", "ka"), ("BM", -8192.0))),
+                        ("IDM", (("NID", -1.0), ("DNG", NEG), ("DKH", "kh"), ("DKL", "kl"), ("DNM", "nk")))):
+        for name, x in names:
+            if isinstance(x, float):
+                act(T[name][:], T[base][:], F.Copy, base, name, 144, scale=x)
+            else:
+                act(T[name][:], T[base][:], F.Copy, base + " c_" + x, name, 144, scale=col(x))
+    fill(T.ALL1[:], 1.0, "ALL1", 128)
+    fill(T.ZERO[:], 0.0, "ZERO")
+    fill(T.ZB[:], 0.0, "ZB")
+    fill(T.SC[:], 0.0, "SC")
+    ts(T.SVE[:], T.CI[:, 0:128], col("pg"), col("kr"), A.is_equal, A.mult, "CI c_pg c_kr", "SVE", 128)
+    ts(T.T2[:], T.MG[:], col("p"), None, A.is_equal, None, "MG c_p", "T2", 128)
+    tt(T.EQM[:], T.IDM[:], T.T2[:], A.subtract, "IDM T2", "EQM", 256)
+    ts(T.T3[:], T.CI[:, 0:128], col("p"), None, A.is_gt, None, "CI c_p", "T3", 128)
+    tt(T.TRI[:], T.T3[:], T.BLK[:], A.mult, "T3 BLK", "TRI", 256)
+    ts(T.KD[:], T.KI[:], col("pg"), 1.0 / 4096, A.add, A.mult, "KI c_pg", "KD")
+    ts(T.V16[:], T.VI[:], col("pgx"), None, A.subtract, None, "VI c_pgx", "V16")
+    ts(V1, T.VI[:], col("pgx"), 1.0, A.subtract, A.add, "VI c_pgx", "V1")
 
-    def prep_v(c):
-        cp(T.UC[:], T.M1[:, 0:256], "#M1", "UC")
-        ts(T.UT[:, c::16], T.UC[:], 4095, None, A.bitwise_and, None, "UC", "UT")
-        tt(T.OA[:], T.M1[:, 256:512], T.UT[:, c::16], A.mult, "#M1 UT", "OA")
-        ts(T.OB[:], T.OA[:], 5, 4095, A.arith_shift_right, A.bitwise_and, "OA", "OB")
-        tt(T.OC[:], T.M1[:, 256:512], T.OB[:], A.add, "#M1 OB", "OC")
-        ts(T["PLO%d" % (c % 2)][:], T.OC[:], col("kc"), None, A.add, None, "OC c_kc", "PLO%d" % (c % 2))
-
-    turn = [0]
-
-    def gather(e, c, q, b=0):
-        G, pl = (T.GE, "PLE") if e else (T.GO, "PLO%d" % (b % 2))
-        src = T.XW[:].indirect(T[pl][:, 64 * c:64 * c + 64])
-        out = G[:, 1024 * c:1024 * c + 1024]
-        key = ("GE%d" if e else "GO%d") % c
-        if q == "v":
-            cp(out, src, Xall + " " + pl, key)
-        else:
-            op("s", "act", (out, src, F.Copy), Xall + " " + pl, key)
-
-    pending = []
-
-    def sums(item):
-        e, c, w, b = item
-        K, key = (T.KE, "#KE") if e else (T.KO, "#KO")
-        o = K[:, 64 * c:64 * c + 64]
-        for h in range(2):
-            if h == 0 and e:
-                mm(o, T.SVE[:], T.SVG[:, 64 * c:64 * c + 64], True, False, "SVE SVG", key)
-                mm(o, T.DNM[:], T.EG[:, 64 * c:64 * c + 64], False, False, "DNM EG", key)
-            elif h == 0:
-                mm(o, T.SVK[:], T.SV[:, 1024 * c + b:1024 * c + 1024:16], True, False, "SVK " + SVall, key)
-            for k in range(8 * h, 8 * h + 8):
-                mm(o, T.Z8[:, 16 - k:144 - k], T["AB%d" % w][:, 64 * k:64 * k + 64], False, k == 15, "Z8 AB%d_%d" % (w, h), key)
-
-    def diff(e, c, b=0, halves=False):
-        w = turn[0] % 2
-        turn[0] += 1
-        G, key = (T.GE, "GE%d" % c) if e else (T.GO, "GO%d" % c)
-        q, qk = (T.QG[:, 64 * c:64 * c + 64], "QG") if e else (T.XW[:, 1024 * c + b:1024 * c + 1024:16], "X1")
-        W, AB = T["W%d" % w], T["AB%d" % w]
-        for k in range(16):
-            o, wk = W[:, 64 * k:64 * k + 64], "#W%d_%d" % (w, k // 8)
-            mm(o, T.IDM[:], G[:, 1024 * c + k:1024 * c + 1024:16], True, False, "IDM " + key, wk)
-            mm(o, T.NID[:], q, False, True, "NID " + qk, wk)
-            if halves and k % 8 == 7:
-                h = k // 8
-                op("s", "act", (AB[:, 512 * h:512 * h + 512], W[:, 512 * h:512 * h + 512], F.Abs), wk, "AB%d_%d" % (w, h))
-        if not halves:
-            op("s", "act", (AB[:], W[:], F.Abs), "#W%d_0 #W%d_1" % (w, w), "AB%d_0 AB%d_1" % (w, w))
-        pending.append((e, c, w, b))
-        while len(pending) > 1:
-            sums(pending.pop(0))
-
-    def flush():
-        while pending:
-            sums(pending.pop(0))
-
-    def own_unit(b, hooks):
-        for c in range(CH + 1):
-            for at, f in hooks:
-                if at == c:
-                    f()
-            if c < CH:
-                gather(False, c, "v" if c in O_ON_V else "s", b)
-            if c:
-                diff(False, c - 1, b)
-
-    def own_table(b):
-        op("s", "act", (T.KOT[:, b::16], T.KO[:, 0:256], F.Copy), "#KO", "KOT")
-
-    def wrap(o, Z, src, zk, sk):
+    def wrap(o, Z, src, zk, sk, bank="#M2"):
         for il in range(16):
-            mm(o, Z[:, 16 - il:144 - il], src(il), il == 0, il == 15, zk + " " + sk, "#M2")
+            mm(o, Z[:, 16 - il:144 - il], src(il), il == 0, il == 15, zk + " " + sk, bank)
+
+    def own_lists(c0, c1):
+        for c in range(c0, c1):
+            wrap(T.KE[:, 16 * c:16 * c + 16], T.ZW, lambda il, c=c: T.XW[:, 16 * il + c:4096:256], "ZW", "X1", "#KE")
+        for c in range(c0, c1):
+            wrap(T.KE[:, 128 + 16 * c:144 + 16 * c], T.ZR, lambda il, c=c: T.SV[:, 16 * il + c:4096:256], "ZR", SVall, "#KE")
+        a, b, key = 16 * c0, 16 * c1, " ".join("PLO%d" % c for c in range(c0, c1))
+        cp(T.OA[:, a:b], T.KE[:, a:b], "#KE", "OA", b - a)
+        ts(T.OU[:, a:b], T.OA[:, a:b], 4095, None, A.bitwise_and, None, "OA", "OU", b - a)
+        tt(T.OA[:, a:b], T.KE[:, 128 + a:128 + b], T.OU[:, a:b], A.mult, "#KE OU", "OA", b - a)
+        ts(T.OB[:, a:b], T.OA[:, a:b], 5, 4095, A.arith_shift_right, A.bitwise_and, "OA", "OB", b - a)
+        tt(T.OA[:, a:b], T.KE[:, 128 + a:128 + b], T.OB[:, a:b], A.add, "#KE OB", "OA", b - a)
+        ts(T.OB[:, a:b], T.OA[:, a:b], 4095, None, A.bitwise_and, None, "OA", "OB", b - a)
+        cp(T.PLO[:, c0:c1, 0:16], T.OB[:, a:b], "OB", key, b - a)
+        for n in (1, 2, 4, 8):
+            ts(T.PLO[:, c0:c1, 16 * n:32 * n], T.PLO[:, c0:c1, 0:16 * n], float(613 * n % 4096), None, A.add, None, key, key, n * (b - a) // 2)
+
+    def wb(b, n=1):
+        if b == 4:
+            return T.M2[:], "#M2"
+        return T["W%d" % (b // 2)][:, 512 * (b % 2):512 * (b % 2 + n)], " ".join("#W%d" % (b + j) for j in range(n))
+
+    def abk(b, n=1):
+        return " ".join("AB%d" % (b + j) for j in range(n))
+
+    mate = helper(core, T, topo)
+    mrid, mpid = topo.addr(mate)[:2]
+    off_chip = set(e for other in T.cores if other != core for e in topo.engines(core, other))
+    free = [e for e in topo.engines(core, mate) if e not in off_chip]
+
+    def gk(c, k):
+        return "G%d_%d" % (c % NB, k // 2)
+
+    def total(c, k, Z, src, sk, first=False):
+        o, bk = ((T.KO, "#KO"), (T.W2, "#W4"))[c % 2]
+        mm(o[:, 0:256], T[Z][:, 16 - k:144 - k], src, first, False, Z + " " + sk, bk, 256)
+
+    def own_gather(c, pieces):
+        G, k0 = T["GO%d" % (c % NB)], 0
+        for n, q in pieces:
+            src = T.XW[:, 0:XA].indirect(T.PLO[:, c, 16 * k0:16 * (k0 + n)])
+            out, rd, wr = G[:, 256 * k0:256 * (k0 + n)], Xown + " PLO%d" % c, " ".join(gk(c, k) for k in range(k0, k0 + n, 2))
+            if q == "v":
+                cp(out, src, rd, wr, GA * 256 * n)
+            else:
+                act(out, src, F.Copy, rd, wr, GA * 256 * n)
+            k0 += n
+
+    def own_fold(c):
+        if c < DIRECT:
+            return
+        G = T["GO%d" % (c % NB)]
+        o, bk = ((T.KO, "#KO"), (T.W2, "#W4"))[c % 2]
+        mm(o[:, 0:256], T.BM[:], T.XW[:, c:4096:16], True, False, "BM X1", bk, 256)
+        for k in range(16):
+            total(c, k, "ZM", G[:, 256 * k:256 * k + 256], gk(c, k))
+        Q = T["Q4%d" % (c % 2)]
+        for h in range(2):
+            select(Q[:, 512 * h:512 * h + 512], T.XW[:, c:8192:16], [[0, 512]], 0, "X1 X2", "Q%d_%d" % (c % 2, h), 512)
+        per = 4 // FOLDS
+        ne = len(free) // per
+        for f in range(FOLDS):
+            trs = []
+            for j in range(per):
+                b = 1024 * (f * per + j)
+                name, c0 = PARK[c]
+                trs.append(RemoteDMATransfer(
+                    dst_ids=[DstId(rid=mrid, pnc=mpid)], dma_engine_mask=sum(1 << e for e in free[ne * j:ne * j + ne]),
+                    remote_sem=T.sem["hf%d_%d" % (c, f)], srcs=[G[:, b:b + 1024], Q[:]], dsts=[T[name][:, c0 + b:c0 + b + 1024]], alu_op=2))
+            wr = [gk(c, k) for k in range(4 * per * f, 4 * per * (f + 1), 2)]
+            remote(lambda trs=trs: g.remote_dma_fused(trs, local_sem=T.sem.sent), ["Q%d_0" % (c % 2), "Q%d_1" % (c % 2)], wr, "mx%d_%d" % (c, f),
+                   len(topo.engines(mate, core)), FLAT / (1 + 0.3 * (FOLDS - 1)), len(free))
+
+    def own_close(c):
+        G = T["GO%d" % (c % NB)]
+        o, bk = ((T.KO, "#KO"), (T.W2, "#W4"))[c % 2]
+        if c < DIRECT:
+            for j in range(4):
+                b = 2 * (j % 2)
+                for h in range(2):
+                    w, wk = wb(b + h)
+                    mm(w, T.IDM[:], T.XW[:, c:8192:16], True, False, "IDM X1 X2", wk, 512)
+                    mm(w, T.NID[:], G[:, 1024 * j + 512 * h:1024 * j + 512 * h + 512], False, True, "NID " + gk(c, 4 * j + 2 * h), wk, 512)
+                w, wk = wb(b, 2)
+                act(T.AB[:, 512 * b:512 * b + 1024], w, F.Abs, wk, abk(b, 2), 1024)
+                for k in range(4):
+                    total(c, 4 * j + k, "Z8", T.AB[:, 512 * b + 256 * k:512 * b + 256 * k + 256], abk(b + k // 2), j + k == 0)
+        else:
+            for k in range(16):
+                total(c, k, "Z16", G[:, 256 * k:256 * k + 256], gk(c, k))
+        mm(o[:, 0:256], T.SVK[:], T.SV[:, c::16], False, True, "SVK " + SVall, bk, 256)
+        act(T.KOT[:, c::16], o[:, 0:256], F.Copy, bk, "KOT", 256)
 
     CNT, AAW, AVW, TRI_, TOT, FITS = (T.M2[:, 256 + 16 * j:272 + 16 * j] for j in range(6))
 
-    def smalls():
-        op("s", "act", (T.QG[:], T.XW[:, 0:4096].indirect(T.V16[:]), F.Copy), "X1 V16", "QG")
-        op("s", "act", (T.AWG[:], T.AW[:, 0:4096].indirect(T.A16[:]), F.Copy), "AW AWr A16", "AWG")
-        op("s", "act", (T.SVG[:], T.SV[:].indirect(T.V16[:]), F.Copy), SVall + " V16", "SVG")
+    def at_v():
+        act(T.QG[:], T.XW[:, 0:4096].indirect(T.V16[:]), F.Copy, "X1 V16", "QG", GA * 256)
+        mm(T.KE[:, 0:256], T.WM[:], T.QG[:], True, True, "WM QG", "#KE", 256)
+        for h in range(2):
+            mm(T.KE[:, 256 + 128 * h:384 + 128 * h], T.QG[:, 128 * h:128 * h + 128], T.IDM[:], True, True, "QG IDM", "#KE", 128)
+        cp(T.UC[:], T.KE[:, 0:256], "#KE", "UC", 256)
+        act(T.QT[:], T.KE[:, 256:512], F.Copy, "#KE", "QT", 256)
+        ts(T.UG[:], T.UC[:], 4095, None, A.bitwise_and, None, "UC", "UG", 256)
 
-    def wraps():
-        wrap(AVW, T.ZB, lambda il: T.SVG[:, il::16], "ZB", "SVG")
-        wrap(AAW, T.ZA, lambda il: T.AWG[:, il::16], "ZA", "AWG")
-        op("s", "act", (T.AAS[:], AAW, F.Copy), "#M2", "AAS")
+    def at_a():
+        act(T.AG[:], T.AW[:, 0:4096].indirect(T.AV[:]), F.Copy, AWall + " A16 V1", "AG", GA * 512)
+        wrap(T.M2[:, 272:304], T.ZA, lambda il: T.AG[:, il::16], "ZA", "AG")
+        act(T.AAS[:], T.M2[:, 272:304], F.Copy, "#M2", "AAS")
+        tt(T.DA[:], T.AAS[:, 16:32], T.AAS[:, 0:16], A.subtract, "AAS", "DA")
 
-    def fits():
-        op("s", "act", (T.JK[:], FITS, F.Copy), "#M2", "JK c_bs", accum_out=col("bs"))
+    def keys(i0, i1):
+        return (T.KE[:, i0:i1], "#KE") if i0 < CUT else (T.M2[:, 352 + i0 - CUT:352 + i1 - CUT], "#M2")
 
-    def place_e():
-        tt(T.TA[:], T.RW[:, 0:4096].indirect(T.A16[:]), T.UG[:], A.mult, "RW A16 UG", "TA")
-        op("s", "act", (T.EG[:], T.RW[:, 0:4096].indirect(T.A16[:]), F.Copy), "RW A16", "EG")
-        ts(T.TB[:], T.TA[:], 5, 4095, A.arith_shift_right, A.bitwise_and, "TA", "TB")
-        tt(T.TC[:], T.RW[:, 0:4096].indirect(T.A16[:]), T.TB[:], A.add, "RW A16 TB", "TC")
-        ts(T.PLE[:], T.TC[:], col("kc"), None, A.add, None, "TC c_kc", "PLE")
+    def strict_pass():
+        for j in range(len(PLACES) - 1):
+            i0, i1 = PLACES[j], PLACES[j + 1]
+            R, n = T.RW[:, 0:4096].indirect(T.AV[:, i0 // 16:i1 // 16]), i1 - i0
+            act(T.EK[:, i0:i1], R, F.Identity, "RW A16 c_kc", "EK%d" % j, GA * n, bias=col("kc"))
+            tt(T.TA[:, i0:i1], R, T.UG[:, i0:i1], A.mult, "RW A16 UG", "TA%d" % j, GA * n)
+            ts(T.TB[:, i0:i1], T.TA[:, i0:i1], 5, 4095, A.arith_shift_right, A.bitwise_and, "TA%d" % j, "TB%d" % j, n)
+            tt(T.PLE[:, i0:i1], T.EK[:, i0:i1], T.TB[:, i0:i1], A.add, "EK%d TB%d" % (j, j), "PLE%d" % j, 2 * n)
+        ek = " ".join("EK%d" % j for j in range(len(PLACES) - 1))
+        mm(T.M2[:, 0:256], T.EQM[:], T.EK[:], True, True, "EQM " + ek, "#M2", 1024)
+        if NEQ_ON == "s":
+            act(T.NEQ[:], T.M2[:, 0:256], F.Abs, "#M2 c_kq", "NEQ", 256, scale=33554432.0, bias=col("kq"))
+        else:
+            ts(T.NEQ[:], T.M2[:, 0:256], col("kc"), 33554432.0, A.not_equal, A.mult, "#M2 c_kc", "NEQ", 256)
+        tt(T.DM[:], T.KOT[:].indirect(T.V16[:]), T.NEQ[:], A.add, "KOT V16 NEQ", "DM", GA * 256)
 
-    def merge(t):
-        cp(T.RW[:, 8 + t:4096:64], T.LAND[:, 64 * t:64 * t + 64], "LAND%d" % t, "RW")
+        way = {u: q for u0, n, q in SIZES for u in range(u0, u0 + n)}
+
+        def add(i0, i1, lhs, rhs, rd, slow=1):
+            o, bk = keys(i0, i1)
+            mm(o, lhs, rhs, False, False, rd + " " + bk, " ".join("K%d" % u for u in range(i0 // 32, i1 // 32)), slow * max(64, i1 - i0))
+
+        def low(i0, i1):
+            add(i0, i1, T.SVE[:], T.AG[:, 256 + i0:256 + i1], "SVE AG")
+            add(i0, i1, T.DKH[:], T.ALL1[:, i0:i1], "DKH ALL1")
+            add(i0, i1, T.DKL[:], T.ALL1[:, i0:i1], "DKL ALL1")
+            add(i0, i1, T.DNM[:], T.EK[:, i0:i1], "DNM " + ek, 4)
+
+        for i0, i1 in ((0, CUT), (CUT, 256)):
+            if i1 > i0:
+                o, bk = keys(i0, i1)
+                mm(o, T.DNG[:], T.ALL1[:, i0:i1], True, False, "DNG ALL1", bk, max(64, i1 - i0))
+                j1 = min([i1] + [32 * u0 for u0, n, q in SIZES if q == "v" and 32 * u0 >= i0])
+                if j1 > i0:
+                    low(i0, j1)
+        for u0, n, q in GATH:
+            src = T.XW[:].indirect(T.PLE[:, 32 * u0:32 * (u0 + n)])
+            rd = Xall + "".join(" PLE%d" % j for j in range(len(PLACES) - 1) if PLACES[j] < 32 * (u0 + n) and PLACES[j + 1] > 32 * u0)
+            key = " ".join("GE%d" % u for u in range(u0, u0 + n))
+            if q == "v":
+                cp(T.GE[:, 512 * u0:512 * (u0 + n)], src, rd, key, GA * 512 * n)
+            else:
+                act(T.GE[:, 512 * u0:512 * (u0 + n)], src, F.Copy, rd, key, GA * 512 * n)
+        for u0, n, q in SIZES:
+            b, i0, i1 = BANK[u0], 32 * u0, 32 * (u0 + n)
+            ge, ab = (" ".join("%s%d" % (x, u) for u in range(u0, u0 + n)) for x in ("GE", "AB"))
+            for u in range(u0, u0 + n):
+                w, wk = wb(BANK[u])
+                mm(w, T.QT[:, 128 * (u // 4):128 * (u // 4) + 128], T.SEL[:, 512 * (u % 4):512 * (u % 4) + 512], True, q == "v", "QT SEL", wk, 512)
+                if q == "s":
+                    mm(w, T.NID[:], T.GE[:, 512 * u:512 * u + 512], False, True, "NID GE%d" % u, wk, 512)
+            w, wk = wb(b, n)
+            if q == "s":
+                act(T.AB[:, 512 * u0:512 * (u0 + n)], w, F.Abs, wk, ab, 512 * n)
+            else:
+                tt(T.AB[:, 512 * u0:512 * (u0 + n)], T.GE[:, 512 * u0:512 * (u0 + n)], w, A.max, wk + " " + ge, ab, 512 * n)
+        for u0, n in SUMS:
+            i0, i1, q = 32 * u0, 32 * (u0 + n), way[u0]
+            ge, ab = (" ".join("%s%d" % (x, u) for u in range(u0, u0 + n)) for x in ("GE", "AB"))
+            if q == "v":
+                add(i0, i1, T.BM[:], T.QG[:, i0:i1], "BM QG")
+                for k in range(16):
+                    add(i0, i1, T.ZM[:, 16 - k:144 - k], T.GE[:, 512 * u0 + k:512 * (u0 + n):16], "ZM " + ge)
+            for k in range(16):
+                add(i0, i1, (T.Z8 if q == "s" else T.Z16)[:, 16 - k:144 - k], T.AB[:, 512 * u0 + k:512 * (u0 + n):16], "Z8 Z16 " + ab)
+            if q == "v":
+                low(i0, i1)
+        for i0, i1 in ((0, CUT), (CUT, 256)):
+            if i1 > i0:
+                o, bk = keys(i0, i0 + 16)
+                mm(o, T.IDM[:], T.ZB[:], False, True, "IDM ZB", bk)
 
     def keep_yh(t):
-        op("s", "act", (T.YH[:, t::8], T.LAND[:, 64 * t:64 * t + 64], F.Copy), "LAND%d" % t, "YH")
+        if t == NST - 1:
+            act(T.YH[:, t::8], T.LAND[:, 64 * t:64 * t + 64], F.Copy, "LAND%d" % t, "YH", 64)
+        else:
+            select(T.YH[:, t::8], T.LAND[:, 64 * t:64 * t + 64], [[0, 64]], 0, "LAND%d" % t, "YH", 64)
 
-    def gathers_e():
-        for c in E_ON_S:
-            gather(True, c, "s")
-        for c in range(CH):
-            if c not in E_ON_S:
-                gather(True, c, "v")
-
-    prep_u(0)
-    prep_v(0)
-    ts(T.ZA[:], T.CI[:], col("pg16"), col("kr"), A.is_equal, A.mult, "CI c_pg16 c_kr", "ZA")
-    ts(T.VF0[:], T.VI[:], col("pgx"), None, A.subtract, None, "VI c_pgx", "VF0")
-    wrap(AAW, T.ZA, lambda il: T.AW[:, 16 * il:4096:256], "ZA", "AW AWr")
-    op("s", "act", (T.XW[:, 4096:8192], T.XW[:, 0:4096], F.Copy), "X1", "X2")
-    cp(T.V16[:], T.VF0[:], "VF0", "V16")
-    cp(T.UG[:], T.UT[:, 0:4096].indirect(T.V16[:]), "UT V16", "UG")
-    cp(T.A16[:], AAW, "#M2", "A16")
-    for h in range(2):
-        cp(T.RW[:, 2048 * h:2048 * h + 2048], T.RI[:, 2048 * h:2048 * h + 2048], "RI%d" % h, "RW")
-    own_unit(0, [(3, smalls), (4, place_e), (4, gathers_e)])
-    ts(T.T0[:], T.MG[:], col("pg"), col("k4"), A.is_equal, A.mult, "MG c_pg c_k4", "T0")
-    ts(T.T1[:], T.CI[:, 0:128], col("pg"), col("kr"), A.is_equal, A.mult, "CI c_pg c_kr", "T1")
-    tt(T.SVE[:], T.T0[:], T.T1[:], A.add, "T0 T1", "SVE")
-    ts(T.DNM[:], T.CI[:, 0:128], col("p"), col("nk"), A.is_equal, A.mult, "CI c_p c_nk", "DNM")
-    ts(T.T0[:], T.MG[:], col("p"), None, A.is_equal, None, "MG c_p", "T0")
-    tt(T.EQM[:], T.IDM[:], T.T0[:], A.subtract, "IDM T0", "EQM")
-    ts(T.ZB[:], T.CI[:], col("pg16"), col("kb"), A.is_equal, A.mult, "CI c_pg16 c_kb", "ZB")
-    prep_u(1)
-    prep_v(1)
-    op("v", "set", (T.ALL1[:], 1.0), wr="ALL1")
-    op("v", "set", (T.ZERO[:], 0.0), wr="ZERO")
-    op("v", "set", (T.SC[:], 0.0), wr="SC")
-    ts(T.Z1[:], T.CI[:], col("pg16"), None, A.is_equal, None, "CI c_pg16", "Z1")
-    ts(T.T1[:], T.CI[:, 0:128], col("p"), None, A.is_gt, None, "CI c_p", "T1")
-    tt(T.TRI[:], T.T1[:], T.BLK[:], A.mult, "T1 BLK", "TRI")
-    ts(T.KD[:], T.KI[:], col("pg"), 1.0 / 4096, A.subtract, A.mult, "KI c_pg", "KD")
-    for t in range(NST):
-        op("s", "act", (T.PRES[:, 64 * t:64 * t + 64], T.RW[:, 8 + t:4096:64], F.Copy), "RW", "PRES%d" % t)
-    before("g", "pre", ["PRES%d" % t for t in range(NST)], [])
+    if X2_BY == "v":
+        cp(T.XW[:, 4096:8192], T.XW[:, 0:4096], "X1", "X2", 2048)
+        cp(T.XW[:, 8192:XA], T.XW[:, 0:XA - 8192], "X1", "X3a", 512)
+    else:
+        dma(T.XW[:, 4096:8192], T.xc[:], 1 << 20, wr="X2")
+        dma(T.XW[:, 8192:XA], T.xc[:, 0:XA - 8192], 1 << 18, wr="X3a")
+    dma(T.XW[:, XA:12288], T.xc[:, XA - 8192:4096], 3 << 18, wr="X3b")
+    own_lists(0, 1)
+    wrap(AAW, T.ZA, lambda il: T.AW[:, 16 * il:4096:256], "ZA", AWall)
+    cp(A16, AAW, "#M2", "A16")
+    at_v()
+    at_a()
+    own_lists(1, NST)
+    for h in range(4):
+        cp(T.RW[:, 1024 * h:1024 * h + 1024], T.RI[:, 1024 * h:1024 * h + 1024], "RI%d" % h, "RW", 1024)
     trs = []
     for t in range(NST):
+        select(T.PRES[:, 64 * t:64 * t + 64], T.RW[:, 8 + t:4096:64], [[0, 64]], 0, "RW", "PRES%d" % t, 64)
         src = T.cores[(rank - 1 - t % (n_ranks - 1)) % n_ranks]
         rid, pid = topo.addr(src)[:2]
         e = topo.engines(core, src)
         trs.append(RemoteDMATransfer(dst_ids=[DstId(rid=rid, pnc=pid)], dma_engine_mask=1 << e[t % len(e)], remote_sem=T.sem.pre,
                                      src=T.PRES[:, 64 * t:64 * t + 64], dst=T.CB[:, CBW * t:CBW * t + 64]))
-    g.remote_dma_fused(trs, local_sem=T.sem.sent)
-    sent = NST
-    after(("pre", NST, {}), [], ["CB%d" % t for t in range(NST)])
-    count["pre"] = NST
+    remote(lambda: g.remote_dma_fused(trs, local_sem=T.sem.sent), ["PRES%d" % t for t in range(NST)],
+           ["CB%d" % t for t in range(NST)], "pre", NST, 8.0, NST, False)
+    for c in range(NB):
+        own_gather(c, OWN0 if c < 2 else OWN)
+    own_fold(0)
+    own_fold(1)
+    own_close(0)
 
     for t in range(NST):
-        lastep = t == NST - 1
-        vf, vn = T["VF%d" % (t % 2)], T["VF%d" % ((t + 1) % 2)]
-        vfk, vnk = "VF%d" % (t % 2), "VF%d" % ((t + 1) % 2)
-        if t > 0 and t + 1 < NST:
-            prep_u(t + 1)
-            prep_v(t + 1)
-        if t > 0:
-            cp(T.BI[:], col("bs"), "c_bs", "BI")
-            ts(T.BI2[:], T.BI[:], 255, None, A.bitwise_and, None, "BI", "BI2")
-            ts(col("thb"), T.BI2[:], 8192.0, col("th"), A.mult, A.add, "BI2 c_th", "c_thb")
-        order = [c for c in E_ON_S] + [c for c in range(CH) if c not in E_ON_S]
-        for c in order:
-            diff(True, c, 0, c == order[-1])
-            if c == order[0]:
-                own_table(t)
-                op("s", "act", (T.IOG[:], T.IOT[:].indirect(T.A16[:]), F.Copy), "IOT A16", "IOG")
-            if c == order[EQ_AFTER]:
-                if t == 0:
-                    wraps()
-                mm(T.M2[:, 0:256], T.EQM[:], T.EG[:], True, True, "EQM EG", "#M2")
-                op("s", "act", (T.NEQ[:], T.M2[:, 0:256], F.Abs), "#M2", "NEQ", scale=33554432.0)
-        flush()
-        tt(T.DM[:], T.KOT[:].indirect(T.V16[:]), T.NEQ[:], A.add, "KOT V16 NEQ", "DM")
-        tt(T.DA[:], AVW, T.AAS[:], A.subtract, "#M2 AAS", "DA")
-        tt(T.MN[:], T.KE[:, 0:256], T.DM[:], A.min, "#KE DM", "MN")
-        ts(T.IND[:], T.MN[:], col("th" if t == 0 else "thb"), None, A.is_lt, None, "MN " + ("c_th" if t == 0 else "c_thb"), "IND")
-        ts(T.FV[:], T.MN[:], 4095, None, A.bitwise_and, None, "MN", "FV")
-        wrap(CNT, T.Z1, lambda il: T.IND[:, il::16], "Z1", "IND")
+        more = t < NST - 1
+        strict_pass()
+        act(T.IOG[:], T.SV[:].indirect(A16), F.Copy, SVall + " A16", "IOG", GA * 256)
+        th = "th" if t == 0 else "thb"
+        for j, (i0, i1) in enumerate(((0, CUT), (CUT, 256))):
+            if i1 > i0:
+                o, bk = keys(i0, i1)
+                tt(T.MN[:, i0:i1], o, T.DM[:, i0:i1], A.min, bk + " DM", "MN%d" % j, i1 - i0)
+                ts(T.IND[:, i0:i1], T.MN[:, i0:i1], col(th), None, A.is_lt, None, "MN%d c_%s" % (j, th), "IND%d" % j, i1 - i0)
+        ts(T.FV[:], T.MN[:], 4095, None, A.bitwise_and, None, "MN0 MN1", "FV", 256)
+        wrap(CNT, T.Z1, lambda il: T.IND[:, il::16], "Z1", "IND0 IND1")
         ts(T.FW[:], CNT, 7.5, None, A.is_gt, None, "#M2", "FW")
         ts(T.NF[:], CNT, 7.5, 4096.0, A.is_lt, A.mult, "#M2", "NF")
         mm(TOT, T.BLK[:], T.FW[:], True, True, "BLK FW", "#M2")
         mm(TRI_, T.TRI[:], T.FW[:], True, True, "TRI FW", "#M2")
-        if not lastep:
-            mm(FITS, T.ALL1[:], T.FW[:], True, True, "ALL1 FW", "#M2")
+        if more:
+            mm(FITS, T.ALL1[:, 0:128], T.FW[:], True, True, "ALL1 FW", "#M2")
         tt(T.GD[:], T.NF[:], T.KD[:], A.mult, "NF KD", "GD")
-        op("v", "scan", (T.SC[:, 1:17], TOT, T.ZERO[:], 0.0, A.add, A.add), "#M2 ZERO SC", "SC")
+        op("v", lambda: g.vector.tensor_tensor_scan(T.SC[:, 1:17], TOT, T.ZERO[:], 0.0, A.add, A.add), "#M2 ZERO SC", "SC", FIX + 16 * CYC)
         tt(T.P1[:], TRI_, T.GD[:], A.add, "#M2 GD", "P1")
-        tt(T.DD[:], vf[:], T.NF[:], A.add, vfk + " NF", "DD")
-        tt(T.P2[:], T.P1[:], T.SC[:, 0:16], A.add, "P1 SC", "P2")
-        tt(T.MA[:], T.FW[:], T.DA[:], A.mult, "FW DA", "MA")
-        cp(T.C16[:], T.P2[:], "P2", "C16")
-        cp(T.D16[:], T.DD[:], "DD", "D16")
-        cp(T.CB[:, CBW * t:CBW * t + CBW].indirect(T.C16[:]), T.FV[:], "C16 FV CB%d" % t, "CB%d" % t)
+        tt(T.C16[:], T.P1[:], T.SC[:, 0:16], A.add, "P1 SC", "C16")
+        cp(T.CB[:, CBW * t:CBW * t + CBW].indirect(T.C16[:]), T.FV[:], "C16 FV CB%d" % t, "CB%d" % t, SC_ * 256)
         dst = T.cores[(rank + 1 + t % (n_ranks - 1)) % n_ranks]
         rid, pid = topo.addr(dst)[:2]
-        ne = len(topo.engines(core, dst))
-        before("g", "x", ["CB%d" % t], [])
-        g.remote_dma(T.LAND[:, 64 * t:64 * t + 64], T.CB[:, CBW * t:CBW * t + 64], T.sem["arr%d" % t], T.sem.sent, pid, rid, topo.mask(core, dst))
-        sent += ne
-        after(("arr%d" % t, ne, {}), [], ["LAND%d" % t])
-        count["arr%d" % t] = ne
-        if lastep:
-            cp(T.RW[:].indirect(T.D16[:]), T.FV[:], "D16 FV", "RW")
-        tt(T.AN[:], T.MA[:], T.AAS[:], A.add, "MA AAS", "AN")
-        tt(vn[:], vf[:], T.FW[:], A.add, vfk + " FW", vnk)
-        cp(T.AW[:].indirect(T.D16[:]), T.IOG[:], "D16 IOG", "AW AWr")
-        cp(T.A16[:], T.AN[:], "AN", "A16")
-        cp(T.V16[:], vn[:], vnk, "V16")
-        if not lastep:
-            cp(T.RW[:].indirect(T.D16[:]), T.FV[:], "D16 FV", "RW")
-            cp(T.UG[:], T.UT[:, 0:4096].indirect(T.V16[:]), "UT V16", "UG")
-            own_unit(t + 1, [(2, fits), (HOOK, smalls), (WHOOK, wraps), (EHOOK, lambda: merge(t)), (EHOOK, place_e), (EHOOK, gathers_e), (4, lambda: keep_yh(t))])
+        remote(lambda t=t, pid=pid, rid=rid, dst=dst: g.remote_dma(
+            T.LAND[:, 64 * t:64 * t + 64], T.CB[:, CBW * t:CBW * t + 64], T.sem["arr%d" % t], T.sem.sent, pid, rid, topo.mask(core, dst)),
+            ["CB%d" % t], ["LAND%d" % t], "arr%d" % t, len(topo.engines(core, dst)), RLAT - 0.6, len(topo.engines(core, dst)), False)
+        tt(T.D16[:], T.V16[:], T.NF[:], A.add, "V16 NF", "D16")
+        tt(T.V16[:], T.V16[:], T.FW[:], A.add, "V16 FW", "V16")
+        tt(T.MA[:], T.FW[:], T.DA[:], A.mult, "FW DA", "MA")
+        tt(A16, T.MA[:], T.AAS[:, 0:16], A.add, "MA AAS", "A16")
+        cp(T.RW[:].indirect(T.D16[:]), T.FV[:], "D16 FV", "RW", SC_ * 256)
+        cp(T.AW[:].indirect(T.D16[:]), T.IOG[:], "D16 IOG", AWall, SC_ * 256)
+        if more:
+            tt(V1, V1, T.FW[:], A.add, "V1 FW", "V1")
+            act(T.JK[:], FITS, F.Copy, "#M2", "JK c_bs", accum_out=col("bs"))
+            cp(T.BI[:], col("bs"), "c_bs", "BI")
+            ts(T.BI2[:], T.BI[:], 255, None, A.bitwise_and, None, "BI", "BI2")
+            ts(col("thb"), T.BI2[:], 8192.0, col("th"), A.mult, A.add, "BI2 c_th", "c_thb")
+            at_v()
+            at_a()
+            if t + NB < NST:
+                own_gather(t + NB, OWN)
+            if t + 2 < NST:
+                own_fold(t + 2)
+            own_close(t + 1)
+            cp(T.RW[:, 8 + t:4096:64], T.LAND[:, 64 * t:64 * t + 64], "LAND%d" % t, "RW", 64)
+        keep_yh(t)
 
+    dma(T.yh[:], T.YH[:], 1 << 18, rd="YH")
     for s in range(4):
-        w, h = s // 2, s % 2
-        o, wk = T["W%d" % w][:, 512 * h:512 * h + 256], "#W%d_%d" % (w, h)
-        op("s", "act", (o, T.RW[:, 4 + s:4096:16], F.Copy), "RW", wk, scale=4096.0)
-        tt(T.KOT[:, s:1024:4], o, T.RW[:, s:4096:16], A.add, "RW " + wk, "YR%d" % s)
-    dma("y", T.yr[:], T.KOT[:, 0:1024], rd="YR0 YR1 YR2 YR3")
-    op("s", "act", (T.IOG[:], T.IOT[:].indirect(T.A16[:]), F.Copy), "IOT A16", "IOG")
-    cp(T.SVG[:], T.IOT[:].indirect(T.V16[:]), "IOT V16", "SVG")
-    keep_yh(NST - 1)
-    dma("y", T.yh[:], T.YH[:], rd="YH")
+        o, wk = T["W%d" % (s // 2)][:, 512 * (s % 2):512 * (s % 2) + 256], "#W%d" % s
+        act(o, T.RW[:, 4 + s:4096:16], F.Copy, "RW", wk, 256, scale=4096.0)
+        tt(T.KOT[:, s:1024:4], o, T.RW[:, s:4096:16], A.add, "RW KOT " + wk, "YR%d" % s, 256)
+    dma(T.yr[:], T.KOT[:, 0:1024], 1 << 19, rd="YR0 YR1 YR2 YR3")
+    act(T.IOG[:], T.SV[:].indirect(A16), F.Copy, SVall + " A16", "IOG", GA * 256)
+    cp(T.AG[:, 0:256], T.SV[:].indirect(T.V16[:]), SVall + " V16", "AG", GA * 256)
+    mm(T.KO[:, 0:256], T.SVA[:], T.AG[:, 0:256], True, True, "SVA AG", "#KO", 256)
+    mm(T.KO[:, 256:512], T.SVA[:], T.IOG[:], True, True, "SVA IOG", "#KO", 256)
+    act(T.YVA[:], T.KO[:], F.Copy, "#KO", "YVA", 512)
     for s in range(8):
-        w, h = s // 2 % 2, s % 2
-        o, wk = T["W%d" % w][:, 512 * h:512 * h + 256], "#W%d_%d" % (w, h)
-        mm(o, T.SVR[:], T.AW[:, s:4096:16], True, True, "SVR AW AWr", wk)
-        if h:
-            op("s", "act", (T.KOT[:, 2048 + s::8], o, F.Copy), wk, "YAN%d" % s)
+        o, wk = T["W%d" % (s // 2 % 2)][:, 512 * (s % 2):512 * (s % 2) + 256], "#W%d" % (s % 4)
+        mm(o, T.SVA[:], T.AW[:, s:4096:16], True, True, "SVA " + AWall, wk, 256)
+        if s % 2:
+            act(T.KOT[:, 2048 + s::8], o, F.Copy, wk, "YAN%d" % s, 256)
         else:
-            cp(T.KOT[:, 2048 + s::8], o, wk, "YAN%d" % s)
-    mm(T.KO[:, 0:256], T.SVR[:], T.SVG[:], True, True, "SVR SVG", "#KO")
-    mm(T.KO[:, 256:512], T.SVR[:], T.IOG[:], True, True, "SVR IOG", "#KO")
-    op("s", "act", (T.YVA[:], T.KO[:], F.Copy), "#KO", "YVA")
-    dma("y", T.yan[:], T.KOT[0::16, 2048:4096], rd=" ".join("YAN%d" % s for s in range(8)))
-    dma("y", T.yv[:], T.YVA[0::16, 0:256], rd="YVA")
-    dma("y", T.ya[:], T.YVA[0::16, 256:512], rd="YVA")
-    count["sent"] = sent
+            cp(T.KOT[:, 2048 + s::8], o, wk, "YAN%d" % s, 256)
+    dma(T.yan[:], T.KOT[0::16, 2048:4096], 1 << 16, rd=" ".join("YAN%d" % s for s in range(8)))
+    dma(T.yv[:], T.YVA[0::16, 0:256], 1 << 13, rd="YVA")
+    dma(T.ya[:], T.YVA[0::16, 256:512], 1 << 13, rd="YVA")
+
+    for j in issue_order(tasks):
+        tasks[j][5]()
+    count["sent"] = sent[0]
     for s in count:
         if seen["g"].get(s, 0) < count[s]:
             g.wait_ge(T.sem[s], count[s])

@@ -1,75 +1,102 @@
 from concourse.bass import DstId, RemoteDMATransfer
-from concourse.mybir import AluOpType as A, AxisListType, ActivationFunctionType as F
+from concourse.mybir import AluOpType as A, ActivationFunctionType as F
 
 NST = 8
 NEG = -255.0 * 65536.0
-CBW = 320
+CBW = 448
 XA = 9216
-GATH = ((0, 2, "s"), (2, 2, "v"), (4, 2, "v"), (6, 1, "v"), (7, 1, "v"))
-SIZES = ((0, 2, "s"), (2, 2, "s"), (4, 2, "s"), (6, 2, "v"))
-BANK = (0, 1, 2, 3, 0, 1, 2, 3)
+HEAVY = (("s", 0, 2, None), ("v", 2, 2, None), ("v", 2, 2, 2), ("s", 6, 1, None), ("s", 0, 2, 0), ("v", 4, 2, None), ("s", 7, 1, None),
+         ("s", 6, 1, 2), ("v", 4, 2, 3), ("s", 7, 1, 5))
 SUMS = ((0, 2), (2, 2), (4, 2), (6, 2))
-CUT, NEQ_ON, ROUNDS, X2_BY = 128, "s", 3, "y"
-PLACES = (0, 128, 256)
-OWN = ((2, "s"),) * 8
-OWN0 = ((4, "s"), (4, "v"), (4, "s"), (4, "s"))
-NB = 3
-DIRECT, FOLDS, FLAT = 1, 2, 21.0
-PARK = (("XW", 0), ("XW", 4096), ("XW", 8192), ("AW", 0), ("AW", 4096), ("SV", 0), ("GE", 0), ("GO0", 0))
-CYC, FIX, PCY, HOP, GA, SC_, DFIX, DBW, RLAT = 0.83e-3, 0.065, 0.417e-3, 0.06, 1.56, 3.8, 1.8, 500e3, 3.6
+CUT, PLACES = 192, (0, 128, 256)
+OWN = ((2, "v", 4), (1, "v", 4), (1, "s", 4)) + ((2, "s", 4),) * 4 + ((2, "s", 3),) * 2
+OWN0 = ("svsv", "sssv", "ssvv")
+CLOSE = ((5, 2), (6, 2), (8, 2), (13, 1))
+DIRECT, FOLD0, AHEAD, NB = 1, 2, 3, 3
+FOLD, QW = ((0, 2, 1280), (2560, 1, 1536)), 1536
+LIST0 = 2
+X2_ON, RW_ON = "y", "gggg"
+ORDER = {
+    "v": "l0 o0_1 o0_3 o1_3 l1 uc0 m13 eqm m12 m10 m11 o2_3 o2_2 "
+         "MA BI A16 V1 AW UC RW UG p2 merge TA0 TA1 TB0 TB1 PL0 PL1 g2 BI2 a2 g4 thb a4 DM o0 y2 MN0 IND0 MN1 IND1 FV DA o1 "
+         "FW NF SC D16 GD P1 V16 C16 CB",
+    "s": "WI X1 TI X3a o0_0 o0_2 o1_0 o1_2 d00 d01 qt0 o1_1 d02 ag0 d03 iog0 o2_1 kot0 o2_0 "
+         "o7 QT AG o8 kot TA0 TA1 IOG AAS g0 NEQ g6 a0 g7 a6 a7 o2 o3 o4 o5 o6 QG y3 yh_ yan_",
+    "p": "l0 l1 d00 m1 d01 d02 e00 d03 e01 e02 e03 "
+         "u k3 kot ZA q0 q1 q2 q3 NEQ open0 q7 q5 n0 n1 x2 open1 q4 q6 n6 s2 s0 n7 x4 s4 stop0 s6 stop1 k0 FW k1 SC k2",
+    "g": "iota XL sel0 idm sel tri rw0 rw1 rw2 rw3 pres Q2 f21 f20 write Q3 fold0 fold1 yh Q",
+    "y": "AR0 AR1 AW0 AW1 X2 RI0 RI1 X3b AW8 AW9 AW2 AW3 yv_ ya_ yr_",
+    "e": "AR0 WI X1 AR1 TI AW0 AW1 X2 RI0 RI1 X3b AW8 AW9 AW2 AW3",
+}
+PARK = (("XW", 0), ("XW", 4096), ("XW", 8192), ("AW", 0), ("AW", 4096), ("AB", 0), ("GE", 0), ("GO0", 0))
+CYC, FIX, PCY, HOP, GA, SC_ = 0.83e-3, 0.065, 0.417e-3, 0.15, 1.56, 3.0
+DQ, DFIX, DROW, DBW = 0.5, 1.8, 0.2, 600e3
+RCALL, RLAT, PLAT, FLAT, ROUNDS = 0.6, 2.6, 10.0, (14.0, 12.0), 3
 
 SCRATCH = {}
 for _n, _s, _d in (
-        ("XW", 12288, "bfloat16"), ("RI", 4096, "int32"), ("RW", 8192, "float32"), ("AW", 8192, "bfloat16"),
-        ("SV", 4096, "bfloat16"), ("SEL", 2048, "bfloat16"),
-        ("KOT", 4096, "float32"), ("CB", NST * CBW, "float32"), ("LAND", NST * 64, "float32"), ("PRES", NST * 64, "float32"),
-        ("GE", 4096, "bfloat16"), ("GO0", 4096, "bfloat16"), ("GO1", 4096, "bfloat16"),
-        ("GO2", 4096, "bfloat16"), ("GO3", 4096, "bfloat16"), ("Q40", 1024, "bfloat16"), ("Q41", 1024, "bfloat16"), ("BM", 128, "bfloat16"),
-        ("AB", 4096, "bfloat16"), ("ZB", 16, "bfloat16"), ("AR", 768, "int32"), ("ARB", 1536, "bfloat16"),
+        ("XW", 12288, "bfloat16"), ("RI", 4096, "int32"), ("RW", 8192, "float32"), ("AW", 8192, "bfloat16"), ("SEL", 2048, "bfloat16"),
+        ("KOT", 4096, "float32"), ("CB", 3 * CBW, "float32"), ("LAND", NST * 64, "float32"), ("PRES", 576, "float32"),
+        ("GE", 4096, "bfloat16"), ("AB", 4096, "bfloat16"), ("GO0", 4096, "bfloat16"), ("GO1", 4096, "bfloat16"), ("GO2", 4096, "bfloat16"),
+        ("MX0", 4096, "bfloat16"), ("MX1", 4096, "bfloat16"), ("MX2", 4096, "bfloat16"),
+        ("QR0", 1536, "bfloat16"), ("QR1", 1536, "bfloat16"), ("QR2", 1536, "bfloat16"),
+        ("AR", 512, "int32"), ("ARB", 1536, "bfloat16"), ("ZB", 16, "bfloat16"),
         ("WI", 1, "int32"), ("TI", 1, "int32"), ("PI", 1, "int32"), ("PGI", 1, "int32"), ("PKI", 1, "int32"), ("PK2", 1, "int32"),
         ("KCI", 1, "int32"), ("KCM", 1, "int32"), ("KCH", 1, "bfloat16"), ("BI", 1, "int32"), ("BI2", 1, "int32"), ("COL", 32, "float32"),
-        ("CI", 144, "int32"), ("MG", 128, "int32"), ("DNG", 128, "bfloat16"), ("T2", 128, "float32"), ("T3", 128, "float32"),
-        ("IDM", 128, "bfloat16"), ("NID", 128, "bfloat16"), ("Z8", 144, "bfloat16"), ("Z16", 144, "bfloat16"), ("ZM", 144, "bfloat16"),
-        ("Z1", 144, "bfloat16"), ("ZA", 144, "bfloat16"), ("ZR", 144, "bfloat16"),
-        ("ZW", 144, "bfloat16"), ("EQM", 128, "float32"), ("DNM", 128, "float32"), ("DKH", 128, "bfloat16"), ("DKL", 128, "bfloat16"),
-        ("SVE", 128, "bfloat16"), ("SVA", 128, "bfloat16"), ("SVK", 128, "bfloat16"), ("TRI", 128, "bfloat16"),
-        ("BLK", 128, "bfloat16"), ("ALL1", 256, "bfloat16"), ("WM", 128, "bfloat16"),
-        ("VI", 16, "int32"), ("KI", 16, "int32"), ("KD", 16, "float32"), ("ZERO", 16, "float32"), ("SC", 32, "float32"),
+        ("CI", 144, "int32"), ("MG", 128, "int32"), ("T2", 128, "float32"), ("ALL1", 256, "bfloat16"),
+        ("Z1", 144, "bfloat16"), ("Z8", 144, "bfloat16"), ("Z16", 144, "bfloat16"), ("ZM", 144, "bfloat16"),
+        ("ZA", 144, "bfloat16"), ("ZR", 144, "bfloat16"), ("ZW", 144, "bfloat16"), ("ZK", 128, "bfloat16"),
+        ("IDM", 128, "bfloat16"), ("NID", 128, "bfloat16"), ("DNG", 128, "bfloat16"), ("DKH", 128, "bfloat16"), ("DKL", 128, "bfloat16"),
+        ("EQM", 128, "float32"), ("DNM", 128, "float32"), ("MVA", 128, "bfloat16"), ("MVV", 128, "bfloat16"),
+        ("BLK", 128, "bfloat16"), ("BM", 128, "bfloat16"), ("WM", 128, "bfloat16"), ("SVK", 128, "bfloat16"), ("TRI", 128, "bfloat16"),
+        ("VI", 16, "int32"), ("KI", 16, "int32"), ("KD", 16, "float32"), ("M1", 16, "float32"), ("SC", 16, "bfloat16"),
         ("AAS", 32, "float32"), ("DA", 16, "float32"), ("MA", 16, "float32"),
-        ("FW", 16, "bfloat16"), ("NF", 16, "float32"), ("GD", 16, "float32"), ("P1", 16, "float32"), ("JK", 16, "float32"),
+        ("FW", 16, "bfloat16"), ("NF", 16, "float32"), ("GD", 16, "float32"), ("P1", 16, "float32"),
         ("AV", 32, "uint16"), ("V16", 16, "uint16"), ("D16", 16, "uint16"), ("C16", 16, "uint16"),
         ("QG", 256, "bfloat16"), ("QT", 256, "bfloat16"), ("AG", 512, "bfloat16"), ("IOG", 256, "bfloat16"),
         ("EK", 256, "float32"), ("UG", 256, "int32"), ("TA", 256, "int32"), ("TB", 256, "int32"), ("UC", 256, "int32"),
         ("PLE", 256, "uint16"), ("OU", 128, "int32"), ("OA", 128, "int32"), ("OB", 128, "int32"),
         ("NEQ", 256, "float32"), ("DM", 256, "float32"), ("MN", 256, "int32"), ("IND", 256, "bfloat16"), ("FV", 256, "int32"),
-        ("YH", 512, "float32"), ("YVA", 512, "float32")):
+        ("XI", 128, "int32"), ("XC", 128, "float32"), ("EX", 8, "uint16"), ("P2", 32, "float32"), ("Y1", 128, "float32"),
+        ("Y2", 128, "float32"), ("YH", 512, "float32"), ("YV", 16, "float32"), ("YA", 16, "float32"), ("YN", 128, "float32")):
     SCRATCH[_n] = ("sbuf", [128, _s], _d)
 SCRATCH["PLO"] = ("sbuf", [128, NST, 256], "uint16")
-for _n, _s in (("W0", 1024), ("W1", 1024), ("W2", 512), ("KE", 512), ("KO", 512), ("M2", 512)):
+SCRATCH["Y3"] = ("sbuf", [128, 16, 16], "float32")
+for _n, _s in (("PW", 2560), ("KE", 512), ("KO", 512), ("M2", 512)):
     SCRATCH[_n] = ("psum", [128, _s], "float32")
-SEMAPHORES = ["qv", "qs", "qp", "qg", "pre", "sent"] + ["arr%d" % t for t in range(NST)] + ["d%d" % i for i in range(32)]
-SEMAPHORES += ["%s%d_%d" % (n, c, f) for n in ("hf", "mx") for c in range(NST) for f in range(2)]
+SEMAPHORES = ["qv", "qs", "qp", "qg", "pre", "sent"] + ["%s%d" % (n, t) for n in ("arr", "out") for t in range(NST)]
+SEMAPHORES += ["d%d" % i for i in range(24)] + ["%s%d_%d" % (n, c, f) for n in ("hf", "mx") for c in range(NST) for f in range(2)]
 
 
 def issue_order(tasks):
     last, readers, preds = {}, {}, []
-    for j, (q, rd, wr, cost, lat, emit) in enumerate(tasks):
+    for j, (q, rd, wr, cost, lat, emit, tag) in enumerate(tasks):
         p = [last[k] for k in rd + wr if k in last] + [i for k in wr for i in readers.get(k, ())]
         p += [i for k in rd if k[0] == "#" for i in readers.get(k, ()) if tasks[i][0] != q]
-        p = {i: -tasks[i][4] if q == "p" == tasks[i][0] else HOP for i in p if i != j}
-        preds.append(p)
+        preds.append({i: 0.0 if q == "p" == tasks[i][0] else HOP + tasks[i][4] for i in p if i != j})
         for k in wr:
             last[k], readers[k] = j, []
         for k in rd:
             readers.setdefault(k, []).append(j)
     every = range(len(tasks))
+    for q, names in ORDER.items():
+        names = names.split()
+        row = sorted((t[6][0], names.index(t[6][1]), j) for j, t in enumerate(tasks) if t[0] == q and t[6][1] in names)
+        for a, b in zip(row, row[1:]):
+            preds[b[2]].setdefault(a[2], 0.0)
     back = [{} for j in every]
-    way = [0.0] * len(tasks)
-    for j in reversed(every):
-        way[j] += tasks[j][3] + tasks[j][4]
+    for j in every:
         for i, h in preds[j].items():
-            preds[j][i] = back[i][j] = h + tasks[i][4]
-            way[i] = max(way[i], way[j] + h)
+            back[i][j] = h
+    way, left = [0.0] * len(tasks), [len(b) for b in back]
+    ready = [j for j in every if not left[j]]
+    for j in ready:
+        way[j] = tasks[j][3] + max([tasks[j][4]] + [h + way[k] for k, h in back[j].items()])
+        for i in preds[j]:
+            left[i] -= 1
+            if not left[i]:
+                ready.append(i)
+    assert len(ready) == len(tasks)
 
     def lay(order, edges, tail):
         end, taken = {}, {}
@@ -102,18 +129,26 @@ def helper(core, T, topo):
     return [c for c in topo.cores_of(core) if c not in T.cores and topo.die(c) == topo.die(core)][0]
 
 
+def fold_engines(owner, mate, T, topo):
+    off_chip = set(e for other in T.cores if other != owner for e in topo.engines(owner, other))
+    return [[e for e in topo.engines(owner, mate) if (e in off_chip) == side] for side in (False, True)]
+
+
+def back_engines(mate, owner, topo):
+    e = topo.engines(mate, owner)
+    return e[:len(e) // 2]
+
+
 def hand_back(g, core, owner, T, topo):
     rid, pid = topo.addr(owner)[:2]
-    off_chip = set(e for other in T.cores if other != owner for e in topo.engines(owner, other))
-    n_in = len([e for e in topo.engines(owner, core) if e not in off_chip])
-    w, n = 4096 // FOLDS, 0
-    for c in range(DIRECT, NST):
+    sets, back, n = fold_engines(owner, core, T, topo), back_engines(core, owner, topo), 0
+    for c in range(FOLD0, NST):
         name, c0 = PARK[c]
-        for f in range(FOLDS):
-            g.wait_ge(T.sem["hf%d_%d" % (c, f)], n_in)
-            g.remote_dma(T["GO%d" % (c % NB)][:, w * f:w * f + w], T[name][:, c0 + w * f:c0 + w * f + w], T.sem["mx%d_%d" % (c, f)],
-                         T.sem.sent, pid, rid, topo.mask(core, owner))
-            n += len(topo.engines(core, owner))
+        for f, (b, per, w) in sorted(enumerate(FOLD), key=lambda x: x[1][1] * x[1][2]):
+            g.wait_ge(T.sem["hf%d_%d" % (c, f)], len(sets[f]))
+            g.remote_dma(T["MX%d" % (c % NB)][:, b:b + per * w], T[name][:, c0 + b:c0 + b + per * w], T.sem["mx%d_%d" % (c, f)],
+                         T.sem.sent, pid, rid, sum(1 << e for e in back))
+            n += len(back)
     g.wait_ge(T.sem.sent, n)
 
 
@@ -130,6 +165,10 @@ def rank_program(g, core, T, topo):
     seen = {q: {} for q in queue}
     count = {}
     last, readers = {}, {}
+    tag, dmas, sent, ncol = [(-9, "")], [0], [0], {}
+
+    def named(w, name=""):
+        tag[0] = (w, name)
 
     def need(q, tok):
         s, n, clock = tok
@@ -169,37 +208,36 @@ def rank_program(g, core, T, topo):
             call().then_inc(T.sem[own], 1)
             count[own] = count.get(own, 0) + 1
             after((own, count[own], dict(seen[q])), rd, wr)
-        tasks.append((q, rd, wr, cost, 0.1 if q == "p" else 0.0, emit))
+        tasks.append((q, rd, wr, cost, 0.1 if q == "p" else 0.0, emit, tag[0]))
 
-    dmas = [0]
-
-    def dma(out, in_, nbytes, rd="", wr=""):
+    def dma(name, out, in_, nbytes, rd="", wr=""):
         rd, wr = rd.split(), wr.split()
-        s = "d%d" % dmas[0]
+        s, q = "d%d" % dmas[0], "s" if name in ORDER["s"].split() else "y"
         dmas[0] += 1
 
         def emit():
-            before("y", s, rd, wr)
-            g.sync.dma_start(out, in_).then_inc(T.sem[s], 16)
+            before(q, s, rd, wr)
+            queue[q].dma_start(out, in_).then_inc(T.sem[s], 16)
             count[s] = 16
-            after((s, 16, dict(seen["y"])), rd, wr)
-        tasks.append(("y", rd, wr, 0.05 + nbytes / DBW, DFIX, emit))
+            after((s, 16, dict(seen[q])), rd, wr)
+        tasks.append((q, rd, wr + [s], DQ, DFIX - DQ, emit, (tag[0][0], name)))
+        tasks.append(("e", rd + [s], wr, DROW + nbytes / DBW, 0.0, None, (tag[0][0], name)))
 
-    sent = [0]
-
-    def remote(call, rd, wr, sem, n, lat, n_sent, back=True):
+    def remote(call, rd, wr, sem, n, lat, n_sent, back=True, left=None):
         def emit():
             before("g", "x", rd, wr if back else [])
             call()
-            sent[0] += n_sent
+            if left:
+                after((left, n_sent, dict(seen["g"])), rd, [])
+                count[left] = n_sent
+            else:
+                sent[0] += n_sent
             after((sem, n, dict(seen["g"]) if back else {}), rd if back else [], wr)
             count[sem] = n
-        tasks.append(("g", rd, wr, 0.6, lat, emit))
+        tasks.append(("g", rd, wr, RCALL, lat, emit, tag[0]))
 
     def mm(out, lhs, rhs, start, stop, rd, wr, cy=64):
         op("p", lambda: g.tensor.matmul(out, lhs, rhs, start, stop), rd, wr, cy * PCY)
-
-    ncol = {}
 
     def col(name):
         if name not in ncol:
@@ -222,47 +260,65 @@ def rank_program(g, core, T, topo):
     def act(out, in_, f, rd, wr, cy=16, **kw):
         op("s", lambda: g.scalar.activation(out, in_, f, **kw), rd, wr, FIX + cy * CYC)
 
-    def iota(out, pattern, base, mult, wr, n):
-        op("g", lambda: g.iota(out, pattern, base, mult), "", wr, 0.13 + 2 * n * CYC)
+    def copy(q, out, in_, rd, wr, cy=16):
+        if q == "v":
+            cp(out, in_, rd, wr, cy)
+        else:
+            act(out, in_, F.Copy, rd, wr, cy)
 
-    def select(out, in_, pattern, mult, rd, wr, n):
-        op("g", lambda: g.affine_select(out, in_, pattern, A.is_equal, 0.0, 0, mult), rd, wr, 0.17 + 2 * n * CYC)
+    def iota(out, pattern, base, mult, wr, n, **kw):
+        op("g", lambda: g.iota(out, pattern, base, mult, **kw), "", wr, 0.13 + 2 * n * CYC)
 
-    dma(T.AR[:, 0:256], T.rf[0::16, :], 1 << 17, wr="AR0")
-    dma(T.AR[:, 256:512], T.an[:, :], 1 << 17, wr="AR1")
-    dma(T.WI[:], T.w[:], 512, wr="WI")
-    dma(T.TI[:], T.th[:], 512, wr="TI")
-    dma(T.XW[:, 0:4096], T.xc[:], 1 << 20, wr="X1")
-    for h in range(4):
-        dma(T.RI[:, 1024 * h:1024 * h + 1024], T.rf[:, 1024 * h:1024 * h + 1024], 1 << 19, wr="RI%d" % h)
-    iota(T.PI[:], [[0, 1]], 0, 1, "PI", 1)
-    iota(T.CI[:], [[1, 144]], 0, 0, "CI", 144)
-    iota(T.AR[:, 512:768], [[1, 256]], 0, 256, "AR2", 256)
-    iota(T.VI[:], [[256, 16]], 0, 16, "VI", 16)
-    iota(T.KI[:], [[-16, 16]], 319, -1, "KI", 16)
+    def select(out, in_, pattern, mult, rd, wr, n, test=A.is_equal):
+        op("g", lambda: g.affine_select(out, in_, pattern, test, 0.0, 0, mult), rd, wr, 0.17 + 2 * n * CYC)
 
-    SVall, AWall = "SV0 SV1 SV8 SV9", "AW0 AW1 AW8 AW9"
+    def wrap(o, Z, src, zk, sk, bank="#M2"):
+        for r in range(16):
+            mm(o, Z[:, 16 - r:144 - r], src(r), r == 0, r == 15, zk + " " + sk, bank)
+
+    AWall, RWall = "AW0 AW1 AW2 AW3 AW8 AW9", "RW0 RW1 RW2 RW3"
     Xown, Xall = "X1 X2 X3a", "X1 X2 X3a X3b"
     A16, V1 = T.AV[:, 0:16], T.AV[:, 16:32]
-    fill(T.SEL[:], 1.0, "SEL", 1024)
-    dma(T.AW[:, 0:4096], T.xc[:], 1 << 20, wr=AWall)
+
+    dma("AR0", T.AR[:, 0:256], T.rf[0::16, :], 1 << 17, wr="AR0")
+    dma("AR1", T.AR[:, 256:512], T.an[:, :], 1 << 17, wr="AR1")
+    dma("WI", T.WI[:], T.w[:], 512, wr="WI")
+    dma("TI", T.TI[:], T.th[:], 512, wr="TI")
+    dma("X1", T.XW[:, 0:4096], T.xc[:], 1 << 20, wr="X1")
+    for h in range(2):
+        dma("RI%d" % h, T.RI[:, 2048 * h:2048 * h + 2048], T.rf[:, 2048 * h:2048 * h + 2048], 1 << 20, wr="RI%d RI%d" % (2 * h, 2 * h + 1))
+    named(-9, "X2")
+    if X2_ON == "y":
+        dma("X2", T.XW[:, 4096:8192], T.xc[:], 1 << 20, wr="X2")
+    else:
+        act(T.XW[:, 4096:8192], T.XW[:, 0:4096], F.Copy, "X1", "X2", 4096)
+    named(-9, "X3a")
+    act(T.XW[:, 8192:XA], T.XW[:, 0:XA - 8192], F.Copy, "X1", "X3a", 1024)
+    dma("X3b", T.XW[:, XA:12288], T.xc[:, XA - 8192:4096], 3 << 18, wr="X3b")
+    named(-9, "iota")
+    iota(T.PI[:], [[0, 1]], 0, 1, "PI", 1)
+    iota(T.CI[:], [[1, 144]], 0, 0, "CI", 144)
+    iota(T.VI[:], [[16, 16]], 0, 256, "VI", 16)
+    iota(T.KI[:], [[1, 16]], -320, 16, "KI", 16)
+    named(-9, "XL")
+    iota(T.ARB[:, 1280:1536], [[1, 256]], 0, 0, "L2", 256, allow_small_or_imprecise_dtypes=True)
+    named(-9, "sel0")
+    iota(T.SEL[:], [[-1, 128], [0, 16]], 1, 1, "SEL", 2048, allow_small_or_imprecise_dtypes=True)
+    named(-9, "sel")
     select(T.SEL[:], T.SEL[:], [[-1, 128], [0, 16]], 1, "SEL", "SEL", 2048)
-    fill(T.SV[:], 1.0, SVall, 2048)
-    ts(T.AR[:, 512:768], T.AR[:, 512:768], 4095, None, A.bitwise_and, None, "AR2", "AR2", 256)
-    for j in range(3):
+    named(-9)
+    fill(T.AW[:, 0:4096], 1.0, AWall, 2048)
+    for j in range(2):
         a, b = 256 * j, 256 * j + 256
         cp(T.ARB[:, a:b], T.AR[:, a:b], "AR%d" % j, "H%d" % j, 256)
         tt(T.ARB[:, 768 + a:768 + b], T.AR[:, a:b], T.ARB[:, a:b], A.subtract, "AR%d H%d" % (j, j), "L%d" % j, 512)
 
-    def rows(name, row, j, shift=0):
+    def rows(row, j, shift=0):
         for h in range(2):
-            dma(T[name][row + h::16, shift:4096 + shift], T.ARB[:, 768 * h + 256 * j:768 * h + 256 * j + 256], 1 << 16,
-                rd="HL"[h] + str(j), wr=name + str(row + h))
+            dma("AW%d" % (row + h), T.AW[row + h::16, shift:4096 + shift], T.ARB[:, 768 * h + 256 * j:768 * h + 256 * j + 256], 1 << 16,
+                rd="HL"[h] + str(j), wr="AW%d LD%d" % (row + h, row + h))
 
-    rows("SV", 0, 0)
-    rows("AW", 8, 1)
-    rows("SV", 8, 2)
-    rows("AW", 0, 0, 1)
+    rows(0, 0, 1)
 
     cp(col("p"), T.PI[:], "PI", "c_p")
     ts(T.PGI[:], T.PI[:], 112, None, A.bitwise_and, None, "PI", "PGI")
@@ -272,13 +328,23 @@ def rank_program(g, core, T, topo):
     cp(col("pg"), T.PGI[:], "PGI", "c_pg")
     ts(col("pg16"), T.PGI[:], 16.0, None, A.add, None, "PGI", "c_pg16")
     ts(col("pgx"), T.PGI[:], 16.0, None, A.mult, None, "PGI", "c_pgx")
-    for name, pair in (("kr", 0), ("ka", 4)):
+    ts(col("pgy"), T.PGI[:], 256.0, None, A.mult, None, "PGI", "c_pgy")
+    ts(col("k256"), T.PKI[:], 256.0, None, A.mult, None, "PKI", "c_k256")
+    fill(T.ALL1[:], 1.0, "ALL1", 128)
+    act(T.ARB[:, 512:768], T.ALL1[:], F.Copy, "ALL1 c_k256", "H2", 256, scale=col("k256"))
+    for name, pair in (("kr", 0), ("kx", 1), ("ka", 4)):
         ts(col(name), T.PK2[:], float(pair), None, A.is_equal, None, "PK2", "c_" + name)
     ts(col("k4"), T.PKI[:], 4.0, NEG, A.is_equal, A.mult, "PKI", "c_k4")
     ts(col("k5"), T.PKI[:], 5.0, 4096.0, A.is_equal, A.mult, "PKI", "c_k5")
     ts(col("nk"), T.PKI[:], 0.0, None, A.is_gt, None, "PKI", "c_nk")
-    tt(col("k45"), col("k4"), col("k5"), A.add, "c_k4 c_k5", "c_k45")
-    tt(col("kk"), col("kr"), col("k45"), A.add, "c_kr c_k45", "c_kk")
+    ts(col("kk"), col("kr"), col("k4"), col("k5"), A.add, A.add, "c_kr c_k4 c_k5", "c_kk")
+    ts(col("k4n"), T.PKI[:], 4.0, -1.0, A.is_equal, A.mult, "PKI", "c_k4n")
+    tt(col("pm"), col("p"), col("k4n"), A.add, "c_p c_k4n", "c_pm")
+    tt(col("kv"), col("kx"), col("k4n"), A.add, "c_kx c_k4n", "c_kv")
+    ts(col("p6"), T.PI[:], 6.0, None, A.add, None, "PI", "c_p6")
+    ts(col("s0"), T.PKI[:], -16.0, 256.0, A.mult, A.add, "PKI", "c_s0")
+    ts(col("s1"), T.PKI[:], 8.0, -248.0, A.mult, A.add, "PKI", "c_s1")
+    ts(col("s2"), T.PKI[:], col("s1"), 64.0, A.mult, A.add, "c_s1 PKI", "c_s2")
     cp(col("w"), T.WI[:], "WI", "c_w")
     ts(col("th"), T.TI[:], 8192.0, NEG, A.mult, A.add, "TI", "c_th")
     ts(T.KCI[:], T.PKI[:], 613.0, None, A.mult, None, "PKI", "KCI")
@@ -291,327 +357,403 @@ def rank_program(g, core, T, topo):
 
     ts(T.Z1[:], T.CI[:], col("pg16"), None, A.is_equal, None, "CI c_pg16", "Z1", 144)
     ts(T.BLK[:], T.MG[:], col("pg"), None, A.is_equal, None, "MG c_pg", "BLK", 128)
-    ts(T.IDM[:], T.CI[:, 0:128], col("p"), None, A.is_equal, None, "CI c_p", "IDM", 128)
+    named(-9, "idm")
+    select(T.IDM[:], T.ALL1[:, 0:128], [[-1, 128]], 1, "ALL1", "IDM", 128)
+    named(-9, "tri")
+    select(T.TRI[:], T.BLK[:], [[1, 128]], -1, "BLK", "TRI", 128, A.is_gt)
     for base, names in (("Z1", (("ZW", "w"), ("ZR", "kr"), ("ZA", "ka"), ("Z8", 8192.0), ("Z16", 16384.0), ("ZM", -8192.0))),
-                        ("BLK", (("WM", "w"), ("SVK", "kk"), ("SVA", "ka"), ("BM", -8192.0))),
+                        ("BLK", (("WM", "w"), ("SVK", "kk"), ("BM", -8192.0))),
                         ("IDM", (("NID", -1.0), ("DNG", NEG), ("DKH", "kh"), ("DKL", "kl"), ("DNM", "nk")))):
         for name, x in names:
+            named(-9, name)
             if isinstance(x, float):
                 act(T[name][:], T[base][:], F.Copy, base, name, 144, scale=x)
             else:
                 act(T[name][:], T[base][:], F.Copy, base + " c_" + x, name, 144, scale=col(x))
-    fill(T.ALL1[:], 1.0, "ALL1", 128)
-    fill(T.ZERO[:], 0.0, "ZERO")
-    fill(T.ZB[:], 0.0, "ZB")
-    fill(T.SC[:], 0.0, "SC")
-    ts(T.SVE[:], T.CI[:, 0:128], col("pg"), col("kr"), A.is_equal, A.mult, "CI c_pg c_kr", "SVE", 128)
+    named(-9, "ZK")
+    for j, (a, b, rd) in enumerate(((T.Z1[:, 12:140], T.DKH[:], "Z1 DKH"), (T.Z1[:, 11:139], T.DKL[:], "Z1 DKL"),
+                                    (T.IDM[:], T.ZR[:, 16:144], "IDM ZR"))):
+        mm(T.M2[:, 0:128], a, b, j == 0, j == 2, rd, "#M2", 128)
+    act(T.ZK[:], T.M2[:, 0:128], F.Copy, "#M2", "ZK", 128)
+    named(-9, "eqm")
     ts(T.T2[:], T.MG[:], col("p"), None, A.is_equal, None, "MG c_p", "T2", 128)
     tt(T.EQM[:], T.IDM[:], T.T2[:], A.subtract, "IDM T2", "EQM", 256)
-    ts(T.T3[:], T.CI[:, 0:128], col("p"), None, A.is_gt, None, "CI c_p", "T3", 128)
-    tt(T.TRI[:], T.T3[:], T.BLK[:], A.mult, "T3 BLK", "TRI", 256)
-    ts(T.KD[:], T.KI[:], col("pg"), 1.0 / 4096, A.add, A.mult, "KI c_pg", "KD")
-    ts(T.V16[:], T.VI[:], col("pgx"), None, A.subtract, None, "VI c_pgx", "V16")
-    ts(V1, T.VI[:], col("pgx"), 1.0, A.subtract, A.add, "VI c_pgx", "V1")
+    named(-9)
+    fill(T.M1[:], -1.0, "M1")
+    fill(T.ZB[:], 0.0, "ZB")
+    ts(T.MVA[:], T.CI[:, 0:128], col("p6"), col("kx"), A.is_equal, A.mult, "CI c_p6 c_kx", "MVA", 128)
+    ts(T.MVV[:], T.CI[:, 0:128], col("pm"), col("kv"), A.is_equal, A.mult, "CI c_pm c_kv", "MVV", 128)
+    ts(T.KD[:], T.KI[:], col("pgx"), None, A.subtract, None, "KI c_pgx", "KD")
+    ts(T.V16[:], T.VI[:], col("pgy"), None, A.subtract, None, "VI c_pgy", "V16")
+    ts(V1, T.VI[:], col("pgy"), 1.0, A.subtract, A.add, "VI c_pgy", "V1")
+    cp(A16, T.AR[:, 256:512:16], "AR1", "A16")
+    named(NST - 4, "Q")
+    iota(T.XI[:], [[16, 16], [1, 8]], 0, 256, "XI", 128)
+    named(NST - 3, "p2")
+    ts(T.XC[:], T.XI[:], col("pgy"), None, A.subtract, None, "XI c_pgy", "XC", 128)
+    ts(col("k8"), T.PKI[:], 7.5, None, A.is_gt, None, "PKI", "c_k8")
+    ts(T.EX[:], T.CI[:, 0:8], 2.0, col("k8"), A.mult, A.add, "CI c_k8", "EX")
 
-    def wrap(o, Z, src, zk, sk, bank="#M2"):
-        for il in range(16):
-            mm(o, Z[:, 16 - il:144 - il], src(il), il == 0, il == 15, zk + " " + sk, bank)
+    def wb(b, n=1):
+        if b == 5:
+            return T.KO[:], "#KO"
+        return T.PW[:, 512 * b:512 * (b + n)], " ".join("#W%d" % (b + j) for j in range(n))
+
+    def units(name, u0, n=1):
+        return " ".join("%s%d" % (name, u) for u in range(u0, u0 + n))
+
+    mate = helper(core, T, topo)
+    mrid, mpid = topo.addr(mate)[:2]
+    sets = fold_engines(core, mate, T, topo)
 
     def own_lists(c0, c1):
-        for c in range(c0, c1):
-            wrap(T.KE[:, 16 * c:16 * c + 16], T.ZW, lambda il, c=c: T.XW[:, 16 * il + c:4096:256], "ZW", "X1", "#KE")
-        for c in range(c0, c1):
-            wrap(T.KE[:, 128 + 16 * c:144 + 16 * c], T.ZR, lambda il, c=c: T.SV[:, 16 * il + c:4096:256], "ZR", SVall, "#KE")
-        a, b, key = 16 * c0, 16 * c1, " ".join("PLO%d" % c for c in range(c0, c1))
-        cp(T.OA[:, a:b], T.KE[:, a:b], "#KE", "OA", b - a)
+        P, z, bk = (T.KO, 0, "#KO") if c0 == 0 else (T.PW, 2048, "#W4")
+        for Z in ("ZW", "ZR") if c0 == 0 else ("ZR", "ZW"):
+            for c in range(c0, c1):
+                if Z == "ZW":
+                    wrap(P[:, z + 16 * c:z + 16 * c + 16], T.ZW, lambda r, c=c: T.XW[:, 16 * r + c:4096:256], "ZW", "X1", bk)
+                else:
+                    wrap(P[:, z + 128 + 16 * c:z + 144 + 16 * c], T.ZR, lambda r, c=c: T.AW[:, 16 * r + c + 1:4096:256], "ZR", AWall, bk)
+        a, b, key = 16 * c0, 16 * c1, units("PLO", c0, c1 - c0)
+        cp(T.OA[:, a:b], P[:, z + a:z + b], bk, "OA", b - a)
         ts(T.OU[:, a:b], T.OA[:, a:b], 4095, None, A.bitwise_and, None, "OA", "OU", b - a)
-        tt(T.OA[:, a:b], T.KE[:, 128 + a:128 + b], T.OU[:, a:b], A.mult, "#KE OU", "OA", b - a)
+        tt(T.OA[:, a:b], P[:, z + 128 + a:z + 128 + b], T.OU[:, a:b], A.mult, bk + " OU", "OA", b - a)
         ts(T.OB[:, a:b], T.OA[:, a:b], 5, 4095, A.arith_shift_right, A.bitwise_and, "OA", "OB", b - a)
-        tt(T.OA[:, a:b], T.KE[:, 128 + a:128 + b], T.OB[:, a:b], A.add, "#KE OB", "OA", b - a)
+        tt(T.OA[:, a:b], P[:, z + 128 + a:z + 128 + b], T.OB[:, a:b], A.add, bk + " OB", "OA", b - a)
         ts(T.OB[:, a:b], T.OA[:, a:b], 4095, None, A.bitwise_and, None, "OA", "OB", b - a)
         cp(T.PLO[:, c0:c1, 0:16], T.OB[:, a:b], "OB", key, b - a)
         for n in (1, 2, 4, 8):
             ts(T.PLO[:, c0:c1, 16 * n:32 * n], T.PLO[:, c0:c1, 0:16 * n], float(613 * n % 4096), None, A.add, None, key, key, n * (b - a) // 2)
 
-    def wb(b, n=1):
-        if b == 4:
-            return T.M2[:], "#M2"
-        return T["W%d" % (b // 2)][:, 512 * (b % 2):512 * (b % 2 + n)], " ".join("#W%d" % (b + j) for j in range(n))
+    def gk(c, k, n=1, name="G"):
+        return units("%s%d_" % (name, c % NB), k, n)
 
-    def abk(b, n=1):
-        return " ".join("AB%d" % (b + j) for j in range(n))
+    def total(k, Z, src, sk, first=False):
+        mm(T.KO[:, 0:256], T[Z][:, 16 - k:144 - k], src, first, False, Z + " " + sk, "#KO", 256)
 
-    mate = helper(core, T, topo)
-    mrid, mpid = topo.addr(mate)[:2]
-    off_chip = set(e for other in T.cores if other != core for e in topo.engines(core, other))
-    free = [e for e in topo.engines(core, mate) if e not in off_chip]
-
-    def gk(c, k):
-        return "G%d_%d" % (c % NB, k // 2)
-
-    def total(c, k, Z, src, sk, first=False):
-        o, bk = ((T.KO, "#KO"), (T.W2, "#W4"))[c % 2]
-        mm(o[:, 0:256], T[Z][:, 16 - k:144 - k], src, first, False, Z + " " + sk, bk, 256)
-
-    def own_gather(c, pieces):
+    def own_gather(c):
         G, k0 = T["GO%d" % (c % NB)], 0
-        for n, q in pieces:
-            src = T.XW[:, 0:XA].indirect(T.PLO[:, c, 16 * k0:16 * (k0 + n)])
-            out, rd, wr = G[:, 256 * k0:256 * (k0 + n)], Xown + " PLO%d" % c, " ".join(gk(c, k) for k in range(k0, k0 + n, 2))
-            if q == "v":
-                cp(out, src, rd, wr, GA * 256 * n)
-            else:
-                act(out, src, F.Copy, rd, wr, GA * 256 * n)
+        for j, (n, q, ahead) in enumerate(OWN if c >= NB else [(4, q, 0) for q in OWN0[c]]):
+            named(*((c - ahead, "o%d" % j) if c >= NB else (-9, "o%d_%d" % (c, j))))
+            copy(q, G[:, 256 * k0:256 * (k0 + n)], T.XW[:, 0:XA].indirect(T.PLO[:, c, 16 * k0:16 * (k0 + n)]), Xown + " PLO%d" % c,
+                 gk(c, k0, n), GA * 256 * n)
             k0 += n
 
-    def own_fold(c):
+    def own_max(c):
+        G, M, Q, qk = T["GO%d" % (c % NB)], T["MX%d" % (c % NB)], T["QR%d" % (c % NB)], []
         if c < DIRECT:
             return
-        G = T["GO%d" % (c % NB)]
-        o, bk = ((T.KO, "#KO"), (T.W2, "#W4"))[c % 2]
-        mm(o[:, 0:256], T.BM[:], T.XW[:, c:4096:16], True, False, "BM X1", bk, 256)
-        for k in range(16):
-            total(c, k, "ZM", G[:, 256 * k:256 * k + 256], gk(c, k))
-        Q = T["Q4%d" % (c % 2)]
-        for h in range(2):
-            select(Q[:, 512 * h:512 * h + 512], T.XW[:, c:8192:16], [[0, 512]], 0, "X1 X2", "Q%d_%d" % (c % 2, h), 512)
-        per = 4 // FOLDS
-        ne = len(free) // per
-        for f in range(FOLDS):
-            trs = []
+        if c < FOLD0:
+            w, wk = wb(4)
+            named(-9, "m%d" % c)
+            mm(w, T.IDM[:], T.XW[:, c:8192:16], True, True, "IDM X1 X2", wk, 512)
+            for k in range(0, 16, 2):
+                named(-9, "m%d%d" % (c, k // 4))
+                tt(M[:, 256 * k:256 * k + 512], G[:, 256 * k:256 * k + 512], w, A.max, wk + " " + gk(c, k, 2), gk(c, k, 2, "MX"), 512)
+            return
+        named(*((c - AHEAD - 1, "Q") if c > NB else (0 if c == NB else -9, "Q%d" % c)))
+        for b in range(0, QW, 512):
+            n = min(512, QW - b)
+            qk.append("Q%d_%d" % (c % NB, b))
+            select(Q[:, b:b + n], T.XW[:, c:16 * n:16], [[0, n]], 0, "X1 X2", qk[-1], n)
+        name, c0 = PARK[c]
+        for f, (b0, per, w) in enumerate(FOLD):
+            ne, trs = len(sets[f]) // per, []
             for j in range(per):
-                b = 1024 * (f * per + j)
-                name, c0 = PARK[c]
+                b = b0 + w * j
                 trs.append(RemoteDMATransfer(
-                    dst_ids=[DstId(rid=mrid, pnc=mpid)], dma_engine_mask=sum(1 << e for e in free[ne * j:ne * j + ne]),
-                    remote_sem=T.sem["hf%d_%d" % (c, f)], srcs=[G[:, b:b + 1024], Q[:]], dsts=[T[name][:, c0 + b:c0 + b + 1024]], alu_op=2))
-            wr = [gk(c, k) for k in range(4 * per * f, 4 * per * (f + 1), 2)]
-            remote(lambda trs=trs: g.remote_dma_fused(trs, local_sem=T.sem.sent), ["Q%d_0" % (c % 2), "Q%d_1" % (c % 2)], wr, "mx%d_%d" % (c, f),
-                   len(topo.engines(mate, core)), FLAT / (1 + 0.3 * (FOLDS - 1)), len(free))
+                    dst_ids=[DstId(rid=mrid, pnc=mpid)], dma_engine_mask=sum(1 << e for e in sets[f][ne * j:ne * j + ne]),
+                    remote_sem=T.sem["hf%d_%d" % (c, f)], srcs=[G[:, b:b + w], Q[:, b % 256:b % 256 + w]],
+                    dsts=[T[name][:, c0 + b:c0 + b + w]], alu_op=2))
+            k0, n = b0 // 256, per * w // 256
+            named(*((c - AHEAD, "fold%d" % f) if c >= NB else (-9, "f%d%d" % (c, f))))
+            remote(lambda trs=trs: g.remote_dma_fused(trs, local_sem=T.sem.sent), qk + gk(c, k0, n).split() + ["LD9"] * (c == FOLD0),
+                   gk(c, k0, n, "MX").split(), "mx%d_%d" % (c, f), len(back_engines(mate, core, topo)), FLAT[f], len(sets[f]))
 
     def own_close(c):
-        G = T["GO%d" % (c % NB)]
-        o, bk = ((T.KO, "#KO"), (T.W2, "#W4"))[c % 2]
+        G, M = T["GO%d" % (c % NB)], T["MX%d" % (c % NB)]
         if c < DIRECT:
             for j in range(4):
                 b = 2 * (j % 2)
+                named(-9, "d%d%d" % (c, j))
                 for h in range(2):
                     w, wk = wb(b + h)
+                    k = 4 * j + 2 * h
                     mm(w, T.IDM[:], T.XW[:, c:8192:16], True, False, "IDM X1 X2", wk, 512)
-                    mm(w, T.NID[:], G[:, 1024 * j + 512 * h:1024 * j + 512 * h + 512], False, True, "NID " + gk(c, 4 * j + 2 * h), wk, 512)
+                    mm(w, T.NID[:], G[:, 256 * k:256 * k + 512], False, True, "NID " + gk(c, k, 2), wk, 512)
                 w, wk = wb(b, 2)
-                act(T.AB[:, 512 * b:512 * b + 1024], w, F.Abs, wk, abk(b, 2), 1024)
+                act(T.AB[:, 512 * b:512 * b + 1024], w, F.Abs, wk, units("AB", b, 2), 1024)
+                named(-9, "e%d%d" % (c, j))
                 for k in range(4):
-                    total(c, 4 * j + k, "Z8", T.AB[:, 512 * b + 256 * k:512 * b + 256 * k + 256], abk(b + k // 2), j + k == 0)
+                    total(4 * j + k, "Z8", T.AB[:, 512 * b + 256 * k:512 * b + 256 * k + 256], units("AB", b + k // 2), j + k == 0)
         else:
+            part = [(c - ahead, "k%d" % j) for j, (n, ahead) in enumerate(CLOSE) for _ in range(n)]
+            named(*part[0])
+            mm(T.KO[:, 0:256], T.BM[:], T.XW[:, c:4096:16], True, False, "BM X1", "#KO", 256)
             for k in range(16):
-                total(c, k, "Z16", G[:, 256 * k:256 * k + 256], gk(c, k))
-        mm(o[:, 0:256], T.SVK[:], T.SV[:, c::16], False, True, "SVK " + SVall, bk, 256)
-        act(T.KOT[:, c::16], o[:, 0:256], F.Copy, bk, "KOT", 256)
+                named(*part[k])
+                total(k, "ZM", G[:, 256 * k:256 * k + 256], gk(c, k))
+            for k in range(16):
+                named(*part[16 + k])
+                total(k, "Z16", M[:, 256 * k:256 * k + 256], gk(c, k, 1, "MX"))
+        named(*((c - 1, "kot") if c >= DIRECT else (-9, "kot%d" % c)))
+        mm(T.KO[:, 0:256], T.SVK[:], T.AW[:, c + 1:4096:16], False, True, "SVK " + AWall, "#KO", 256)
+        act(T.KOT[:, c::16], T.KO[:, 0:256], F.Copy, "#KO", "KOT", 256)
 
-    CNT, AAW, AVW, TRI_, TOT, FITS = (T.M2[:, 256 + 16 * j:272 + 16 * j] for j in range(6))
+    CNT, AAW, ROW, TOT = T.M2[:, 256:272], T.M2[:, 272:304], T.M2[:, 304:305], T.M2[:, 305:306]
 
-    def at_v():
+    def at(w, name, early=0):
+        named(*((w - early, name) if w >= 0 else (-9, name.lower() + "0")))
+
+    def at_v(w):
+        at(w, "QG", 1)
         act(T.QG[:], T.XW[:, 0:4096].indirect(T.V16[:]), F.Copy, "X1 V16", "QG", GA * 256)
+        at(w, "u")
         mm(T.KE[:, 0:256], T.WM[:], T.QG[:], True, True, "WM QG", "#KE", 256)
+        P, z, bk = (T.PW, 2048, "#W4") if w >= 0 else (T.M2, 0, "#M2")
         for h in range(2):
-            mm(T.KE[:, 256 + 128 * h:384 + 128 * h], T.QG[:, 128 * h:128 * h + 128], T.IDM[:], True, True, "QG IDM", "#KE", 128)
+            mm(P[:, z + 128 * h:z + 128 + 128 * h], T.QG[:, 128 * h:128 * h + 128], T.IDM[:], True, True, "QG IDM", bk, 128)
+        at(w, "QT")
+        act(T.QT[:], P[:, z:z + 256], F.Copy, bk, "QT", 256)
+        at(w, "UC")
         cp(T.UC[:], T.KE[:, 0:256], "#KE", "UC", 256)
-        act(T.QT[:], T.KE[:, 256:512], F.Copy, "#KE", "QT", 256)
+        at(w, "UG")
         ts(T.UG[:], T.UC[:], 4095, None, A.bitwise_and, None, "UC", "UG", 256)
 
-    def at_a():
+    def at_a(w):
+        at(w, "AG")
         act(T.AG[:], T.AW[:, 0:4096].indirect(T.AV[:]), F.Copy, AWall + " A16 V1", "AG", GA * 512)
-        wrap(T.M2[:, 272:304], T.ZA, lambda il: T.AG[:, il::16], "ZA", "AG")
-        act(T.AAS[:], T.M2[:, 272:304], F.Copy, "#M2", "AAS")
+        at(w, "ZA")
+        wrap(AAW, T.ZA, lambda r: T.AG[:, r::16], "ZA", "AG")
+        if w < NST - 2:
+            mm(T.M2[:, 0:256], T.MVA[:], T.AG[:, 0:256], True, False, "MVA AG", "#M2", 256)
+            mm(T.M2[:, 0:256], T.MVV[:], T.AG[:, 256:512], False, True, "MVV AG", "#M2", 256)
+            at(w, "IOG")
+            act(T.IOG[:], T.M2[:, 0:256], F.Copy, "#M2", "IOG", 256)
+        at(w, "AAS")
+        act(T.AAS[:], AAW, F.Copy, "#M2", "AAS", 32)
+        at(w, "DA")
         tt(T.DA[:], T.AAS[:, 16:32], T.AAS[:, 0:16], A.subtract, "AAS", "DA")
 
     def keys(i0, i1):
-        return (T.KE[:, i0:i1], "#KE") if i0 < CUT else (T.M2[:, 352 + i0 - CUT:352 + i1 - CUT], "#M2")
+        return (T.KE[:, i0:i1], "#KE") if i0 < CUT else (T.M2[:, 320 + i0 - CUT:320 + i1 - CUT], "#M2")
 
-    def strict_pass():
-        for j in range(len(PLACES) - 1):
-            i0, i1 = PLACES[j], PLACES[j + 1]
+    def strict_pass(s):
+        parts = list(zip(PLACES, PLACES[1:]))
+        for j, (i0, i1) in enumerate(parts):
             R, n = T.RW[:, 0:4096].indirect(T.AV[:, i0 // 16:i1 // 16]), i1 - i0
-            act(T.EK[:, i0:i1], R, F.Identity, "RW A16 c_kc", "EK%d" % j, GA * n, bias=col("kc"))
-            tt(T.TA[:, i0:i1], R, T.UG[:, i0:i1], A.mult, "RW A16 UG", "TA%d" % j, GA * n)
+            named(s, "TA%d" % j)
+            act(T.EK[:, i0:i1], R, F.Identity, RWall + " A16 c_kc", "EK%d" % j, GA * n, bias=col("kc"))
+            tt(T.TA[:, i0:i1], R, T.UG[:, i0:i1], A.mult, RWall + " A16 UG", "TA%d" % j, GA * n)
+            named(s, "TB%d" % j)
             ts(T.TB[:, i0:i1], T.TA[:, i0:i1], 5, 4095, A.arith_shift_right, A.bitwise_and, "TA%d" % j, "TB%d" % j, n)
+            named(s, "PL%d" % j)
             tt(T.PLE[:, i0:i1], T.EK[:, i0:i1], T.TB[:, i0:i1], A.add, "EK%d TB%d" % (j, j), "PLE%d" % j, 2 * n)
-        ek = " ".join("EK%d" % j for j in range(len(PLACES) - 1))
+        ek = units("EK", 0, len(parts))
+        named(s, "NEQ")
         mm(T.M2[:, 0:256], T.EQM[:], T.EK[:], True, True, "EQM " + ek, "#M2", 1024)
-        if NEQ_ON == "s":
-            act(T.NEQ[:], T.M2[:, 0:256], F.Abs, "#M2 c_kq", "NEQ", 256, scale=33554432.0, bias=col("kq"))
-        else:
-            ts(T.NEQ[:], T.M2[:, 0:256], col("kc"), 33554432.0, A.not_equal, A.mult, "#M2 c_kc", "NEQ", 256)
+        act(T.NEQ[:], T.M2[:, 0:256], F.Abs, "#M2 c_kq", "NEQ", 256, scale=33554432.0, bias=col("kq"))
+        named(s, "DM")
         tt(T.DM[:], T.KOT[:].indirect(T.V16[:]), T.NEQ[:], A.add, "KOT V16 NEQ", "DM", GA * 256)
 
-        way = {u: q for u0, n, q in SIZES for u in range(u0, u0 + n)}
+        way = {u: q for q, u0, n, bank in HEAVY if bank is not None for u in range(u0, u0 + n)}
 
         def add(i0, i1, lhs, rhs, rd, slow=1):
             o, bk = keys(i0, i1)
-            mm(o, lhs, rhs, False, False, rd + " " + bk, " ".join("K%d" % u for u in range(i0 // 32, i1 // 32)), slow * max(64, i1 - i0))
+            mm(o, lhs, rhs, False, False, rd + " " + bk, units("K", i0 // 32, (i1 - i0) // 32), slow * max(64, i1 - i0))
 
         def low(i0, i1):
-            add(i0, i1, T.SVE[:], T.AG[:, 256 + i0:256 + i1], "SVE AG")
-            add(i0, i1, T.DKH[:], T.ALL1[:, i0:i1], "DKH ALL1")
-            add(i0, i1, T.DKL[:], T.ALL1[:, i0:i1], "DKL ALL1")
+            add(i0, i1, T.ZK[:], T.AG[:, 256 + i0:256 + i1], "ZK AG")
             add(i0, i1, T.DNM[:], T.EK[:, i0:i1], "DNM " + ek, 4)
 
-        for i0, i1 in ((0, CUT), (CUT, 256)):
-            if i1 > i0:
-                o, bk = keys(i0, i1)
-                mm(o, T.DNG[:], T.ALL1[:, i0:i1], True, False, "DNG ALL1", bk, max(64, i1 - i0))
-                j1 = min([i1] + [32 * u0 for u0, n, q in SIZES if q == "v" and 32 * u0 >= i0])
-                if j1 > i0:
-                    low(i0, j1)
-        for u0, n, q in GATH:
-            src = T.XW[:].indirect(T.PLE[:, 32 * u0:32 * (u0 + n)])
-            rd = Xall + "".join(" PLE%d" % j for j in range(len(PLACES) - 1) if PLACES[j] < 32 * (u0 + n) and PLACES[j + 1] > 32 * u0)
-            key = " ".join("GE%d" % u for u in range(u0, u0 + n))
-            if q == "v":
-                cp(T.GE[:, 512 * u0:512 * (u0 + n)], src, rd, key, GA * 512 * n)
-            else:
-                act(T.GE[:, 512 * u0:512 * (u0 + n)], src, F.Copy, rd, key, GA * 512 * n)
-        for u0, n, q in SIZES:
-            b, i0, i1 = BANK[u0], 32 * u0, 32 * (u0 + n)
-            ge, ab = (" ".join("%s%d" % (x, u) for u in range(u0, u0 + n)) for x in ("GE", "AB"))
+        for j, (i0, i1) in enumerate(((0, CUT), (CUT, 256))):
+            o, bk = keys(i0, i1)
+            named(s, "open%d" % j)
+            mm(o, T.DNG[:], T.ALL1[:, i0:i1], True, False, "DNG ALL1", bk, max(64, i1 - i0))
+            for u0, n in SUMS:
+                if way[u0] == "s" and i0 <= 32 * u0 < i1:
+                    low(32 * u0, 32 * (u0 + n))
+        for q, u0, n, bank in HEAVY:
+            i0, i1, ge, ab = 32 * u0, 32 * (u0 + n), units("GE", u0, n), units("AB", u0, n)
+            if bank is None:
+                rd = Xall + "".join(" PLE%d" % j for j, (a, b) in enumerate(parts) if a < i1 and b > i0)
+                named(s, "g%d" % u0)
+                copy(q, T.GE[:, 16 * i0:16 * i1], T.XW[:].indirect(T.PLE[:, i0:i1]), rd, ge, GA * 512 * n)
+                continue
             for u in range(u0, u0 + n):
-                w, wk = wb(BANK[u])
+                w, wk = wb(bank + u - u0)
+                named(s, "q%d" % u)
                 mm(w, T.QT[:, 128 * (u // 4):128 * (u // 4) + 128], T.SEL[:, 512 * (u % 4):512 * (u % 4) + 512], True, q == "v", "QT SEL", wk, 512)
                 if q == "s":
+                    named(s, "n%d" % u)
                     mm(w, T.NID[:], T.GE[:, 512 * u:512 * u + 512], False, True, "NID GE%d" % u, wk, 512)
-            w, wk = wb(b, n)
+            w, wk = wb(bank, n)
+            named(s, "a%d" % u0)
             if q == "s":
-                act(T.AB[:, 512 * u0:512 * (u0 + n)], w, F.Abs, wk, ab, 512 * n)
+                act(T.AB[:, 16 * i0:16 * i1], w, F.Abs, wk, ab, 512 * n)
             else:
-                tt(T.AB[:, 512 * u0:512 * (u0 + n)], T.GE[:, 512 * u0:512 * (u0 + n)], w, A.max, wk + " " + ge, ab, 512 * n)
+                tt(T.AB[:, 16 * i0:16 * i1], T.GE[:, 16 * i0:16 * i1], w, A.max, wk + " " + ge, ab, 512 * n)
         for u0, n in SUMS:
-            i0, i1, q = 32 * u0, 32 * (u0 + n), way[u0]
-            ge, ab = (" ".join("%s%d" % (x, u) for u in range(u0, u0 + n)) for x in ("GE", "AB"))
+            i0, i1, q, ge, ab = 32 * u0, 32 * (u0 + n), way[u0], units("GE", u0, n), units("AB", u0, n)
             if q == "v":
+                named(s, "x%d" % u0)
                 add(i0, i1, T.BM[:], T.QG[:, i0:i1], "BM QG")
                 for k in range(16):
-                    add(i0, i1, T.ZM[:, 16 - k:144 - k], T.GE[:, 512 * u0 + k:512 * (u0 + n):16], "ZM " + ge)
+                    add(i0, i1, T.ZM[:, 16 - k:144 - k], T.GE[:, 16 * i0 + k:16 * i1:16], "ZM " + ge)
+            named(s, "s%d" % u0)
             for k in range(16):
-                add(i0, i1, (T.Z8 if q == "s" else T.Z16)[:, 16 - k:144 - k], T.AB[:, 512 * u0 + k:512 * (u0 + n):16], "Z8 Z16 " + ab)
+                add(i0, i1, (T.Z8 if q == "s" else T.Z16)[:, 16 - k:144 - k], T.AB[:, 16 * i0 + k:16 * i1:16], "Z8 Z16 " + ab)
             if q == "v":
                 low(i0, i1)
-        for i0, i1 in ((0, CUT), (CUT, 256)):
-            if i1 > i0:
-                o, bk = keys(i0, i0 + 16)
-                mm(o, T.IDM[:], T.ZB[:], False, True, "IDM ZB", bk)
+        for j, i0 in enumerate((0, CUT)):
+            o, bk = keys(i0, i0 + 16)
+            named(s, "stop%d" % j)
+            mm(o, T.IDM[:], T.ZB[:], False, True, "IDM ZB", bk)
 
-    def keep_yh(t):
-        if t == NST - 1:
-            act(T.YH[:, t::8], T.LAND[:, 64 * t:64 * t + 64], F.Copy, "LAND%d" % t, "YH", 64)
-        else:
-            select(T.YH[:, t::8], T.LAND[:, 64 * t:64 * t + 64], [[0, 64]], 0, "LAND%d" % t, "YH", 64)
-
-    if X2_BY == "v":
-        cp(T.XW[:, 4096:8192], T.XW[:, 0:4096], "X1", "X2", 2048)
-        cp(T.XW[:, 8192:XA], T.XW[:, 0:XA - 8192], "X1", "X3a", 512)
-    else:
-        dma(T.XW[:, 4096:8192], T.xc[:], 1 << 20, wr="X2")
-        dma(T.XW[:, 8192:XA], T.xc[:, 0:XA - 8192], 1 << 18, wr="X3a")
-    dma(T.XW[:, XA:12288], T.xc[:, XA - 8192:4096], 3 << 18, wr="X3b")
-    own_lists(0, 1)
-    wrap(AAW, T.ZA, lambda il: T.AW[:, 16 * il:4096:256], "ZA", AWall)
-    cp(A16, AAW, "#M2", "A16")
-    at_v()
-    at_a()
-    own_lists(1, NST)
+    named(-9, "l0")
+    own_lists(0, LIST0)
+    named(-9, "l1")
+    own_lists(LIST0, NST)
+    rows(8, 1)
+    rows(2, 2)
+    at_v(-1)
+    at_a(-1)
     for h in range(4):
-        cp(T.RW[:, 1024 * h:1024 * h + 1024], T.RI[:, 1024 * h:1024 * h + 1024], "RI%d" % h, "RW", 1024)
-    trs = []
-    for t in range(NST):
-        select(T.PRES[:, 64 * t:64 * t + 64], T.RW[:, 8 + t:4096:64], [[0, 64]], 0, "RW", "PRES%d" % t, 64)
-        src = T.cores[(rank - 1 - t % (n_ranks - 1)) % n_ranks]
+        named(-9, "rw%d" % h)
+        a, b = T.RW[:, 1024 * h:1024 * h + 1024], T.RI[:, 1024 * h:1024 * h + 1024]
+        if RW_ON[h] == "v":
+            cp(a, b, "RI%d" % h, "RW%d" % h, 1024)
+        else:
+            select(a, b, [[0, 1024]], 0, "RI%d" % h, "RW%d" % h, 1024)
+    trs, n_eng = [], 0
+    named(-9, "pres")
+    for m in range(3):
+        for n in range(3):
+            b = 192 * m + 128 - 64 * n
+            select(T.PRES[:, b:b + 64], T.RI[:, 8 + m + 3 * n:4096:64], [[0, 64]], 0, units("RI", 0, 4), "PRES%d" % (m + 3 * n), 64)
+        src = T.cores[(rank - 1 - m) % n_ranks]
         rid, pid = topo.addr(src)[:2]
         e = topo.engines(core, src)
-        trs.append(RemoteDMATransfer(dst_ids=[DstId(rid=rid, pnc=pid)], dma_engine_mask=1 << e[t % len(e)], remote_sem=T.sem.pre,
-                                     src=T.PRES[:, 64 * t:64 * t + 64], dst=T.CB[:, CBW * t:CBW * t + 64]))
-    remote(lambda: g.remote_dma_fused(trs, local_sem=T.sem.sent), ["PRES%d" % t for t in range(NST)],
-           ["CB%d" % t for t in range(NST)], "pre", NST, 8.0, NST, False)
+        e = e[:len(e) // 2] if m == 0 else e[len(e) // 4 * (m + 1):len(e) // 4 * (m + 2)]
+        n_eng += len(e)
+        trs.append(RemoteDMATransfer(dst_ids=[DstId(rid=rid, pnc=pid)], dma_engine_mask=sum(1 << x for x in e), remote_sem=T.sem.pre,
+                                     src=T.PRES[:, 192 * m:192 * m + 192], dst=T.CB[:, CBW * m:CBW * m + 192]))
+    remote(lambda: g.remote_dma_fused(trs, local_sem=T.sem.sent), units("PRES", 0, 9).split(), units("CB", 0, NST).split(),
+           "pre", n_eng, PLAT, n_eng, False)
     for c in range(NB):
-        own_gather(c, OWN0 if c < 2 else OWN)
-    own_fold(0)
-    own_fold(1)
-    own_close(0)
+        own_gather(c)
+        own_max(c)
+    for c in range(DIRECT):
+        own_close(c)
+    own_gather(NB)
+    own_max(NB)
 
     for t in range(NST):
-        more = t < NST - 1
-        strict_pass()
-        act(T.IOG[:], T.SV[:].indirect(A16), F.Copy, SVall + " A16", "IOG", GA * 256)
+        more, s = t < NST - 1, t - 1
+        strict_pass(s)
         th = "th" if t == 0 else "thb"
         for j, (i0, i1) in enumerate(((0, CUT), (CUT, 256))):
-            if i1 > i0:
-                o, bk = keys(i0, i1)
-                tt(T.MN[:, i0:i1], o, T.DM[:, i0:i1], A.min, bk + " DM", "MN%d" % j, i1 - i0)
-                ts(T.IND[:, i0:i1], T.MN[:, i0:i1], col(th), None, A.is_lt, None, "MN%d c_%s" % (j, th), "IND%d" % j, i1 - i0)
+            o, bk = keys(i0, i1)
+            named(s, "MN%d" % j)
+            tt(T.MN[:, i0:i1], o, T.DM[:, i0:i1], A.min, bk + " DM", "MN%d" % j, i1 - i0)
+            named(s, "IND%d" % j)
+            ts(T.IND[:, i0:i1], T.MN[:, i0:i1], col(th), None, A.is_lt, None, "MN%d c_%s" % (j, th), "IND%d" % j, i1 - i0)
+        named(s, "FV")
         ts(T.FV[:], T.MN[:], 4095, None, A.bitwise_and, None, "MN0 MN1", "FV", 256)
-        wrap(CNT, T.Z1, lambda il: T.IND[:, il::16], "Z1", "IND0 IND1")
+        if not more:
+            for r in range(16):
+                named(s, "k%d" % min(r // 4, 2))
+                mm(T.KO[:, 0:256], T.ZA[:, 16 - r:144 - r], T.AW[:, 256 * r:256 * r + 256], r == 0, r == 15, "ZA " + AWall, "#KO", 256)
+            named(s, "y3")
+            act(T.Y3[:], T.KO[:, 0:256], F.Copy, "#KO", "Y3", 256)
+            act(T.YN[:], T.Y3[:, :, 0:8], F.Copy, "Y3", "YN", 128)
+        named(s, "FW")
+        wrap(CNT, T.Z1, lambda r: T.IND[:, r::16], "Z1", "IND0 IND1")
         ts(T.FW[:], CNT, 7.5, None, A.is_gt, None, "#M2", "FW")
+        named(s, "NF")
         ts(T.NF[:], CNT, 7.5, 4096.0, A.is_lt, A.mult, "#M2", "NF")
-        mm(TOT, T.BLK[:], T.FW[:], True, True, "BLK FW", "#M2")
-        mm(TRI_, T.TRI[:], T.FW[:], True, True, "TRI FW", "#M2")
+        named(s, "SC")
+        op("v", lambda: g.vector.tensor_tensor_scan(T.SC[:], T.FW[:], T.M1[:], col("s0"), A.add, A.add), "FW M1 c_s0", "SC", FIX + 16 * CYC)
+        mm(ROW, T.TRI[:], T.SC[:, 15:16], True, True, "TRI SC", "#M2")
         if more:
-            mm(FITS, T.ALL1[:, 0:128], T.FW[:], True, True, "ALL1 FW", "#M2")
-        tt(T.GD[:], T.NF[:], T.KD[:], A.mult, "NF KD", "GD")
-        op("v", lambda: g.vector.tensor_tensor_scan(T.SC[:, 1:17], TOT, T.ZERO[:], 0.0, A.add, A.add), "#M2 ZERO SC", "SC", FIX + 16 * CYC)
-        tt(T.P1[:], TRI_, T.GD[:], A.add, "#M2 GD", "P1")
-        tt(T.C16[:], T.P1[:], T.SC[:, 0:16], A.add, "P1 SC", "C16")
-        cp(T.CB[:, CBW * t:CBW * t + CBW].indirect(T.C16[:]), T.FV[:], "C16 FV CB%d" % t, "CB%d" % t, SC_ * 256)
+            mm(TOT, T.ALL1[:, 0:128], T.SC[:, 15:16], True, True, "ALL1 SC", "#M2")
+        named(s, "GD")
+        tt(T.GD[:], T.FW[:], T.KD[:], A.mult, "FW KD", "GD")
+        named(s, "P1")
+        tt(T.P1[:], T.GD[:], T.SC[:], A.add, "GD SC", "P1")
+        named(s, "D16")
+        tt(T.D16[:], T.V16[:], T.NF[:], A.add, "V16 NF", "D16")
+        named(s, "V16")
+        tt(T.V16[:] if more else T.YV[:], T.V16[:], T.FW[:], A.add, "V16 FW", "V16" if more else "YV")
+        named(s, "C16")
+        ts(T.C16[:], T.P1[:], ROW, col("s2"), A.add, A.add, "P1 c_s2 #M2", "C16")
+        named(s, "CB")
+        b = CBW * (t % 3) + 128 - 64 * (t // 3)
+        cp(T.CB[:, b:b + 320].indirect(T.C16[:]), T.FV[:], "C16 FV CB%d" % t, " ".join("CB%d" % x for x in range(t, -1, -3)), SC_ * 256)
         dst = T.cores[(rank + 1 + t % (n_ranks - 1)) % n_ranks]
         rid, pid = topo.addr(dst)[:2]
-        remote(lambda t=t, pid=pid, rid=rid, dst=dst: g.remote_dma(
-            T.LAND[:, 64 * t:64 * t + 64], T.CB[:, CBW * t:CBW * t + 64], T.sem["arr%d" % t], T.sem.sent, pid, rid, topo.mask(core, dst)),
-            ["CB%d" % t], ["LAND%d" % t], "arr%d" % t, len(topo.engines(core, dst)), RLAT - 0.6, len(topo.engines(core, dst)), False)
-        tt(T.D16[:], T.V16[:], T.NF[:], A.add, "V16 NF", "D16")
-        tt(T.V16[:], T.V16[:], T.FW[:], A.add, "V16 FW", "V16")
+        n_eng = len(topo.engines(core, dst))
+        named(t, "write")
+        remote(lambda t=t, b=b, pid=pid, rid=rid, dst=dst: g.remote_dma(
+            T.LAND[:, 64 * t:64 * t + 64], T.CB[:, b:b + 64], T.sem["arr%d" % t], T.sem["out%d" % t], pid, rid, topo.mask(core, dst)),
+            ["CB%d" % t], ["LAND%d" % t], "arr%d" % t, n_eng, RLAT - RCALL, n_eng, False, "out%d" % t)
+        named(t, "RW" if more else "BI")
+        cp(T.RW[:].indirect(T.D16[:]), T.FV[:], "D16 FV", RWall, SC_ * 256)
+        named(t, "MA")
         tt(T.MA[:], T.FW[:], T.DA[:], A.mult, "FW DA", "MA")
-        tt(A16, T.MA[:], T.AAS[:, 0:16], A.add, "MA AAS", "A16")
-        cp(T.RW[:].indirect(T.D16[:]), T.FV[:], "D16 FV", "RW", SC_ * 256)
-        cp(T.AW[:].indirect(T.D16[:]), T.IOG[:], "D16 IOG", AWall, SC_ * 256)
+        named(t, "A16")
+        tt(A16 if more else T.YA[:], T.MA[:], T.AAS[:, 0:16], A.add, "MA AAS", "A16" if more else "YA")
         if more:
+            named(t, "AW")
+            cp(T.AW[:].indirect(T.D16[:]), T.IOG[:], "D16 IOG", AWall, SC_ * 256)
+            named(t, "V1")
             tt(V1, V1, T.FW[:], A.add, "V1 FW", "V1")
-            act(T.JK[:], FITS, F.Copy, "#M2", "JK c_bs", accum_out=col("bs"))
-            cp(T.BI[:], col("bs"), "c_bs", "BI")
+            named(t, "BI")
+            cp(T.BI[:], TOT, "#M2", "BI")
+            named(t, "BI2")
             ts(T.BI2[:], T.BI[:], 255, None, A.bitwise_and, None, "BI", "BI2")
+            named(t, "thb")
             ts(col("thb"), T.BI2[:], 8192.0, col("th"), A.mult, A.add, "BI2 c_th", "c_thb")
-            at_v()
-            at_a()
-            if t + NB < NST:
-                own_gather(t + NB, OWN)
-            if t + 2 < NST:
-                own_fold(t + 2)
-            own_close(t + 1)
-            cp(T.RW[:, 8 + t:4096:64], T.LAND[:, 64 * t:64 * t + 64], "LAND%d" % t, "RW", 64)
-        keep_yh(t)
-
-    dma(T.yh[:], T.YH[:], 1 << 18, rd="YH")
-    for s in range(4):
-        o, wk = T["W%d" % (s // 2)][:, 512 * (s % 2):512 * (s % 2) + 256], "#W%d" % s
-        act(o, T.RW[:, 4 + s:4096:16], F.Copy, "RW", wk, 256, scale=4096.0)
-        tt(T.KOT[:, s:1024:4], o, T.RW[:, s:4096:16], A.add, "RW KOT " + wk, "YR%d" % s, 256)
-    dma(T.yr[:], T.KOT[:, 0:1024], 1 << 19, rd="YR0 YR1 YR2 YR3")
-    act(T.IOG[:], T.SV[:].indirect(A16), F.Copy, SVall + " A16", "IOG", GA * 256)
-    cp(T.AG[:, 0:256], T.SV[:].indirect(T.V16[:]), SVall + " V16", "AG", GA * 256)
-    mm(T.KO[:, 0:256], T.SVA[:], T.AG[:, 0:256], True, True, "SVA AG", "#KO", 256)
-    mm(T.KO[:, 256:512], T.SVA[:], T.IOG[:], True, True, "SVA IOG", "#KO", 256)
-    act(T.YVA[:], T.KO[:], F.Copy, "#KO", "YVA", 512)
-    for s in range(8):
-        o, wk = T["W%d" % (s // 2 % 2)][:, 512 * (s % 2):512 * (s % 2) + 256], "#W%d" % (s % 4)
-        mm(o, T.SVA[:], T.AW[:, s:4096:16], True, True, "SVA " + AWall, wk, 256)
-        if s % 2:
-            act(T.KOT[:, 2048 + s::8], o, F.Copy, wk, "YAN%d" % s, 256)
+            at_v(t)
+            at_a(t)
+            if t + 1 >= DIRECT:
+                own_close(t + 1)
+            if t + NB + 1 < NST:
+                own_gather(t + NB + 1)
+                own_max(t + NB + 1)
+            named(t, "merge")
+            cp(T.RW[:, 8 + t:4096:64], T.LAND[:, 64 * t:64 * t + 64], "LAND%d" % t, RWall, 64)
+            named(t, "yh")
+            select(T.YH[:, t::8], T.LAND[:, 64 * t:64 * t + 64], [[0, 64]], 0, "LAND%d" % t, "YH", 64)
         else:
-            cp(T.KOT[:, 2048 + s::8], o, wk, "YAN%d" % s, 256)
-    dma(T.yan[:], T.KOT[0::16, 2048:4096], 1 << 16, rd=" ".join("YAN%d" % s for s in range(8)))
-    dma(T.yv[:], T.YVA[0::16, 0:256], 1 << 13, rd="YVA")
-    dma(T.ya[:], T.YVA[0::16, 256:512], 1 << 13, rd="YVA")
+            named(t)
+            act(T.YH[:, t::8], T.LAND[:, 64 * t:64 * t + 64], F.Copy, "LAND%d" % t, "YH", 64)
+        if t == NST - 2:
+            named(t, "p2")
+            cp(T.P2[:, 0:16], A16, "A16", "PA")
+            cp(T.P2[:, 16:32], T.V16[:], "V16", "PV")
+            named(t, "y2")
+            tt(T.Y2[:], T.P2[:, 16:32].indirect(T.EX[:]), T.XC[:], A.is_equal, "PV EX XC", "Y2", GA * 128)
+
+    named(NST - 1, "UC")
+    dma("yh_", T.yh[:], T.YH[:], 1 << 18, rd="YH")
+    dma("yv_", T.yv[:], T.YV[:], 1 << 13, rd="YV")
+    dma("ya_", T.ya[:], T.YA[:], 1 << 13, rd="YA")
+    for s in range(4):
+        o, wk = T.PW[:, 512 * s:512 * s + 256], "#W%d" % s
+        act(o, T.RW[:, 4 + s:4096:16], F.Copy, RWall, wk, 256, scale=4096.0)
+        tt(T.KOT[:, s:1024:4], o, T.RW[:, s:4096:16], A.add, RWall + " KOT " + wk, "YR%d" % s, 256)
+    dma("yr_", T.yr[:], T.KOT[:, 0:1024], 1 << 19, rd=units("YR", 0, 4))
+    named(NST - 1, "UG")
+    tt(T.Y1[:], T.P2[:, 0:16].indirect(T.EX[:]), T.YN[:], A.subtract, "PA EX YN", "Y1", GA * 128)
+    tt(T.Y2[:], T.FW[:].indirect(T.EX[:]), T.Y2[:], A.mult, "FW EX Y2", "Y2", GA * 128)
+    tt(T.Y1[:], T.Y1[:], T.Y2[:], A.mult, "Y1 Y2", "Y1", 256)
+    tt(T.YN[:], T.YN[:], T.Y1[:], A.add, "YN Y1", "YN", 256)
+    dma("yan_", T.yan[:], T.YN[:], 1 << 16, rd="YN")
 
     for j in issue_order(tasks):
-        tasks[j][5]()
+        if tasks[j][5]:
+            tasks[j][5]()
     count["sent"] = sent[0]
     for s in count:
         if seen["g"].get(s, 0) < count[s]:

from concourse.bass import DstId, RemoteDMATransfer
from concourse.mybir import AluOpType as A, ActivationFunctionType as F

NST = 8
NEG = -255.0 * 65536.0
CBW = 448
XA = 9216
HEAVY = (("s", 0, 2, None), ("v", 2, 2, None), ("v", 2, 2, 2), ("s", 6, 1, None), ("s", 0, 2, 0), ("v", 4, 2, None), ("s", 7, 1, None),
         ("s", 6, 1, 2), ("v", 4, 2, 3), ("s", 7, 1, 5))
SUMS = ((0, 2), (2, 2), (4, 2), (6, 2))
CUT, PLACES = 192, (0, 128, 256)
OWN = ((2, "v", 4), (1, "v", 4), (1, "s", 4)) + ((2, "s", 4),) * 4 + ((2, "s", 3),) * 2
OWN0 = ("svsv", "sssv", "ssvv")
CLOSE = ((5, 2), (6, 2), (8, 2), (13, 1))
DIRECT, FOLD0, AHEAD, NB = 1, 2, 3, 3
FOLD, QW = ((0, 2, 1280), (2560, 1, 1536)), 1536
LIST0 = 2
X2_ON, RW_ON = "y", "gggg"
ORDER = {
    "v": "l0 o0_1 o0_3 o1_3 l1 uc0 m13 eqm m12 m10 m11 o2_3 o2_2 "
         "MA BI A16 V1 AW UC RW UG p2 merge TA0 TA1 TB0 TB1 PL0 PL1 g2 BI2 a2 g4 thb a4 DM o0 y2 MN0 IND0 MN1 IND1 FV DA o1 "
         "FW NF SC D16 GD P1 V16 C16 CB",
    "s": "WI X1 TI X3a o0_0 o0_2 o1_0 o1_2 d00 d01 qt0 o1_1 d02 ag0 d03 iog0 o2_1 kot0 o2_0 "
         "o7 QT AG o8 kot TA0 TA1 IOG AAS g0 NEQ g6 a0 g7 a6 a7 o2 o3 o4 o5 o6 QG y3 yh_ yan_",
    "p": "l0 l1 d00 m1 d01 d02 e00 d03 e01 e02 e03 "
         "u k3 kot ZA q0 q1 q2 q3 NEQ open0 q7 q5 n0 n1 x2 open1 q4 q6 n6 s2 s0 n7 x4 s4 stop0 s6 stop1 k0 FW k1 SC k2",
    "g": "iota XL sel0 idm sel tri rw0 rw1 rw2 rw3 pres Q2 f21 f20 write Q3 fold0 fold1 yh Q",
    "y": "AR0 AR1 AW0 AW1 X2 RI0 RI1 X3b AW8 AW9 AW2 AW3 yv_ ya_ yr_",
    "e": "AR0 WI X1 AR1 TI AW0 AW1 X2 RI0 RI1 X3b AW8 AW9 AW2 AW3",
}
PARK = (("XW", 0), ("XW", 4096), ("XW", 8192), ("AW", 0), ("AW", 4096), ("AB", 0), ("GE", 0), ("GO0", 0))
CYC, FIX, PCY, HOP, GA, SC_ = 0.83e-3, 0.065, 0.417e-3, 0.15, 1.56, 3.0
DQ, DFIX, DROW, DBW = 0.5, 1.8, 0.2, 600e3
RCALL, RLAT, PLAT, FLAT, ROUNDS = 0.6, 2.6, 10.0, (14.0, 12.0), 3

SCRATCH = {}
for _n, _s, _d in (
        ("XW", 12288, "bfloat16"), ("RI", 4096, "int32"), ("RW", 8192, "float32"), ("AW", 8192, "bfloat16"), ("SEL", 2048, "bfloat16"),
        ("KOT", 4096, "float32"), ("CB", 3 * CBW, "float32"), ("LAND", NST * 64, "float32"), ("PRES", 576, "float32"),
        ("GE", 4096, "bfloat16"), ("AB", 4096, "bfloat16"), ("GO0", 4096, "bfloat16"), ("GO1", 4096, "bfloat16"), ("GO2", 4096, "bfloat16"),
        ("MX0", 4096, "bfloat16"), ("MX1", 4096, "bfloat16"), ("MX2", 4096, "bfloat16"),
        ("QR0", 1536, "bfloat16"), ("QR1", 1536, "bfloat16"), ("QR2", 1536, "bfloat16"),
        ("AR", 512, "int32"), ("ARB", 1536, "bfloat16"), ("ZB", 16, "bfloat16"),
        ("WI", 1, "int32"), ("TI", 1, "int32"), ("PI", 1, "int32"), ("PGI", 1, "int32"), ("PKI", 1, "int32"), ("PK2", 1, "int32"),
        ("KCI", 1, "int32"), ("KCM", 1, "int32"), ("KCH", 1, "bfloat16"), ("BI", 1, "int32"), ("BI2", 1, "int32"), ("COL", 32, "float32"),
        ("CI", 144, "int32"), ("MG", 128, "int32"), ("T2", 128, "float32"), ("ALL1", 256, "bfloat16"),
        ("Z1", 144, "bfloat16"), ("Z8", 144, "bfloat16"), ("Z16", 144, "bfloat16"), ("ZM", 144, "bfloat16"),
        ("ZA", 144, "bfloat16"), ("ZR", 144, "bfloat16"), ("ZW", 144, "bfloat16"), ("ZK", 128, "bfloat16"),
        ("IDM", 128, "bfloat16"), ("NID", 128, "bfloat16"), ("DNG", 128, "bfloat16"), ("DKH", 128, "bfloat16"), ("DKL", 128, "bfloat16"),
        ("EQM", 128, "float32"), ("DNM", 128, "float32"), ("MVA", 128, "bfloat16"), ("MVV", 128, "bfloat16"),
        ("BLK", 128, "bfloat16"), ("BM", 128, "bfloat16"), ("WM", 128, "bfloat16"), ("SVK", 128, "bfloat16"), ("TRI", 128, "bfloat16"),
        ("VI", 16, "int32"), ("KI", 16, "int32"), ("KD", 16, "float32"), ("M1", 16, "float32"), ("SC", 16, "bfloat16"),
        ("AAS", 32, "float32"), ("DA", 16, "float32"), ("MA", 16, "float32"),
        ("FW", 16, "bfloat16"), ("NF", 16, "float32"), ("GD", 16, "float32"), ("P1", 16, "float32"),
        ("AV", 32, "uint16"), ("V16", 16, "uint16"), ("D16", 16, "uint16"), ("C16", 16, "uint16"),
        ("QG", 256, "bfloat16"), ("QT", 256, "bfloat16"), ("AG", 512, "bfloat16"), ("IOG", 256, "bfloat16"),
        ("EK", 256, "float32"), ("UG", 256, "int32"), ("TA", 256, "int32"), ("TB", 256, "int32"), ("UC", 256, "int32"),
        ("PLE", 256, "uint16"), ("OU", 128, "int32"), ("OA", 128, "int32"), ("OB", 128, "int32"),
        ("NEQ", 256, "float32"), ("DM", 256, "float32"), ("MN", 256, "int32"), ("IND", 256, "bfloat16"), ("FV", 256, "int32"),
        ("XI", 128, "int32"), ("XC", 128, "float32"), ("EX", 8, "uint16"), ("P2", 32, "float32"), ("Y1", 128, "float32"),
        ("Y2", 128, "float32"), ("YH", 512, "float32"), ("YV", 16, "float32"), ("YA", 16, "float32"), ("YN", 128, "float32")):
    SCRATCH[_n] = ("sbuf", [128, _s], _d)
SCRATCH["PLO"] = ("sbuf", [128, NST, 256], "uint16")
SCRATCH["Y3"] = ("sbuf", [128, 16, 16], "float32")
for _n, _s in (("PW", 2560), ("KE", 512), ("KO", 512), ("M2", 512)):
    SCRATCH[_n] = ("psum", [128, _s], "float32")
SEMAPHORES = ["qv", "qs", "qp", "qg", "pre", "sent"] + ["%s%d" % (n, t) for n in ("arr", "out") for t in range(NST)]
SEMAPHORES += ["d%d" % i for i in range(24)] + ["%s%d_%d" % (n, c, f) for n in ("hf", "mx") for c in range(NST) for f in range(2)]


def issue_order(tasks):
    last, readers, preds = {}, {}, []
    for j, (q, rd, wr, cost, lat, emit, tag) in enumerate(tasks):
        p = [last[k] for k in rd + wr if k in last] + [i for k in wr for i in readers.get(k, ())]
        p += [i for k in rd if k[0] == "#" for i in readers.get(k, ()) if tasks[i][0] != q]
        preds.append({i: 0.0 if q == "p" == tasks[i][0] else HOP + tasks[i][4] for i in p if i != j})
        for k in wr:
            last[k], readers[k] = j, []
        for k in rd:
            readers.setdefault(k, []).append(j)
    every = range(len(tasks))
    for q, names in ORDER.items():
        names = names.split()
        row = sorted((t[6][0], names.index(t[6][1]), j) for j, t in enumerate(tasks) if t[0] == q and t[6][1] in names)
        for a, b in zip(row, row[1:]):
            preds[b[2]].setdefault(a[2], 0.0)
    back = [{} for j in every]
    for j in every:
        for i, h in preds[j].items():
            back[i][j] = h
    way, left = [0.0] * len(tasks), [len(b) for b in back]
    ready = [j for j in every if not left[j]]
    for j in ready:
        way[j] = tasks[j][3] + max([tasks[j][4]] + [h + way[k] for k, h in back[j].items()])
        for i in preds[j]:
            left[i] -= 1
            if not left[i]:
                ready.append(i)
    assert len(ready) == len(tasks)

    def lay(order, edges, tail):
        end, taken = {}, {}
        for j in order:
            q, cost = tasks[j][0], tasks[j][3]
            t = max([end[i] + h for i, h in edges[j].items()] + [tasks[j][4] if tail else 0.0])
            slots = taken.setdefault(q, [])
            n = len(slots)
            while n and slots[n - 1][1] > t:
                n -= 1
            while n < len(slots) and slots[n][0] < t + cost - 1e-9:
                t = max(t, slots[n][1])
                n += 1
            slots.insert(n, (t, t + cost))
            end[j] = t + cost
        return end, max(end[j] + (0.0 if tail else tasks[j][4]) for j in every)

    end, span = lay(sorted(every, key=lambda j: (-way[j], j)), preds, False)
    best = (span, end)
    for _ in range(ROUNDS):
        late = lay(sorted(every, key=lambda j: (-end[j], -j)), back, True)[0]
        end, span = lay(sorted(every, key=lambda j: (-late[j], j)), preds, False)
        if span < best[0]:
            best = (span, end)
    end = best[1]
    return sorted(every, key=lambda j: (end[j] - tasks[j][3], j))


def helper(core, T, topo):
    return [c for c in topo.cores_of(core) if c not in T.cores and topo.die(c) == topo.die(core)][0]


def fold_engines(owner, mate, T, topo):
    off_chip = set(e for other in T.cores if other != owner for e in topo.engines(owner, other))
    return [[e for e in topo.engines(owner, mate) if (e in off_chip) == side] for side in (False, True)]


def back_engines(mate, owner, topo):
    e = topo.engines(mate, owner)
    return e[:len(e) // 2]


def hand_back(g, core, owner, T, topo):
    rid, pid = topo.addr(owner)[:2]
    sets, back, n = fold_engines(owner, core, T, topo), back_engines(core, owner, topo), 0
    for c in range(FOLD0, NST):
        name, c0 = PARK[c]
        for f, (b, per, w) in sorted(enumerate(FOLD), key=lambda x: x[1][1] * x[1][2]):
            g.wait_ge(T.sem["hf%d_%d" % (c, f)], len(sets[f]))
            g.remote_dma(T["MX%d" % (c % NB)][:, b:b + per * w], T[name][:, c0 + b:c0 + b + per * w], T.sem["mx%d_%d" % (c, f)],
                         T.sem.sent, pid, rid, sum(1 << e for e in back))
            n += len(back)
    g.wait_ge(T.sem.sent, n)


def rank_program(g, core, T, topo):
    rank = T.rank_of(core)
    if rank is None:
        for other in T.cores:
            if helper(other, T, topo) == core:
                hand_back(g, core, other, T, topo)
        return
    n_ranks = len(T.cores)
    queue = {"v": g.vector, "s": g.scalar, "p": g.tensor, "g": g, "y": g.sync}
    tasks = []
    seen = {q: {} for q in queue}
    count = {}
    last, readers = {}, {}
    tag, dmas, sent, ncol = [(-9, "")], [0], [0], {}

    def named(w, name=""):
        tag[0] = (w, name)

    def need(q, tok):
        s, n, clock = tok
        if seen[q].get(s, 0) < n:
            queue[q].wait_ge(T.sem[s], n)
            for k, x in clock.items():
                seen[q][k] = max(seen[q].get(k, 0), x)
            seen[q][s] = n

    def before(q, own, rd, wr):
        for k in rd:
            if k in last and (q != "p" or last[k][0] != own):
                need(q, last[k])
            if k[0] == "#":
                for s, tok in readers.get(k, {}).items():
                    if s != own:
                        need(q, tok)
        for k in wr:
            if k in last and (q != "p" or last[k][0] != own):
                need(q, last[k])
            for s, tok in readers.get(k, {}).items():
                if q != "p" or s != own:
                    need(q, tok)

    def after(tok, rd, wr):
        for k in wr:
            last[k] = tok
            readers[k] = {}
        for k in rd:
            readers.setdefault(k, {})[tok[0]] = tok

    def op(q, call, rd, wr, cost):
        rd, wr, own = rd.split(), wr.split(), "q" + q

        def emit():
            before(q, own, rd, wr)
            call().then_inc(T.sem[own], 1)
            count[own] = count.get(own, 0) + 1
            after((own, count[own], dict(seen[q])), rd, wr)
        tasks.append((q, rd, wr, cost, 0.1 if q == "p" else 0.0, emit, tag[0]))

    def dma(name, out, in_, nbytes, rd="", wr=""):
        rd, wr = rd.split(), wr.split()
        s, q = "d%d" % dmas[0], "s" if name in ORDER["s"].split() else "y"
        dmas[0] += 1

        def emit():
            before(q, s, rd, wr)
            queue[q].dma_start(out, in_).then_inc(T.sem[s], 16)
            count[s] = 16
            after((s, 16, dict(seen[q])), rd, wr)
        tasks.append((q, rd, wr + [s], DQ, DFIX - DQ, emit, (tag[0][0], name)))
        tasks.append(("e", rd + [s], wr, DROW + nbytes / DBW, 0.0, None, (tag[0][0], name)))

    def remote(call, rd, wr, sem, n, lat, n_sent, back=True, left=None):
        def emit():
            before("g", "x", rd, wr if back else [])
            call()
            if left:
                after((left, n_sent, dict(seen["g"])), rd, [])
                count[left] = n_sent
            else:
                sent[0] += n_sent
            after((sem, n, dict(seen["g"]) if back else {}), rd if back else [], wr)
            count[sem] = n
        tasks.append(("g", rd, wr, RCALL, lat, emit, tag[0]))

    def mm(out, lhs, rhs, start, stop, rd, wr, cy=64):
        op("p", lambda: g.tensor.matmul(out, lhs, rhs, start, stop), rd, wr, cy * PCY)

    def col(name):
        if name not in ncol:
            ncol[name] = len(ncol)
        return T.COL[:, ncol[name]:ncol[name] + 1]

    def ts(out, in0, s1, s2, o0, o1, rd, wr, cy=16):
        args = (out, in0, s1, s2, o0) if o1 is None else (out, in0, s1, s2, o0, o1)
        op("v", lambda: g.vector.tensor_scalar(*args), rd, wr, FIX + cy * CYC)

    def tt(out, a, b, o, rd, wr, cy=16):
        op("v", lambda: g.vector.tensor_tensor(out, a, b, o), rd, wr, FIX + cy * CYC)

    def cp(out, in_, rd, wr, cy=16):
        op("v", lambda: g.vector.tensor_copy(out, in_), rd, wr, FIX + cy * CYC)

    def fill(out, x, wr, cy=16):
        op("v", lambda: g.vector.memset(out, x), "", wr, FIX + cy * CYC)

    def act(out, in_, f, rd, wr, cy=16, **kw):
        op("s", lambda: g.scalar.activation(out, in_, f, **kw), rd, wr, FIX + cy * CYC)

    def copy(q, out, in_, rd, wr, cy=16):
        if q == "v":
            cp(out, in_, rd, wr, cy)
        else:
            act(out, in_, F.Copy, rd, wr, cy)

    def iota(out, pattern, base, mult, wr, n, **kw):
        op("g", lambda: g.iota(out, pattern, base, mult, **kw), "", wr, 0.13 + 2 * n * CYC)

    def select(out, in_, pattern, mult, rd, wr, n, test=A.is_equal):
        op("g", lambda: g.affine_select(out, in_, pattern, test, 0.0, 0, mult), rd, wr, 0.17 + 2 * n * CYC)

    def wrap(o, Z, src, zk, sk, bank="#M2"):
        for r in range(16):
            mm(o, Z[:, 16 - r:144 - r], src(r), r == 0, r == 15, zk + " " + sk, bank)

    AWall, RWall = "AW0 AW1 AW2 AW3 AW8 AW9", "RW0 RW1 RW2 RW3"
    Xown, Xall = "X1 X2 X3a", "X1 X2 X3a X3b"
    A16, V1 = T.AV[:, 0:16], T.AV[:, 16:32]

    dma("AR0", T.AR[:, 0:256], T.rf[0::16, :], 1 << 17, wr="AR0")
    dma("AR1", T.AR[:, 256:512], T.an[:, :], 1 << 17, wr="AR1")
    dma("WI", T.WI[:], T.w[:], 512, wr="WI")
    dma("TI", T.TI[:], T.th[:], 512, wr="TI")
    dma("X1", T.XW[:, 0:4096], T.xc[:], 1 << 20, wr="X1")
    for h in range(2):
        dma("RI%d" % h, T.RI[:, 2048 * h:2048 * h + 2048], T.rf[:, 2048 * h:2048 * h + 2048], 1 << 20, wr="RI%d RI%d" % (2 * h, 2 * h + 1))
    named(-9, "X2")
    if X2_ON == "y":
        dma("X2", T.XW[:, 4096:8192], T.xc[:], 1 << 20, wr="X2")
    else:
        act(T.XW[:, 4096:8192], T.XW[:, 0:4096], F.Copy, "X1", "X2", 4096)
    named(-9, "X3a")
    act(T.XW[:, 8192:XA], T.XW[:, 0:XA - 8192], F.Copy, "X1", "X3a", 1024)
    dma("X3b", T.XW[:, XA:12288], T.xc[:, XA - 8192:4096], 3 << 18, wr="X3b")
    named(-9, "iota")
    iota(T.PI[:], [[0, 1]], 0, 1, "PI", 1)
    iota(T.CI[:], [[1, 144]], 0, 0, "CI", 144)
    iota(T.VI[:], [[16, 16]], 0, 256, "VI", 16)
    iota(T.KI[:], [[1, 16]], -320, 16, "KI", 16)
    named(-9, "XL")
    iota(T.ARB[:, 1280:1536], [[1, 256]], 0, 0, "L2", 256, allow_small_or_imprecise_dtypes=True)
    named(-9, "sel0")
    iota(T.SEL[:], [[-1, 128], [0, 16]], 1, 1, "SEL", 2048, allow_small_or_imprecise_dtypes=True)
    named(-9, "sel")
    select(T.SEL[:], T.SEL[:], [[-1, 128], [0, 16]], 1, "SEL", "SEL", 2048)
    named(-9)
    fill(T.AW[:, 0:4096], 1.0, AWall, 2048)
    for j in range(2):
        a, b = 256 * j, 256 * j + 256
        cp(T.ARB[:, a:b], T.AR[:, a:b], "AR%d" % j, "H%d" % j, 256)
        tt(T.ARB[:, 768 + a:768 + b], T.AR[:, a:b], T.ARB[:, a:b], A.subtract, "AR%d H%d" % (j, j), "L%d" % j, 512)

    def rows(row, j, shift=0):
        for h in range(2):
            dma("AW%d" % (row + h), T.AW[row + h::16, shift:4096 + shift], T.ARB[:, 768 * h + 256 * j:768 * h + 256 * j + 256], 1 << 16,
                rd="HL"[h] + str(j), wr="AW%d LD%d" % (row + h, row + h))

    rows(0, 0, 1)

    cp(col("p"), T.PI[:], "PI", "c_p")
    ts(T.PGI[:], T.PI[:], 112, None, A.bitwise_and, None, "PI", "PGI")
    ts(T.PKI[:], T.PI[:], 15, None, A.bitwise_and, None, "PI", "PKI")
    ts(T.PK2[:], T.PI[:], 1, 7, A.arith_shift_right, A.bitwise_and, "PI", "PK2")
    ts(T.MG[:], T.CI[:, 0:128], 112, None, A.bitwise_and, None, "CI", "MG", 128)
    cp(col("pg"), T.PGI[:], "PGI", "c_pg")
    ts(col("pg16"), T.PGI[:], 16.0, None, A.add, None, "PGI", "c_pg16")
    ts(col("pgx"), T.PGI[:], 16.0, None, A.mult, None, "PGI", "c_pgx")
    ts(col("pgy"), T.PGI[:], 256.0, None, A.mult, None, "PGI", "c_pgy")
    ts(col("k256"), T.PKI[:], 256.0, None, A.mult, None, "PKI", "c_k256")
    fill(T.ALL1[:], 1.0, "ALL1", 128)
    act(T.ARB[:, 512:768], T.ALL1[:], F.Copy, "ALL1 c_k256", "H2", 256, scale=col("k256"))
    for name, pair in (("kr", 0), ("kx", 1), ("ka", 4)):
        ts(col(name), T.PK2[:], float(pair), None, A.is_equal, None, "PK2", "c_" + name)
    ts(col("k4"), T.PKI[:], 4.0, NEG, A.is_equal, A.mult, "PKI", "c_k4")
    ts(col("k5"), T.PKI[:], 5.0, 4096.0, A.is_equal, A.mult, "PKI", "c_k5")
    ts(col("nk"), T.PKI[:], 0.0, None, A.is_gt, None, "PKI", "c_nk")
    ts(col("kk"), col("kr"), col("k4"), col("k5"), A.add, A.add, "c_kr c_k4 c_k5", "c_kk")
    ts(col("k4n"), T.PKI[:], 4.0, -1.0, A.is_equal, A.mult, "PKI", "c_k4n")
    tt(col("pm"), col("p"), col("k4n"), A.add, "c_p c_k4n", "c_pm")
    tt(col("kv"), col("kx"), col("k4n"), A.add, "c_kx c_k4n", "c_kv")
    ts(col("p6"), T.PI[:], 6.0, None, A.add, None, "PI", "c_p6")
    ts(col("s0"), T.PKI[:], -16.0, 256.0, A.mult, A.add, "PKI", "c_s0")
    ts(col("s1"), T.PKI[:], 8.0, -248.0, A.mult, A.add, "PKI", "c_s1")
    ts(col("s2"), T.PKI[:], col("s1"), 64.0, A.mult, A.add, "c_s1 PKI", "c_s2")
    cp(col("w"), T.WI[:], "WI", "c_w")
    ts(col("th"), T.TI[:], 8192.0, NEG, A.mult, A.add, "TI", "c_th")
    ts(T.KCI[:], T.PKI[:], 613.0, None, A.mult, None, "PKI", "KCI")
    ts(T.KCM[:], T.KCI[:], 4095, None, A.bitwise_and, None, "KCI", "KCM")
    cp(col("kc"), T.KCM[:], "KCM", "c_kc")
    cp(T.KCH[:], T.KCM[:], "KCM", "KCH")
    ts(col("kq"), T.KCM[:], -33554432.0, None, A.mult, None, "KCM", "c_kq")
    tt(col("kl"), T.KCH[:], T.KCM[:], A.subtract, "KCH KCM", "c_kl")
    ts(col("kh"), T.KCH[:], -1.0, None, A.mult, None, "KCH", "c_kh")

    ts(T.Z1[:], T.CI[:], col("pg16"), None, A.is_equal, None, "CI c_pg16", "Z1", 144)
    ts(T.BLK[:], T.MG[:], col("pg"), None, A.is_equal, None, "MG c_pg", "BLK", 128)
    named(-9, "idm")
    select(T.IDM[:], T.ALL1[:, 0:128], [[-1, 128]], 1, "ALL1", "IDM", 128)
    named(-9, "tri")
    select(T.TRI[:], T.BLK[:], [[1, 128]], -1, "BLK", "TRI", 128, A.is_gt)
    for base, names in (("Z1", (("ZW", "w"), ("ZR", "kr"), ("ZA", "ka"), ("Z8", 8192.0), ("Z16", 16384.0), ("ZM", -8192.0))),
                        ("BLK", (("WM", "w"), ("SVK", "kk"), ("BM", -8192.0))),
                        ("IDM", (("NID", -1.0), ("DNG", NEG), ("DKH", "kh"), ("DKL", "kl"), ("DNM", "nk")))):
        for name, x in names:
            named(-9, name)
            if isinstance(x, float):
                act(T[name][:], T[base][:], F.Copy, base, name, 144, scale=x)
            else:
                act(T[name][:], T[base][:], F.Copy, base + " c_" + x, name, 144, scale=col(x))
    named(-9, "ZK")
    for j, (a, b, rd) in enumerate(((T.Z1[:, 12:140], T.DKH[:], "Z1 DKH"), (T.Z1[:, 11:139], T.DKL[:], "Z1 DKL"),
                                    (T.IDM[:], T.ZR[:, 16:144], "IDM ZR"))):
        mm(T.M2[:, 0:128], a, b, j == 0, j == 2, rd, "#M2", 128)
    act(T.ZK[:], T.M2[:, 0:128], F.Copy, "#M2", "ZK", 128)
    named(-9, "eqm")
    ts(T.T2[:], T.MG[:], col("p"), None, A.is_equal, None, "MG c_p", "T2", 128)
    tt(T.EQM[:], T.IDM[:], T.T2[:], A.subtract, "IDM T2", "EQM", 256)
    named(-9)
    fill(T.M1[:], -1.0, "M1")
    fill(T.ZB[:], 0.0, "ZB")
    ts(T.MVA[:], T.CI[:, 0:128], col("p6"), col("kx"), A.is_equal, A.mult, "CI c_p6 c_kx", "MVA", 128)
    ts(T.MVV[:], T.CI[:, 0:128], col("pm"), col("kv"), A.is_equal, A.mult, "CI c_pm c_kv", "MVV", 128)
    ts(T.KD[:], T.KI[:], col("pgx"), None, A.subtract, None, "KI c_pgx", "KD")
    ts(T.V16[:], T.VI[:], col("pgy"), None, A.subtract, None, "VI c_pgy", "V16")
    ts(V1, T.VI[:], col("pgy"), 1.0, A.subtract, A.add, "VI c_pgy", "V1")
    cp(A16, T.AR[:, 256:512:16], "AR1", "A16")
    named(NST - 4, "Q")
    iota(T.XI[:], [[16, 16], [1, 8]], 0, 256, "XI", 128)
    named(NST - 3, "p2")
    ts(T.XC[:], T.XI[:], col("pgy"), None, A.subtract, None, "XI c_pgy", "XC", 128)
    ts(col("k8"), T.PKI[:], 7.5, None, A.is_gt, None, "PKI", "c_k8")
    ts(T.EX[:], T.CI[:, 0:8], 2.0, col("k8"), A.mult, A.add, "CI c_k8", "EX")

    def wb(b, n=1):
        if b == 5:
            return T.KO[:], "#KO"
        return T.PW[:, 512 * b:512 * (b + n)], " ".join("#W%d" % (b + j) for j in range(n))

    def units(name, u0, n=1):
        return " ".join("%s%d" % (name, u) for u in range(u0, u0 + n))

    mate = helper(core, T, topo)
    mrid, mpid = topo.addr(mate)[:2]
    sets = fold_engines(core, mate, T, topo)

    def own_lists(c0, c1):
        P, z, bk = (T.KO, 0, "#KO") if c0 == 0 else (T.PW, 2048, "#W4")
        for Z in ("ZW", "ZR") if c0 == 0 else ("ZR", "ZW"):
            for c in range(c0, c1):
                if Z == "ZW":
                    wrap(P[:, z + 16 * c:z + 16 * c + 16], T.ZW, lambda r, c=c: T.XW[:, 16 * r + c:4096:256], "ZW", "X1", bk)
                else:
                    wrap(P[:, z + 128 + 16 * c:z + 144 + 16 * c], T.ZR, lambda r, c=c: T.AW[:, 16 * r + c + 1:4096:256], "ZR", AWall, bk)
        a, b, key = 16 * c0, 16 * c1, units("PLO", c0, c1 - c0)
        cp(T.OA[:, a:b], P[:, z + a:z + b], bk, "OA", b - a)
        ts(T.OU[:, a:b], T.OA[:, a:b], 4095, None, A.bitwise_and, None, "OA", "OU", b - a)
        tt(T.OA[:, a:b], P[:, z + 128 + a:z + 128 + b], T.OU[:, a:b], A.mult, bk + " OU", "OA", b - a)
        ts(T.OB[:, a:b], T.OA[:, a:b], 5, 4095, A.arith_shift_right, A.bitwise_and, "OA", "OB", b - a)
        tt(T.OA[:, a:b], P[:, z + 128 + a:z + 128 + b], T.OB[:, a:b], A.add, bk + " OB", "OA", b - a)
        ts(T.OB[:, a:b], T.OA[:, a:b], 4095, None, A.bitwise_and, None, "OA", "OB", b - a)
        cp(T.PLO[:, c0:c1, 0:16], T.OB[:, a:b], "OB", key, b - a)
        for n in (1, 2, 4, 8):
            ts(T.PLO[:, c0:c1, 16 * n:32 * n], T.PLO[:, c0:c1, 0:16 * n], float(613 * n % 4096), None, A.add, None, key, key, n * (b - a) // 2)

    def gk(c, k, n=1, name="G"):
        return units("%s%d_" % (name, c % NB), k, n)

    def total(k, Z, src, sk, first=False):
        mm(T.KO[:, 0:256], T[Z][:, 16 - k:144 - k], src, first, False, Z + " " + sk, "#KO", 256)

    def own_gather(c):
        G, k0 = T["GO%d" % (c % NB)], 0
        for j, (n, q, ahead) in enumerate(OWN if c >= NB else [(4, q, 0) for q in OWN0[c]]):
            named(*((c - ahead, "o%d" % j) if c >= NB else (-9, "o%d_%d" % (c, j))))
            copy(q, G[:, 256 * k0:256 * (k0 + n)], T.XW[:, 0:XA].indirect(T.PLO[:, c, 16 * k0:16 * (k0 + n)]), Xown + " PLO%d" % c,
                 gk(c, k0, n), GA * 256 * n)
            k0 += n

    def own_max(c):
        G, M, Q, qk = T["GO%d" % (c % NB)], T["MX%d" % (c % NB)], T["QR%d" % (c % NB)], []
        if c < DIRECT:
            return
        if c < FOLD0:
            w, wk = wb(4)
            named(-9, "m%d" % c)
            mm(w, T.IDM[:], T.XW[:, c:8192:16], True, True, "IDM X1 X2", wk, 512)
            for k in range(0, 16, 2):
                named(-9, "m%d%d" % (c, k // 4))
                tt(M[:, 256 * k:256 * k + 512], G[:, 256 * k:256 * k + 512], w, A.max, wk + " " + gk(c, k, 2), gk(c, k, 2, "MX"), 512)
            return
        named(*((c - AHEAD - 1, "Q") if c > NB else (0 if c == NB else -9, "Q%d" % c)))
        for b in range(0, QW, 512):
            n = min(512, QW - b)
            qk.append("Q%d_%d" % (c % NB, b))
            select(Q[:, b:b + n], T.XW[:, c:16 * n:16], [[0, n]], 0, "X1 X2", qk[-1], n)
        name, c0 = PARK[c]
        for f, (b0, per, w) in enumerate(FOLD):
            ne, trs = len(sets[f]) // per, []
            for j in range(per):
                b = b0 + w * j
                trs.append(RemoteDMATransfer(
                    dst_ids=[DstId(rid=mrid, pnc=mpid)], dma_engine_mask=sum(1 << e for e in sets[f][ne * j:ne * j + ne]),
                    remote_sem=T.sem["hf%d_%d" % (c, f)], srcs=[G[:, b:b + w], Q[:, b % 256:b % 256 + w]],
                    dsts=[T[name][:, c0 + b:c0 + b + w]], alu_op=2))
            k0, n = b0 // 256, per * w // 256
            named(*((c - AHEAD, "fold%d" % f) if c >= NB else (-9, "f%d%d" % (c, f))))
            remote(lambda trs=trs: g.remote_dma_fused(trs, local_sem=T.sem.sent), qk + gk(c, k0, n).split() + ["LD9"] * (c == FOLD0),
                   gk(c, k0, n, "MX").split(), "mx%d_%d" % (c, f), len(back_engines(mate, core, topo)), FLAT[f], len(sets[f]))

    def own_close(c):
        G, M = T["GO%d" % (c % NB)], T["MX%d" % (c % NB)]
        if c < DIRECT:
            for j in range(4):
                b = 2 * (j % 2)
                named(-9, "d%d%d" % (c, j))
                for h in range(2):
                    w, wk = wb(b + h)
                    k = 4 * j + 2 * h
                    mm(w, T.IDM[:], T.XW[:, c:8192:16], True, False, "IDM X1 X2", wk, 512)
                    mm(w, T.NID[:], G[:, 256 * k:256 * k + 512], False, True, "NID " + gk(c, k, 2), wk, 512)
                w, wk = wb(b, 2)
                act(T.AB[:, 512 * b:512 * b + 1024], w, F.Abs, wk, units("AB", b, 2), 1024)
                named(-9, "e%d%d" % (c, j))
                for k in range(4):
                    total(4 * j + k, "Z8", T.AB[:, 512 * b + 256 * k:512 * b + 256 * k + 256], units("AB", b + k // 2), j + k == 0)
        else:
            part = [(c - ahead, "k%d" % j) for j, (n, ahead) in enumerate(CLOSE) for _ in range(n)]
            named(*part[0])
            mm(T.KO[:, 0:256], T.BM[:], T.XW[:, c:4096:16], True, False, "BM X1", "#KO", 256)
            for k in range(16):
                named(*part[k])
                total(k, "ZM", G[:, 256 * k:256 * k + 256], gk(c, k))
            for k in range(16):
                named(*part[16 + k])
                total(k, "Z16", M[:, 256 * k:256 * k + 256], gk(c, k, 1, "MX"))
        named(*((c - 1, "kot") if c >= DIRECT else (-9, "kot%d" % c)))
        mm(T.KO[:, 0:256], T.SVK[:], T.AW[:, c + 1:4096:16], False, True, "SVK " + AWall, "#KO", 256)
        act(T.KOT[:, c::16], T.KO[:, 0:256], F.Copy, "#KO", "KOT", 256)

    CNT, AAW, ROW, TOT = T.M2[:, 256:272], T.M2[:, 272:304], T.M2[:, 304:305], T.M2[:, 305:306]

    def at(w, name, early=0):
        named(*((w - early, name) if w >= 0 else (-9, name.lower() + "0")))

    def at_v(w):
        at(w, "QG", 1)
        act(T.QG[:], T.XW[:, 0:4096].indirect(T.V16[:]), F.Copy, "X1 V16", "QG", GA * 256)
        at(w, "u")
        mm(T.KE[:, 0:256], T.WM[:], T.QG[:], True, True, "WM QG", "#KE", 256)
        P, z, bk = (T.PW, 2048, "#W4") if w >= 0 else (T.M2, 0, "#M2")
        for h in range(2):
            mm(P[:, z + 128 * h:z + 128 + 128 * h], T.QG[:, 128 * h:128 * h + 128], T.IDM[:], True, True, "QG IDM", bk, 128)
        at(w, "QT")
        act(T.QT[:], P[:, z:z + 256], F.Copy, bk, "QT", 256)
        at(w, "UC")
        cp(T.UC[:], T.KE[:, 0:256], "#KE", "UC", 256)
        at(w, "UG")
        ts(T.UG[:], T.UC[:], 4095, None, A.bitwise_and, None, "UC", "UG", 256)

    def at_a(w):
        at(w, "AG")
        act(T.AG[:], T.AW[:, 0:4096].indirect(T.AV[:]), F.Copy, AWall + " A16 V1", "AG", GA * 512)
        at(w, "ZA")
        wrap(AAW, T.ZA, lambda r: T.AG[:, r::16], "ZA", "AG")
        if w < NST - 2:
            mm(T.M2[:, 0:256], T.MVA[:], T.AG[:, 0:256], True, False, "MVA AG", "#M2", 256)
            mm(T.M2[:, 0:256], T.MVV[:], T.AG[:, 256:512], False, True, "MVV AG", "#M2", 256)
            at(w, "IOG")
            act(T.IOG[:], T.M2[:, 0:256], F.Copy, "#M2", "IOG", 256)
        at(w, "AAS")
        act(T.AAS[:], AAW, F.Copy, "#M2", "AAS", 32)
        at(w, "DA")
        tt(T.DA[:], T.AAS[:, 16:32], T.AAS[:, 0:16], A.subtract, "AAS", "DA")

    def keys(i0, i1):
        return (T.KE[:, i0:i1], "#KE") if i0 < CUT else (T.M2[:, 320 + i0 - CUT:320 + i1 - CUT], "#M2")

    def strict_pass(s):
        parts = list(zip(PLACES, PLACES[1:]))
        for j, (i0, i1) in enumerate(parts):
            R, n = T.RW[:, 0:4096].indirect(T.AV[:, i0 // 16:i1 // 16]), i1 - i0
            named(s, "TA%d" % j)
            act(T.EK[:, i0:i1], R, F.Identity, RWall + " A16 c_kc", "EK%d" % j, GA * n, bias=col("kc"))
            tt(T.TA[:, i0:i1], R, T.UG[:, i0:i1], A.mult, RWall + " A16 UG", "TA%d" % j, GA * n)
            named(s, "TB%d" % j)
            ts(T.TB[:, i0:i1], T.TA[:, i0:i1], 5, 4095, A.arith_shift_right, A.bitwise_and, "TA%d" % j, "TB%d" % j, n)
            named(s, "PL%d" % j)
            tt(T.PLE[:, i0:i1], T.EK[:, i0:i1], T.TB[:, i0:i1], A.add, "EK%d TB%d" % (j, j), "PLE%d" % j, 2 * n)
        ek = units("EK", 0, len(parts))
        named(s, "NEQ")
        mm(T.M2[:, 0:256], T.EQM[:], T.EK[:], True, True, "EQM " + ek, "#M2", 1024)
        act(T.NEQ[:], T.M2[:, 0:256], F.Abs, "#M2 c_kq", "NEQ", 256, scale=33554432.0, bias=col("kq"))
        named(s, "DM")
        tt(T.DM[:], T.KOT[:].indirect(T.V16[:]), T.NEQ[:], A.add, "KOT V16 NEQ", "DM", GA * 256)

        way = {u: q for q, u0, n, bank in HEAVY if bank is not None for u in range(u0, u0 + n)}

        def add(i0, i1, lhs, rhs, rd, slow=1):
            o, bk = keys(i0, i1)
            mm(o, lhs, rhs, False, False, rd + " " + bk, units("K", i0 // 32, (i1 - i0) // 32), slow * max(64, i1 - i0))

        def low(i0, i1):
            add(i0, i1, T.ZK[:], T.AG[:, 256 + i0:256 + i1], "ZK AG")
            add(i0, i1, T.DNM[:], T.EK[:, i0:i1], "DNM " + ek, 4)

        for j, (i0, i1) in enumerate(((0, CUT), (CUT, 256))):
            o, bk = keys(i0, i1)
            named(s, "open%d" % j)
            mm(o, T.DNG[:], T.ALL1[:, i0:i1], True, False, "DNG ALL1", bk, max(64, i1 - i0))
            for u0, n in SUMS:
                if way[u0] == "s" and i0 <= 32 * u0 < i1:
                    low(32 * u0, 32 * (u0 + n))
        for q, u0, n, bank in HEAVY:
            i0, i1, ge, ab = 32 * u0, 32 * (u0 + n), units("GE", u0, n), units("AB", u0, n)
            if bank is None:
                rd = Xall + "".join(" PLE%d" % j for j, (a, b) in enumerate(parts) if a < i1 and b > i0)
                named(s, "g%d" % u0)
                copy(q, T.GE[:, 16 * i0:16 * i1], T.XW[:].indirect(T.PLE[:, i0:i1]), rd, ge, GA * 512 * n)
                continue
            for u in range(u0, u0 + n):
                w, wk = wb(bank + u - u0)
                named(s, "q%d" % u)
                mm(w, T.QT[:, 128 * (u // 4):128 * (u // 4) + 128], T.SEL[:, 512 * (u % 4):512 * (u % 4) + 512], True, q == "v", "QT SEL", wk, 512)
                if q == "s":
                    named(s, "n%d" % u)
                    mm(w, T.NID[:], T.GE[:, 512 * u:512 * u + 512], False, True, "NID GE%d" % u, wk, 512)
            w, wk = wb(bank, n)
            named(s, "a%d" % u0)
            if q == "s":
                act(T.AB[:, 16 * i0:16 * i1], w, F.Abs, wk, ab, 512 * n)
            else:
                tt(T.AB[:, 16 * i0:16 * i1], T.GE[:, 16 * i0:16 * i1], w, A.max, wk + " " + ge, ab, 512 * n)
        for u0, n in SUMS:
            i0, i1, q, ge, ab = 32 * u0, 32 * (u0 + n), way[u0], units("GE", u0, n), units("AB", u0, n)
            if q == "v":
                named(s, "x%d" % u0)
                add(i0, i1, T.BM[:], T.QG[:, i0:i1], "BM QG")
                for k in range(16):
                    add(i0, i1, T.ZM[:, 16 - k:144 - k], T.GE[:, 16 * i0 + k:16 * i1:16], "ZM " + ge)
            named(s, "s%d" % u0)
            for k in range(16):
                add(i0, i1, (T.Z8 if q == "s" else T.Z16)[:, 16 - k:144 - k], T.AB[:, 16 * i0 + k:16 * i1:16], "Z8 Z16 " + ab)
            if q == "v":
                low(i0, i1)
        for j, i0 in enumerate((0, CUT)):
            o, bk = keys(i0, i0 + 16)
            named(s, "stop%d" % j)
            mm(o, T.IDM[:], T.ZB[:], False, True, "IDM ZB", bk)

    named(-9, "l0")
    own_lists(0, LIST0)
    named(-9, "l1")
    own_lists(LIST0, NST)
    rows(8, 1)
    rows(2, 2)
    at_v(-1)
    at_a(-1)
    for h in range(4):
        named(-9, "rw%d" % h)
        a, b = T.RW[:, 1024 * h:1024 * h + 1024], T.RI[:, 1024 * h:1024 * h + 1024]
        if RW_ON[h] == "v":
            cp(a, b, "RI%d" % h, "RW%d" % h, 1024)
        else:
            select(a, b, [[0, 1024]], 0, "RI%d" % h, "RW%d" % h, 1024)
    trs, n_eng = [], 0
    named(-9, "pres")
    for m in range(3):
        for n in range(3):
            b = 192 * m + 128 - 64 * n
            select(T.PRES[:, b:b + 64], T.RI[:, 8 + m + 3 * n:4096:64], [[0, 64]], 0, units("RI", 0, 4), "PRES%d" % (m + 3 * n), 64)
        src = T.cores[(rank - 1 - m) % n_ranks]
        rid, pid = topo.addr(src)[:2]
        e = topo.engines(core, src)
        e = e[:len(e) // 2] if m == 0 else e[len(e) // 4 * (m + 1):len(e) // 4 * (m + 2)]
        n_eng += len(e)
        trs.append(RemoteDMATransfer(dst_ids=[DstId(rid=rid, pnc=pid)], dma_engine_mask=sum(1 << x for x in e), remote_sem=T.sem.pre,
                                     src=T.PRES[:, 192 * m:192 * m + 192], dst=T.CB[:, CBW * m:CBW * m + 192]))
    remote(lambda: g.remote_dma_fused(trs, local_sem=T.sem.sent), units("PRES", 0, 9).split(), units("CB", 0, NST).split(),
           "pre", n_eng, PLAT, n_eng, False)
    for c in range(NB):
        own_gather(c)
        own_max(c)
    for c in range(DIRECT):
        own_close(c)
    own_gather(NB)
    own_max(NB)

    for t in range(NST):
        more, s = t < NST - 1, t - 1
        strict_pass(s)
        th = "th" if t == 0 else "thb"
        for j, (i0, i1) in enumerate(((0, CUT), (CUT, 256))):
            o, bk = keys(i0, i1)
            named(s, "MN%d" % j)
            tt(T.MN[:, i0:i1], o, T.DM[:, i0:i1], A.min, bk + " DM", "MN%d" % j, i1 - i0)
            named(s, "IND%d" % j)
            ts(T.IND[:, i0:i1], T.MN[:, i0:i1], col(th), None, A.is_lt, None, "MN%d c_%s" % (j, th), "IND%d" % j, i1 - i0)
        named(s, "FV")
        ts(T.FV[:], T.MN[:], 4095, None, A.bitwise_and, None, "MN0 MN1", "FV", 256)
        if not more:
            for r in range(16):
                named(s, "k%d" % min(r // 4, 2))
                mm(T.KO[:, 0:256], T.ZA[:, 16 - r:144 - r], T.AW[:, 256 * r:256 * r + 256], r == 0, r == 15, "ZA " + AWall, "#KO", 256)
            named(s, "y3")
            act(T.Y3[:], T.KO[:, 0:256], F.Copy, "#KO", "Y3", 256)
            act(T.YN[:], T.Y3[:, :, 0:8], F.Copy, "Y3", "YN", 128)
        named(s, "FW")
        wrap(CNT, T.Z1, lambda r: T.IND[:, r::16], "Z1", "IND0 IND1")
        ts(T.FW[:], CNT, 7.5, None, A.is_gt, None, "#M2", "FW")
        named(s, "NF")
        ts(T.NF[:], CNT, 7.5, 4096.0, A.is_lt, A.mult, "#M2", "NF")
        named(s, "SC")
        op("v", lambda: g.vector.tensor_tensor_scan(T.SC[:], T.FW[:], T.M1[:], col("s0"), A.add, A.add), "FW M1 c_s0", "SC", FIX + 16 * CYC)
        mm(ROW, T.TRI[:], T.SC[:, 15:16], True, True, "TRI SC", "#M2")
        if more:
            mm(TOT, T.ALL1[:, 0:128], T.SC[:, 15:16], True, True, "ALL1 SC", "#M2")
        named(s, "GD")
        tt(T.GD[:], T.FW[:], T.KD[:], A.mult, "FW KD", "GD")
        named(s, "P1")
        tt(T.P1[:], T.GD[:], T.SC[:], A.add, "GD SC", "P1")
        named(s, "D16")
        tt(T.D16[:], T.V16[:], T.NF[:], A.add, "V16 NF", "D16")
        named(s, "V16")
        tt(T.V16[:] if more else T.YV[:], T.V16[:], T.FW[:], A.add, "V16 FW", "V16" if more else "YV")
        named(s, "C16")
        ts(T.C16[:], T.P1[:], ROW, col("s2"), A.add, A.add, "P1 c_s2 #M2", "C16")
        named(s, "CB")
        b = CBW * (t % 3) + 128 - 64 * (t // 3)
        cp(T.CB[:, b:b + 320].indirect(T.C16[:]), T.FV[:], "C16 FV CB%d" % t, " ".join("CB%d" % x for x in range(t, -1, -3)), SC_ * 256)
        dst = T.cores[(rank + 1 + t % (n_ranks - 1)) % n_ranks]
        rid, pid = topo.addr(dst)[:2]
        n_eng = len(topo.engines(core, dst))
        named(t, "write")
        remote(lambda t=t, b=b, pid=pid, rid=rid, dst=dst: g.remote_dma(
            T.LAND[:, 64 * t:64 * t + 64], T.CB[:, b:b + 64], T.sem["arr%d" % t], T.sem["out%d" % t], pid, rid, topo.mask(core, dst)),
            ["CB%d" % t], ["LAND%d" % t], "arr%d" % t, n_eng, RLAT - RCALL, n_eng, False, "out%d" % t)
        named(t, "RW" if more else "BI")
        cp(T.RW[:].indirect(T.D16[:]), T.FV[:], "D16 FV", RWall, SC_ * 256)
        named(t, "MA")
        tt(T.MA[:], T.FW[:], T.DA[:], A.mult, "FW DA", "MA")
        named(t, "A16")
        tt(A16 if more else T.YA[:], T.MA[:], T.AAS[:, 0:16], A.add, "MA AAS", "A16" if more else "YA")
        if more:
            named(t, "AW")
            cp(T.AW[:].indirect(T.D16[:]), T.IOG[:], "D16 IOG", AWall, SC_ * 256)
            named(t, "V1")
            tt(V1, V1, T.FW[:], A.add, "V1 FW", "V1")
            named(t, "BI")
            cp(T.BI[:], TOT, "#M2", "BI")
            named(t, "BI2")
            ts(T.BI2[:], T.BI[:], 255, None, A.bitwise_and, None, "BI", "BI2")
            named(t, "thb")
            ts(col("thb"), T.BI2[:], 8192.0, col("th"), A.mult, A.add, "BI2 c_th", "c_thb")
            at_v(t)
            at_a(t)
            if t + 1 >= DIRECT:
                own_close(t + 1)
            if t + NB + 1 < NST:
                own_gather(t + NB + 1)
                own_max(t + NB + 1)
            named(t, "merge")
            cp(T.RW[:, 8 + t:4096:64], T.LAND[:, 64 * t:64 * t + 64], "LAND%d" % t, RWall, 64)
            named(t, "yh")
            select(T.YH[:, t::8], T.LAND[:, 64 * t:64 * t + 64], [[0, 64]], 0, "LAND%d" % t, "YH", 64)
        else:
            named(t)
            act(T.YH[:, t::8], T.LAND[:, 64 * t:64 * t + 64], F.Copy, "LAND%d" % t, "YH", 64)
        if t == NST - 2:
            named(t, "p2")
            cp(T.P2[:, 0:16], A16, "A16", "PA")
            cp(T.P2[:, 16:32], T.V16[:], "V16", "PV")
            named(t, "y2")
            tt(T.Y2[:], T.P2[:, 16:32].indirect(T.EX[:]), T.XC[:], A.is_equal, "PV EX XC", "Y2", GA * 128)

    named(NST - 1, "UC")
    dma("yh_", T.yh[:], T.YH[:], 1 << 18, rd="YH")
    dma("yv_", T.yv[:], T.YV[:], 1 << 13, rd="YV")
    dma("ya_", T.ya[:], T.YA[:], 1 << 13, rd="YA")
    for s in range(4):
        o, wk = T.PW[:, 512 * s:512 * s + 256], "#W%d" % s
        act(o, T.RW[:, 4 + s:4096:16], F.Copy, RWall, wk, 256, scale=4096.0)
        tt(T.KOT[:, s:1024:4], o, T.RW[:, s:4096:16], A.add, RWall + " KOT " + wk, "YR%d" % s, 256)
    dma("yr_", T.yr[:], T.KOT[:, 0:1024], 1 << 19, rd=units("YR", 0, 4))
    named(NST - 1, "UG")
    tt(T.Y1[:], T.P2[:, 0:16].indirect(T.EX[:]), T.YN[:], A.subtract, "PA EX YN", "Y1", GA * 128)
    tt(T.Y2[:], T.FW[:].indirect(T.EX[:]), T.Y2[:], A.mult, "FW EX Y2", "Y2", GA * 128)
    tt(T.Y1[:], T.Y1[:], T.Y2[:], A.mult, "Y1 Y2", "Y1", 256)
    tt(T.YN[:], T.YN[:], T.Y1[:], A.add, "YN Y1", "YN", 256)
    dma("yan_", T.yan[:], T.YN[:], 1 << 16, rd="YN")

    for j in issue_order(tasks):
        if tasks[j][5]:
            tasks[j][5]()
    count["sent"] = sent[0]
    for s in count:
        if seen["g"].get(s, 0) < count[s]:
            g.wait_ge(T.sem[s], count[s])
